import numpy as np
import ml_dtypes


def mxq(x, axis, fmt="e4m3"):
    dtype, down = {"e4m3": (ml_dtypes.float8_e4m3fn, 7), "e5m2": (ml_dtypes.float8_e5m2, 14)}[fmt]
    v = np.moveaxis(np.asarray(x, np.float32).astype(ml_dtypes.bfloat16).astype(np.float64), axis, -1)
    blocks = v.reshape(v.shape[:-1] + (-1, 32))
    amax = np.abs(blocks).max(-1, keepdims=True)
    byte = np.maximum(np.where(amax > 0, np.frexp(amax)[1] - 1 + 127, 0) - down, 1)
    scale = np.exp2(byte - 127.0)
    codes = (blocks / scale).astype(np.float32).astype(dtype).astype(np.float64)
    return np.moveaxis((codes * scale).reshape(v.shape), -1, axis)


WIDE = False


def mx_kscale(k):
    if not WIDE:
        return np.ones(k)
    levels = np.array([10, -10, 5, -5, 0])
    if k % 512:
        return np.exp2(np.random.permutation(np.resize(levels, k // 32))).repeat(32)
    a = np.empty((k // 512, 16))
    for p in range(k // 512):
        a[p, :8] = np.random.permutation(np.resize(levels, 8))
        for g in range(8):
            far = levels[np.abs(levels - a[p, g]) >= 10]
            a[p, g + 8] = far[np.random.randint(len(far))]
    return np.exp2(a.ravel()).repeat(32)


def f64(x):
    return np.asarray(x).astype(np.float64)


def striped(idx):
    return np.tile(idx.reshape(-1, 16).T, (8, 1)).astype(np.uint16)


def unstriped(offs):
    return offs[:16].T.reshape(-1).astype(np.int64)


E2M1 = np.array([0.0, 0.5, 1.0, 1.5, 2.0, 3.0, 4.0, 6.0, -0.0, -0.5, -1.0, -1.5, -2.0, -3.0, -4.0, -6.0])


def pack_weight(w, fmt):
    k, n = w.shape
    w = f64(np.asarray(w, np.float32).astype(ml_dtypes.bfloat16)).reshape(k // 32, 32, n)
    amax = np.abs(w).max(1)
    if fmt == "e4m3":
        byte = np.frexp(amax)[1] - 1 + 127 - 7
    else:
        mant, ex = np.frexp(amax / 6.0)
        byte = np.where(mant > 0.5, ex, ex - 1) + 127
    byte = np.clip(np.where(amax > 0, byte, 1), 1, 254)
    scaled = (w * np.exp2(127.0 - byte)[:, None, :]).reshape(k, n).astype(np.float32)
    by_word = np.ascontiguousarray(scaled.reshape(k // 512, 128, 4, n).transpose(0, 1, 3, 2))
    if fmt == "e4m3":
        words = by_word.astype(ml_dtypes.float8_e4m3fn).view(np.uint8)
    else:
        c = by_word.astype(ml_dtypes.float4_e2m1fn).view(np.uint8) & 0xF
        words = (c[..., 0::2] | (c[..., 1::2] << 4)).reshape(k // 512, 128, 2 * n)
    return np.ascontiguousarray(words), np.ascontiguousarray(byte.astype(np.uint8).reshape(k // 512, 16, n))


def unpack_weight(words, scales, fmt):
    g, _, n = scales.shape
    words = np.ascontiguousarray(words).reshape(g, 128, n, -1)
    if fmt == "e4m3":
        vals = words.view(ml_dtypes.float8_e4m3fn).astype(np.float64)
    else:
        nib = np.empty((g, 128, n, 4), np.uint8)
        nib[..., 0::2] = words & 0xF
        nib[..., 1::2] = words >> 4
        vals = E2M1[nib]
    vals = vals * np.repeat(np.exp2(scales.astype(np.float64) - 127.0), 8, axis=1)[..., None]
    return vals.transpose(0, 1, 3, 2).reshape(g * 512, n)


def gelu(v):
    return 0.5 * v * (1.0 + np.tanh(np.sqrt(2.0 / np.pi) * (v + 0.044715 * v**3)))


def striped8(idx):
    return np.concatenate([v.reshape(-1, 16).T for v in idx]).astype(np.uint16)


def unstriped8(offs):
    return np.stack([offs[16 * g:16 * g + 16].T.reshape(-1) for g in range(8)]).astype(np.int64)


def runs(v, idx8):
    k = np.arange(v.shape[0])
    return v[k[:, None], idx8[k % 512 // 64]]


def often(T, S):
    return np.random.permutation(T)[(T * np.random.uniform(0, 1, S) ** 4).astype(np.int64)]


K, T, S, H, N = 1024, 2048, 1024, 1024, 512

def setup_inputs():
    n = np.random.standard_normal
    s = mx_kscale(K)[:, None]
    u = mx_kscale(H)[:, None]
    tab_words, tab_scales = pack_weight(n((K, T)) * s, "e4m3")
    offs = striped8(np.stack([often(T, S) for _ in range(8)]))
    w1_words, w1_scales = pack_weight(n((K, H)) / np.sqrt(K) / s, "e2m1")
    w2 = (n((K, N)) * 1.5 / np.sqrt(K) / s).astype(np.float32)
    gain = (1.5 * np.exp(0.3 * n(H)) * u[:, 0]).astype(np.float32)
    w3_words, w3_scales = pack_weight(n((H, N)) * 1.2 / np.sqrt(H) / u, "e4m3")
    old = n((N, S)).astype(np.float32)
    return {"tab_words": tab_words, "tab_scales": tab_scales, "offs": offs,
            "w1_words": w1_words, "w1_scales": w1_scales, "w2": w2,
            "gain": gain, "w3_words": w3_words, "w3_scales": w3_scales,
            "old": old}

def reference(tab_words, tab_scales, offs, w1_words, w1_scales, w2, gain,
              w3_words, w3_scales, old):
    v = runs(unpack_weight(tab_words, tab_scales, "e4m3"), unstriped8(offs))
    w1 = unpack_weight(w1_words, w1_scales, "e2m1")
    w3 = unpack_weight(w3_words, w3_scales, "e4m3")
    a = w1.T @ v
    h = a / (1.0 + np.exp(-a)) * f64(gain)[:, None]
    e = mxq(f64(w2), 0, "e4m3").T @ v
    gate = 1.0 / (1.0 + np.exp(-e))
    y = w3.T @ mxq(h, 0, "e4m3")
    o = f64(old)
    return o + gate * (y - o)

@@ -1,0 +1,273 @@
+from contextlib import ExitStack
+
+import concourse.mybir as mybir
+
+K, T, S, H, N = 1024, 2048, 1024, 1024, 512
+FLOPS = 2 * S * (K * H + K * N + H * N)
+
+F32 = mybir.dt.float32
+BF16 = mybir.dt.bfloat16
+I32 = mybir.dt.int32
+U32 = mybir.dt.uint32
+U16 = mybir.dt.uint16
+U8 = mybir.dt.uint8
+FP8X4 = mybir.dt.float8_e4m3fn_x4
+FP4X4 = mybir.dt.float4_e2m1fn_x4
+ACT = mybir.ActivationFunctionType
+ALU = mybir.AluOpType
+
+P = 128
+PACK = 4
+PASSES = 2
+W = 512
+HALVES = S // W
+TILES = N // P
+ROW = W + H + N
+W1_AT = W
+W3_AT = W + H
+
+
+def tile_list_register_file_step_kernel(
+    tc, tab_words, tab_scales, offs, w1_words, w1_scales, w2, gain, w3_words, w3_scales, old, out
+):
+    nc = tc.nc
+    with ExitStack() as ctx:
+        keep = ctx.enter_context(tc.tile_pool(name="keep", bufs=1))
+        psum = ctx.enter_context(tc.psum_pool(name="psum", bufs=8))
+
+        def tile(shape, dtype, name, tag=None):
+            return keep.tile(shape, dtype, name=name, tag=tag or name, align_bytes=64)
+
+        offsets = keep.tile([P, S // 16], U16, name="offsets")
+        nc.sync.dma_start(offsets[:], offs)
+
+        w1_raw = {}
+
+        def load_w1(b):
+            w1_raw[b] = tile([P, PASSES, 2 * W], U8, "w1_raw%d" % b)
+            src = w1_words[:, :, 2 * W * b : 2 * W * (b + 1)].bitcast(I32).rearrange("a p c -> p a c")
+            nc.sync.dma_start(w1_raw[b][:].bitcast(I32), src)
+
+        gains = tile([P, PASSES, PACK], F32, "gains")
+        nc.sync.dma_start(gains[:], gain.rearrange("(b p t) -> p b t", b=PASSES, t=PACK))
+        load_w1(0)
+
+        tab_rows = tile([P, T], U8, "tab_rows")
+        w1_rows = tile([P, H], U8, "w1_rows")
+        rows = tile([P, ROW], U8, "rows")
+        planes = tile([P, PASSES, ROW], U8, "planes")
+        late_planes = tile([P, PASSES, W], U8, "late_planes")
+        warm = tile([P, 2], F32, "warm")
+        nc.vector.memset(w1_rows[:].bitcast(I32), 0)
+        nc.vector.memset(rows[:, W3_AT:].bitcast(I32), 0)
+        nc.vector.memset(tab_rows[:].bitcast(I32), 0)
+        nc.vector.memset(warm[:, 0:1], 0.0)
+        nc.vector.memset(planes[:].rearrange("p a c -> p (a c)").bitcast(I32), 0)
+        nc.vector.memset(late_planes[:].rearrange("p a c -> p (a c)").bitcast(I32), 0)
+        nc.scalar.activation(warm[:, 1:2], warm[:, 0:1], ACT.Silu)
+
+        def load_rows(dst, scales):
+            nc.sync.dma_start(dst.bitcast(I32), scales.bitcast(I32).rearrange("a q c -> q a c"))
+
+        load_rows(w1_rows[0:P:4, :], w1_scales)
+        load_rows(rows[0:P:4, W3_AT:], w3_scales)
+        load_rows(tab_rows[0:P:4, :], tab_scales)
+
+        table = []
+        for a in range(PASSES):
+            words = tile([P, T], U32, "table%d" % a)
+            nc.sync.dma_start(words[:].bitcast(I32), tab_words[a].rearrange("p t i -> p (t i)").bitcast(I32))
+            table.append(words)
+
+
+        w1 = {}
+
+        def order_w1(b, tag=None):
+            w1[b] = tile([P, PASSES * 2 * W], U8, "w1_%d" % b, tag)
+            nc.vector.tensor_copy(
+                w1[b][:].bitcast(U16).rearrange("p (a t c i) -> p a c t i", a=PASSES, t=PACK, i=8),
+                w1_raw[b][:].rearrange("p a c -> p (a c)").bitcast(U16).rearrange("p (a c i t) -> p a c t i", a=PASSES, t=PACK, i=8),
+            )
+
+        def offsets_of(h):
+            return offsets[:, h * (W // 16) : (h + 1) * (W // 16)]
+
+        def gather_rows(h, tag=None):
+            picked_rows = tile([P, W], U8, "picked_rows%d" % h, tag)
+            nc.vector.tensor_copy(picked_rows[:], tab_rows[:].indirect(offsets_of(h)))
+            return picked_rows
+
+        def move_rows(dst, src):
+            for d in range(4):
+                nc.sync.dma_start(dst[32 * d : 32 * d + 4, :, :].bitcast(I32), src[32 * d : 32 * d + 32 : 4, :].bitcast(I32))
+
+        nc.vector.tensor_copy(
+            rows[:, W1_AT:W3_AT].rearrange("p (b t c i) -> p b c t i", b=2, t=PACK, i=16),
+            w1_rows[:].rearrange("p (b c i t) -> p b c t i", b=2, t=PACK, i=16),
+        )
+        nc.vector.tensor_copy(rows[:, 0:W1_AT].bitcast(I32), gather_rows(0)[:].bitcast(I32))
+        move_rows(planes, rows)
+        order_w1(0, "picked_rows0")
+        load_w1(1)
+
+        w2_raw = {}
+
+        def load_w2(a, tag=None):
+            w2_raw[a] = tile([P, PACK, N], F32, "w2_raw%d" % a, tag)
+            nc.sync.dma_start(w2_raw[a][:], w2[a * W : (a + 1) * W, :].rearrange("(p t) n -> p t n", t=PACK))
+
+        olds = {}
+
+        def load_old(h):
+            olds[h] = tile([P, TILES, W], F32, "old%d" % h)
+            nc.sync.dma_start(olds[h][:], old[:, h * W : (h + 1) * W].rearrange("(u p) j -> p u j", p=P))
+
+        load_w2(0)
+        w3 = tile([P, PASSES, N], U32, "w3")
+        nc.sync.dma_start(w3[:].bitcast(I32), w3_words.rearrange("b p c i -> p b (c i)").bitcast(I32))
+
+        picked = {}
+
+        def gather(a, h, tag=None):
+            v = tile([P, W], U32, "picked%d%d" % (a, h), tag)
+            nc.vector.tensor_copy(v[:], table[a][:].indirect(offsets_of(h)))
+            picked[a, h] = v
+
+        def table_operand(a, h):
+            return {"rhs": picked[a, h][:].bitcast(FP8X4), "rhs_scale": (planes, late_planes)[h][:, a, 0:W]}
+
+        silus = {}
+
+        def features(h, b):
+            banks = [psum.tile([P, W], F32, name="bank", tag="bank") for t in range(PACK)]
+            for t in range(PACK):
+                for a in range(PASSES):
+                    c = b * W + t * P
+                    nc.tensor.matmul_mx(
+                        banks[t][:],
+                        lhsT=w1[b][:, 2 * (a * W + t * P) : 2 * (a * W + (t + 1) * P)].bitcast(FP4X4),
+                        lhsT_scale=planes[:, a, W1_AT + c : W1_AT + c + P],
+                        start=(a == 0),
+                        stop=(a == PASSES - 1),
+                        **table_operand(a, h),
+                    )
+            s = tile([P, PACK, W], F32, "silu%d%d" % (h, b))
+            for t in range(PACK):
+                nc.scalar.activation(s[:, t, :], banks[t][:], ACT.Silu)
+            silus[h, b] = s
+
+        h_bf = {}
+
+        def apply_gain(h, b):
+            x = tile([P, PACK * W], BF16, "h_bf%d%d" % (h, b))
+            nc.vector.tensor_tensor(
+                x[:].rearrange("p (c i t) -> p c t i", t=PACK, i=4),
+                silus[h, b][:].rearrange("p t (c i) -> p c t i", i=4),
+                gains[:, b, :].unsqueeze(1).unsqueeze(3).broadcast_to([P, W // 4, PACK, 4]),
+                ALU.mult,
+            )
+            h_bf[h, b] = x
+
+        def quantize(x, name):
+            codes = tile([P, W], U32, name + "_codes")
+            scales = tile([P, W], U8, name + "_scales")
+            nc.vector.quantize_mx(out=codes[:].bitcast(FP8X4), scales=scales[:], in_=x[:])
+            return codes, scales
+
+        w2_bf = [tile([P, PACK * N], BF16, "w2_bf%d" % a) for a in range(PASSES)]
+
+        def round_w2(a):
+            for u in range(TILES):
+                nc.scalar.copy(
+                    w2_bf[a][:, u * PACK * P : (u + 1) * PACK * P].rearrange("p (c i t) -> p c t i", t=PACK, i=4),
+                    w2_raw[a][:, :, u * P : (u + 1) * P].rearrange("p t (c i) -> p c t i", i=4),
+                )
+
+        h_q = {}
+        w2_q = {}
+        diffs = {}
+        tanhs = {}
+
+        def output_diff(h, u):
+            bank = psum.tile([P, W], F32, name="bank", tag="bank")
+            for b in range(PASSES):
+                codes, scales = h_q[h, b]
+                nc.tensor.matmul_mx(
+                    bank[:],
+                    lhsT=w3[:, b, u * P : (u + 1) * P].bitcast(FP8X4),
+                    lhsT_scale=planes[:, b, W3_AT + u * P : W3_AT + (u + 1) * P],
+                    rhs=codes[:].bitcast(FP8X4),
+                    rhs_scale=scales[:],
+                    start=(b == 0),
+                    stop=(b == PASSES - 1),
+                )
+            d = tile([P, W], F32, "diff%d%d" % (h, u))
+            nc.vector.tensor_tensor(d[:], bank[:], olds[h][:, u, :], ALU.subtract)
+            diffs[h, u] = d
+
+        def gate(h, u):
+            bank = psum.tile([P, W], F32, name="bank", tag="bank")
+            for a in range(PASSES):
+                codes, scales = w2_q[a]
+                nc.tensor.matmul_mx(
+                    bank[:],
+                    lhsT=codes[:, u * P : (u + 1) * P].bitcast(FP8X4),
+                    lhsT_scale=scales[:, u * P : (u + 1) * P],
+                    start=(a == 0),
+                    stop=(a == PASSES - 1),
+                    **table_operand(a, h),
+                )
+            th = tile([P, W], F32, "tanh%d%d" % (h, u))
+            nc.scalar.activation(th[:], bank[:], ACT.Tanh, scale=0.5)
+            tanhs[h, u] = th
+
+        steps = {}
+
+        def step(h, u):
+            m = tile([P, W], F32, "step%d%d" % (h, u))
+            nc.vector.scalar_tensor_tensor(m[:], tanhs[h, u][:], 1.0, diffs[h, u][:], ALU.add, ALU.mult)
+            steps[h, u] = m
+
+        def finish(h, u):
+            r = tile([P, W], F32, "result%d%d" % (h, u))
+            nc.vector.scalar_tensor_tensor(r[:], steps[h, u][:], 0.5, olds[h][:, u, :], ALU.mult, ALU.add)
+            nc.sync.dma_start(out[u * P : (u + 1) * P, h * W : (h + 1) * W], r[:])
+
+        gather(0, 0)
+        gather(1, 0)
+        features(0, 0)
+        order_w1(1)
+        features(0, 1)
+        move_rows(late_planes, gather_rows(1, "w1_raw1"))
+        load_old(0)
+        load_w2(1)
+        load_old(1)
+        gather(0, 1, "tab_rows")
+        gather(1, 1)
+        features(1, 0)
+        round_w2(0)
+        apply_gain(0, 0)
+        apply_gain(0, 1)
+        h_q[0, 0] = quantize(h_bf[0, 0], "h00")
+        features(1, 1)
+        round_w2(1)
+        apply_gain(1, 0)
+        h_q[0, 1] = quantize(h_bf[0, 1], "h01")
+        w2_q[0] = quantize(w2_bf[0], "w20")
+        apply_gain(1, 1)
+        h_q[1, 0] = quantize(h_bf[1, 0], "h10")
+        w2_q[1] = quantize(w2_bf[1], "w21")
+        for u in range(TILES):
+            output_diff(0, u)
+        h_q[1, 1] = quantize(h_bf[1, 1], "h11")
+        for h in range(HALVES):
+            for u in range(TILES):
+                gate(h, u)
+        units = [(h, u) for h in range(HALVES) for u in range(TILES)]
+        for i in range(len(units) + 1):
+            if TILES <= i + 2 < len(units):
+                output_diff(*units[i + 2])
+            if i < len(units):
+                step(*units[i])
+            if i >= 1:
+                finish(*units[i - 1])

@@ -22,9 +22,8 @@ PASSES = 2
 W = 512
 HALVES = S // W
 TILES = N // P
-ROW = W + H + N
-W1_AT = W
-W3_AT = W + H
+EARLY_ROW = W + H
+LATE_ROW = W + N
 
 
 def tile_list_register_file_step_kernel(
@@ -48,20 +47,21 @@ def tile_list_register_file_step_kernel(
             src = w1_words[:, :, 2 * W * b : 2 * W * (b + 1)].bitcast(I32).rearrange("a p c -> p a c")
             nc.sync.dma_start(w1_raw[b][:].bitcast(I32), src)
 
+        load_w1(0)
         gains = tile([P, PASSES, PACK], F32, "gains")
         nc.sync.dma_start(gains[:], gain.rearrange("(b p t) -> p b t", b=PASSES, t=PACK))
-        load_w1(0)
 
         tab_rows = tile([P, T], U8, "tab_rows")
         w1_rows = tile([P, H], U8, "w1_rows")
-        rows = tile([P, ROW], U8, "rows")
-        planes = tile([P, PASSES, ROW], U8, "planes")
-        late_planes = tile([P, PASSES, W], U8, "late_planes")
+        rows = tile([P, EARLY_ROW], U8, "rows")
+        late_rows = tile([P, LATE_ROW], U8, "late_rows")
+        planes = tile([P, PASSES, EARLY_ROW], U8, "planes")
+        late_planes = tile([P, PASSES, LATE_ROW], U8, "late_planes")
         warm = tile([P, 2], F32, "warm")
         nc.vector.memset(w1_rows[:].bitcast(I32), 0)
-        nc.vector.memset(rows[:, W3_AT:].bitcast(I32), 0)
         nc.vector.memset(tab_rows[:].bitcast(I32), 0)
         nc.vector.memset(warm[:, 0:1], 0.0)
+        nc.vector.memset(late_rows[:, W:].bitcast(I32), 0)
         nc.vector.memset(planes[:].rearrange("p a c -> p (a c)").bitcast(I32), 0)
         nc.vector.memset(late_planes[:].rearrange("p a c -> p (a c)").bitcast(I32), 0)
         nc.scalar.activation(warm[:, 1:2], warm[:, 0:1], ACT.Silu)
@@ -70,7 +70,6 @@ def tile_list_register_file_step_kernel(
             nc.sync.dma_start(dst.bitcast(I32), scales.bitcast(I32).rearrange("a q c -> q a c"))
 
         load_rows(w1_rows[0:P:4, :], w1_scales)
-        load_rows(rows[0:P:4, W3_AT:], w3_scales)
         load_rows(tab_rows[0:P:4, :], tab_scales)
 
         table = []
@@ -80,10 +79,13 @@ def tile_list_register_file_step_kernel(
             table.append(words)
 
 
+        load_w1(1)
+        load_rows(late_rows[0:P:4, W:], w3_scales)
+
         w1 = {}
 
-        def order_w1(b, tag=None):
-            w1[b] = tile([P, PASSES * 2 * W], U8, "w1_%d" % b, tag)
+        def order_w1(b):
+            w1[b] = tile([P, PASSES * 2 * W], U8, "w1_%d" % b)
             nc.vector.tensor_copy(
                 w1[b][:].bitcast(U16).rearrange("p (a t c i) -> p a c t i", a=PASSES, t=PACK, i=8),
                 w1_raw[b][:].rearrange("p a c -> p (a c)").bitcast(U16).rearrange("p (a c i t) -> p a c t i", a=PASSES, t=PACK, i=8),
@@ -92,23 +94,23 @@ def tile_list_register_file_step_kernel(
         def offsets_of(h):
             return offsets[:, h * (W // 16) : (h + 1) * (W // 16)]
 
-        def gather_rows(h, tag=None):
-            picked_rows = tile([P, W], U8, "picked_rows%d" % h, tag)
+        def gather_rows(h, dst):
+            picked_rows = tile([P, W], U8, "picked_rows%d" % h, "picked_rows")
             nc.vector.tensor_copy(picked_rows[:], tab_rows[:].indirect(offsets_of(h)))
-            return picked_rows
+            nc.vector.tensor_copy(dst[:, 0:W].bitcast(I32), picked_rows[:].bitcast(I32))
 
-        def move_rows(dst, src):
-            for d in range(4):
-                nc.sync.dma_start(dst[32 * d : 32 * d + 4, :, :].bitcast(I32), src[32 * d : 32 * d + 32 : 4, :].bitcast(I32))
+        def move_rows(queue, dst, src):
+            for d in (0, 2, 1, 3):
+                queue.dma_start(dst[32 * d : 32 * d + 4, :, :].bitcast(I32), src[32 * d : 32 * d + 32 : 4, :].bitcast(I32))
 
+        order_w1(0)
         nc.vector.tensor_copy(
-            rows[:, W1_AT:W3_AT].rearrange("p (b t c i) -> p b c t i", b=2, t=PACK, i=16),
+            rows[:, W:].rearrange("p (b t c i) -> p b c t i", b=2, t=PACK, i=16),
             w1_rows[:].rearrange("p (b c i t) -> p b c t i", b=2, t=PACK, i=16),
         )
-        nc.vector.tensor_copy(rows[:, 0:W1_AT].bitcast(I32), gather_rows(0)[:].bitcast(I32))
-        move_rows(planes, rows)
-        order_w1(0, "picked_rows0")
-        load_w1(1)
+        gather_rows(0, rows)
+        move_rows(nc.scalar, planes, rows)
+        gather_rows(1, late_rows)
 
         w2_raw = {}
 
@@ -122,9 +124,11 @@ def tile_list_register_file_step_kernel(
             olds[h] = tile([P, TILES, W], F32, "old%d" % h)
             nc.sync.dma_start(olds[h][:], old[:, h * W : (h + 1) * W].rearrange("(u p) j -> p u j", p=P))
 
-        load_w2(0)
-        w3 = tile([P, PASSES, N], U32, "w3")
-        nc.sync.dma_start(w3[:].bitcast(I32), w3_words.rearrange("b p c i -> p b (c i)").bitcast(I32))
+        load_w2(0, "tab_rows")
+        move_rows(nc.sync, late_planes, late_rows)
+        load_old(0)
+        load_w2(1)
+        load_old(1)
 
         picked = {}
 
@@ -133,39 +137,44 @@ def tile_list_register_file_step_kernel(
             nc.vector.tensor_copy(v[:], table[a][:].indirect(offsets_of(h)))
             picked[a, h] = v
 
-        def table_operand(a, h):
-            return {"rhs": picked[a, h][:].bitcast(FP8X4), "rhs_scale": (planes, late_planes)[h][:, a, 0:W]}
+        def table_operand(a, h, c0, c1):
+            return {"rhs": picked[a, h][:, c0:c1].bitcast(FP8X4), "rhs_scale": (planes, late_planes)[h][:, a, c0:c1]}
 
         silus = {}
 
         def features(h, b):
-            banks = [psum.tile([P, W], F32, name="bank", tag="bank") for t in range(PACK)]
-            for t in range(PACK):
-                for a in range(PASSES):
-                    c = b * W + t * P
-                    nc.tensor.matmul_mx(
-                        banks[t][:],
-                        lhsT=w1[b][:, 2 * (a * W + t * P) : 2 * (a * W + (t + 1) * P)].bitcast(FP4X4),
-                        lhsT_scale=planes[:, a, W1_AT + c : W1_AT + c + P],
-                        start=(a == 0),
-                        stop=(a == PASSES - 1),
-                        **table_operand(a, h),
-                    )
-            s = tile([P, PACK, W], F32, "silu%d%d" % (h, b))
-            for t in range(PACK):
-                nc.scalar.activation(s[:, t, :], banks[t][:], ACT.Silu)
+            s = tile([P, W * PACK], F32, "silu%d%d" % (h, b))
+            for q in range(W // P):
+                bank = psum.tile([P, PACK * P], F32, name="bank", tag="bank")
+                for t in range(PACK):
+                    for a in range(PASSES):
+                        c = W + b * W + t * P
+                        nc.tensor.matmul_mx(
+                            bank[:, t * P : (t + 1) * P],
+                            lhsT=w1[b][:, 2 * (a * W + t * P) : 2 * (a * W + (t + 1) * P)].bitcast(FP4X4),
+                            lhsT_scale=planes[:, a, c : c + P],
+                            start=(a == 0),
+                            stop=(a == PASSES - 1),
+                            **table_operand(a, h, q * P, (q + 1) * P),
+                        )
+                nc.scalar.activation(
+                    s[:, q * W : (q + 1) * W].rearrange("p (n t) -> p n t", t=PACK),
+                    bank[:].rearrange("p (t n) -> p n t", t=PACK),
+                    ACT.Silu,
+                )
             silus[h, b] = s
 
         h_bf = {}
 
         def apply_gain(h, b):
             x = tile([P, PACK * W], BF16, "h_bf%d%d" % (h, b))
-            nc.vector.tensor_tensor(
-                x[:].rearrange("p (c i t) -> p c t i", t=PACK, i=4),
-                silus[h, b][:].rearrange("p t (c i) -> p c t i", i=4),
-                gains[:, b, :].unsqueeze(1).unsqueeze(3).broadcast_to([P, W // 4, PACK, 4]),
-                ALU.mult,
-            )
+            for c0 in range(0, PACK * W, 2 * W):
+                nc.vector.tensor_tensor(
+                    x[:, c0 : c0 + 2 * W].rearrange("p (n t) -> p n t", t=PACK),
+                    silus[h, b][:, c0 : c0 + 2 * W].rearrange("p (n t) -> p n t", t=PACK),
+                    gains[:, b, :].unsqueeze(1).broadcast_to([P, 2 * W // PACK, PACK]),
+                    ALU.mult,
+                )
             h_bf[h, b] = x
 
         def quantize(x, name):
@@ -174,9 +183,10 @@ def tile_list_register_file_step_kernel(
             nc.vector.quantize_mx(out=codes[:].bitcast(FP8X4), scales=scales[:], in_=x[:])
             return codes, scales
 
-        w2_bf = [tile([P, PACK * N], BF16, "w2_bf%d" % a) for a in range(PASSES)]
+        w2_bf = {}
 
-        def round_w2(a):
+        def round_w2(a, tag=None):
+            w2_bf[a] = tile([P, PACK * N], BF16, "w2_bf%d" % a, tag)
             for u in range(TILES):
                 nc.scalar.copy(
                     w2_bf[a][:, u * PACK * P : (u + 1) * PACK * P].rearrange("p (c i t) -> p c t i", t=PACK, i=4),
@@ -195,7 +205,7 @@ def tile_list_register_file_step_kernel(
                 nc.tensor.matmul_mx(
                     bank[:],
                     lhsT=w3[:, b, u * P : (u + 1) * P].bitcast(FP8X4),
-                    lhsT_scale=planes[:, b, W3_AT + u * P : W3_AT + (u + 1) * P],
+                    lhsT_scale=late_planes[:, b, W + u * P : W + (u + 1) * P],
                     rhs=codes[:].bitcast(FP8X4),
                     rhs_scale=scales[:],
                     start=(b == 0),
@@ -215,7 +225,7 @@ def tile_list_register_file_step_kernel(
                     lhsT_scale=scales[:, u * P : (u + 1) * P],
                     start=(a == 0),
                     stop=(a == PASSES - 1),
-                    **table_operand(a, h),
+                    **table_operand(a, h, 0, W),
                 )
             th = tile([P, W], F32, "tanh%d%d" % (h, u))
             nc.scalar.activation(th[:], bank[:], ACT.Tanh, scale=0.5)
@@ -228,46 +238,46 @@ def tile_list_register_file_step_kernel(
             nc.vector.scalar_tensor_tensor(m[:], tanhs[h, u][:], 1.0, diffs[h, u][:], ALU.add, ALU.mult)
             steps[h, u] = m
 
-        def finish(h, u):
-            r = tile([P, W], F32, "result%d%d" % (h, u))
-            nc.vector.scalar_tensor_tensor(r[:], steps[h, u][:], 0.5, olds[h][:, u, :], ALU.mult, ALU.add)
-            nc.sync.dma_start(out[u * P : (u + 1) * P, h * W : (h + 1) * W], r[:])
+        def finish(h, u, c0, c1):
+            r = tile([P, c1 - c0], F32, "result%d%d_%d" % (h, u, c0))
+            nc.vector.scalar_tensor_tensor(r[:], steps[h, u][:, c0:c1], 0.5, olds[h][:, u, c0:c1], ALU.mult, ALU.add)
+            nc.sync.dma_start(out[u * P : (u + 1) * P, h * W + c0 : h * W + c1], r[:])
 
         gather(0, 0)
         gather(1, 0)
         features(0, 0)
         order_w1(1)
         features(0, 1)
-        move_rows(late_planes, gather_rows(1, "w1_raw1"))
-        load_old(0)
-        load_w2(1)
-        load_old(1)
-        gather(0, 1, "tab_rows")
+        gather(0, 1, "w1_raw1")
         gather(1, 1)
         features(1, 0)
-        round_w2(0)
+        w3 = tile([P, PASSES, N], U32, "w3", "w1_0")
+        nc.sync.dma_start(w3[:].bitcast(I32), w3_words.rearrange("b p c i -> p b (c i)").bitcast(I32))
+        features(1, 1)
+        round_w2(0, "w1_1")
+        round_w2(1)
         apply_gain(0, 0)
         apply_gain(0, 1)
         h_q[0, 0] = quantize(h_bf[0, 0], "h00")
-        features(1, 1)
-        round_w2(1)
         apply_gain(1, 0)
         h_q[0, 1] = quantize(h_bf[0, 1], "h01")
-        w2_q[0] = quantize(w2_bf[0], "w20")
         apply_gain(1, 1)
         h_q[1, 0] = quantize(h_bf[1, 0], "h10")
+        output_diff(0, 0)
+        h_q[1, 1] = quantize(h_bf[1, 1], "h11")
+        for u in range(1, TILES):
+            output_diff(0, u)
+        w2_q[0] = quantize(w2_bf[0], "w20")
         w2_q[1] = quantize(w2_bf[1], "w21")
         for u in range(TILES):
-            output_diff(0, u)
-        h_q[1, 1] = quantize(h_bf[1, 1], "h11")
-        for h in range(HALVES):
-            for u in range(TILES):
-                gate(h, u)
+            gate(0, u)
+            output_diff(1, u)
+        for u in range(TILES):
+            gate(1, u)
         units = [(h, u) for h in range(HALVES) for u in range(TILES)]
-        for i in range(len(units) + 1):
-            if TILES <= i + 2 < len(units):
-                output_diff(*units[i + 2])
-            if i < len(units):
-                step(*units[i])
+        for i in range(len(units)):
+            step(*units[i])
             if i >= 1:
-                finish(*units[i - 1])
+                finish(*units[i - 1], 0, W)
+        finish(*units[-1], 0, W // 2)
+        finish(*units[-1], W // 2, W)

@@ -243,7 +243,21 @@ def tile_list_register_file_step_kernel(
             nc.vector.scalar_tensor_tensor(r[:], steps[h, u][:, c0:c1], 0.5, olds[h][:, u, c0:c1], ALU.mult, ALU.add)
             nc.sync.dma_start(out[u * P : (u + 1) * P, h * W + c0 : h * W + c1], r[:])
 
+        def warm_up(words, passes):
+            bank = psum.tile([P, W], F32, name="bank", tag="bank")
+            for i in range(passes):
+                nc.tensor.matmul_mx(
+                    bank[:],
+                    lhsT=w1[0][:, 0 : 2 * P].bitcast(FP4X4),
+                    lhsT_scale=rows[:, W : W + P],
+                    rhs=words[:, 0:W].bitcast(FP8X4),
+                    rhs_scale=rows[:, 0:W],
+                    start=(i == 0),
+                    stop=(i == passes - 1),
+                )
+
         gather(0, 0)
+        warm_up(picked[0, 0], 3)
         gather(1, 0)
         features(0, 0)
         order_w1(1)

@@ -57,14 +57,11 @@ def tile_list_register_file_step_kernel(
         late_rows = tile([P, LATE_ROW], U8, "late_rows")
         planes = tile([P, PASSES, EARLY_ROW], U8, "planes")
         late_planes = tile([P, PASSES, LATE_ROW], U8, "late_planes")
-        warm = tile([P, 2], F32, "warm")
         nc.vector.memset(w1_rows[:].bitcast(I32), 0)
         nc.vector.memset(tab_rows[:].bitcast(I32), 0)
-        nc.vector.memset(warm[:, 0:1], 0.0)
         nc.vector.memset(late_rows[:, W:].bitcast(I32), 0)
         nc.vector.memset(planes[:].rearrange("p a c -> p (a c)").bitcast(I32), 0)
         nc.vector.memset(late_planes[:].rearrange("p a c -> p (a c)").bitcast(I32), 0)
-        nc.scalar.activation(warm[:, 1:2], warm[:, 0:1], ACT.Silu)
 
         def load_rows(dst, scales):
             nc.sync.dma_start(dst.bitcast(I32), scales.bitcast(I32).rearrange("a q c -> q a c"))
@@ -243,21 +240,7 @@ def tile_list_register_file_step_kernel(
             nc.vector.scalar_tensor_tensor(r[:], steps[h, u][:, c0:c1], 0.5, olds[h][:, u, c0:c1], ALU.mult, ALU.add)
             nc.sync.dma_start(out[u * P : (u + 1) * P, h * W + c0 : h * W + c1], r[:])
 
-        def warm_up(words, passes):
-            bank = psum.tile([P, W], F32, name="bank", tag="bank")
-            for i in range(passes):
-                nc.tensor.matmul_mx(
-                    bank[:],
-                    lhsT=w1[0][:, 0 : 2 * P].bitcast(FP4X4),
-                    lhsT_scale=rows[:, W : W + P],
-                    rhs=words[:, 0:W].bitcast(FP8X4),
-                    rhs_scale=rows[:, 0:W],
-                    start=(i == 0),
-                    stop=(i == passes - 1),
-                )
-
         gather(0, 0)
-        warm_up(picked[0, 0], 3)
         gather(1, 0)
         features(0, 0)
         order_w1(1)

@@ -1,6 +1,7 @@
 from contextlib import ExitStack
 
 import concourse.mybir as mybir
+from concourse.masks import make_identity
 
 K, T, S, H, N = 1024, 2048, 1024, 1024, 512
 FLOPS = 2 * S * (K * H + K * N + H * N)
@@ -42,14 +43,13 @@ def tile_list_register_file_step_kernel(
 
         w1_raw = {}
 
-        def load_w1(b):
+        def load_w1(b, pieces):
             w1_raw[b] = tile([P, PASSES, 2 * W], U8, "w1_raw%d" % b)
             src = w1_words[:, :, 2 * W * b : 2 * W * (b + 1)].bitcast(I32).rearrange("a p c -> p a c")
-            nc.sync.dma_start(w1_raw[b][:].bitcast(I32), src)
+            for a0, a1 in pieces:
+                nc.sync.dma_start(w1_raw[b][:, a0:a1, :].bitcast(I32), src[:, a0:a1, :])
 
-        load_w1(0)
-        gains = tile([P, PASSES, PACK], F32, "gains")
-        nc.sync.dma_start(gains[:], gain.rearrange("(b p t) -> p b t", b=PASSES, t=PACK))
+        load_w1(0, [(0, 1), (1, 2)])
 
         tab_rows = tile([P, T], U8, "tab_rows")
         w1_rows = tile([P, H], U8, "w1_rows")
@@ -57,17 +57,25 @@ def tile_list_register_file_step_kernel(
         late_rows = tile([P, LATE_ROW], U8, "late_rows")
         planes = tile([P, PASSES, EARLY_ROW], U8, "planes")
         late_planes = tile([P, PASSES, LATE_ROW], U8, "late_planes")
+        warm = tile([P, 2], F32, "warm")
         nc.vector.memset(w1_rows[:].bitcast(I32), 0)
         nc.vector.memset(tab_rows[:].bitcast(I32), 0)
+        nc.vector.memset(warm[:, 0:1], 0.0)
         nc.vector.memset(late_rows[:, W:].bitcast(I32), 0)
         nc.vector.memset(planes[:].rearrange("p a c -> p (a c)").bitcast(I32), 0)
         nc.vector.memset(late_planes[:].rearrange("p a c -> p (a c)").bitcast(I32), 0)
+        gain_rows = tile([P, W], F32, "gain_rows")
+        identity = tile([P, P], F32, "identity")
+        nc.gpsimd.memset(gain_rows[:], 0.0)
+        make_identity(nc, identity[:])
+        nc.scalar.activation(warm[:, 1:2], warm[:, 0:1], ACT.Silu)
 
         def load_rows(dst, scales):
             nc.sync.dma_start(dst.bitcast(I32), scales.bitcast(I32).rearrange("a q c -> q a c"))
 
         load_rows(w1_rows[0:P:4, :], w1_scales)
         load_rows(tab_rows[0:P:4, :], tab_scales)
+        nc.sync.dma_start(gain_rows[0:PASSES, :], gain.rearrange("(b k) -> b k", b=PASSES))
 
         table = []
         for a in range(PASSES):
@@ -76,23 +84,27 @@ def tile_list_register_file_step_kernel(
             table.append(words)
 
 
-        load_w1(1)
+        load_w1(1, [(0, 2)])
         load_rows(late_rows[0:P:4, W:], w3_scales)
+        gain_bank = psum.tile([P, PACK * P], F32, name="gain_bank", tag="bank")
+        for t in range(PACK):
+            nc.tensor.transpose(gain_bank[:, t * P : (t + 1) * P], gain_rows[:, t:W:PACK], identity[:])
+        gains = gain_bank[:].rearrange("p (t b) -> p b t", t=PACK)
 
         w1 = {}
 
-        def order_w1(b):
-            w1[b] = tile([P, PASSES * 2 * W], U8, "w1_%d" % b)
+        def order_w1(b, tag=None):
+            w1[b] = tile([P, PASSES * 2 * W], U8, "w1_%d" % b, tag)
             nc.vector.tensor_copy(
-                w1[b][:].bitcast(U16).rearrange("p (a t c i) -> p a c t i", a=PASSES, t=PACK, i=8),
-                w1_raw[b][:].rearrange("p a c -> p (a c)").bitcast(U16).rearrange("p (a c i t) -> p a c t i", a=PASSES, t=PACK, i=8),
+                w1[b][:].bitcast(U16).rearrange("p (a t m) -> p a t m", a=PASSES, t=PACK),
+                w1_raw[b][:].rearrange("p a c -> p (a c)").bitcast(U16).rearrange("p (a m t) -> p a t m", a=PASSES, t=PACK),
             )
 
         def offsets_of(h):
             return offsets[:, h * (W // 16) : (h + 1) * (W // 16)]
 
-        def gather_rows(h, dst):
-            picked_rows = tile([P, W], U8, "picked_rows%d" % h, "picked_rows")
+        def gather_rows(h, dst, tag=None):
+            picked_rows = tile([P, W], U8, "picked_rows%d" % h, tag)
             nc.vector.tensor_copy(picked_rows[:], tab_rows[:].indirect(offsets_of(h)))
             nc.vector.tensor_copy(dst[:, 0:W].bitcast(I32), picked_rows[:].bitcast(I32))
 
@@ -100,32 +112,27 @@ def tile_list_register_file_step_kernel(
             for d in (0, 2, 1, 3):
                 queue.dma_start(dst[32 * d : 32 * d + 4, :, :].bitcast(I32), src[32 * d : 32 * d + 32 : 4, :].bitcast(I32))
 
-        order_w1(0)
         nc.vector.tensor_copy(
-            rows[:, W:].rearrange("p (b t c i) -> p b c t i", b=2, t=PACK, i=16),
-            w1_rows[:].rearrange("p (b c i t) -> p b c t i", b=2, t=PACK, i=16),
+            rows[:, W:].rearrange("p (b t m) -> p b t m", b=2, t=PACK),
+            w1_rows[:].rearrange("p (b m t) -> p b t m", b=2, t=PACK),
         )
         gather_rows(0, rows)
         move_rows(nc.scalar, planes, rows)
-        gather_rows(1, late_rows)
+        order_w1(0, "picked_rows0")
 
-        w2_raw = {}
+        w2_raw = tile([P, PASSES, PACK, N], F32, "w2_raw", "w1_raw0")
 
-        def load_w2(a, tag=None):
-            w2_raw[a] = tile([P, PACK, N], F32, "w2_raw%d" % a, tag)
-            nc.sync.dma_start(w2_raw[a][:], w2[a * W : (a + 1) * W, :].rearrange("(p t) n -> p t n", t=PACK))
+        def load_w2(a):
+            nc.sync.dma_start(w2_raw[:, a, :, :], w2[a * W : (a + 1) * W, :].rearrange("(p t) n -> p t n", t=PACK))
 
         olds = {}
 
-        def load_old(h):
-            olds[h] = tile([P, TILES, W], F32, "old%d" % h)
+        def load_old(h, tag):
+            olds[h] = tile([P, TILES, W], F32, "old%d" % h, tag)
             nc.sync.dma_start(olds[h][:], old[:, h * W : (h + 1) * W].rearrange("(u p) j -> p u j", p=P))
 
-        load_w2(0, "tab_rows")
-        move_rows(nc.sync, late_planes, late_rows)
-        load_old(0)
+        load_w2(0)
         load_w2(1)
-        load_old(1)
 
         picked = {}
 
@@ -163,13 +170,17 @@ def tile_list_register_file_step_kernel(
 
         h_bf = {}
 
-        def apply_gain(h, b):
-            x = tile([P, PACK * W], BF16, "h_bf%d%d" % (h, b))
-            for c0 in range(0, PACK * W, 2 * W):
-                nc.vector.tensor_tensor(
-                    x[:, c0 : c0 + 2 * W].rearrange("p (n t) -> p n t", t=PACK),
-                    silus[h, b][:, c0 : c0 + 2 * W].rearrange("p (n t) -> p n t", t=PACK),
-                    gains[:, b, :].unsqueeze(1).broadcast_to([P, 2 * W // PACK, PACK]),
+        gain_copy = tile([P, PASSES, PACK], F32, "gain_copy")
+        nc.scalar.copy(gain_copy[:], gains[:, 0:PASSES, :])
+
+        def apply_gain(h, b, shared, tag=None):
+            x = tile([P, PACK * W], BF16, "h_bf%d%d" % (h, b), tag)
+            for q in range(W // P):
+                engine, factor = (nc.gpsimd, gain_copy) if q in shared else (nc.vector, gains)
+                engine.tensor_tensor(
+                    x[:, q * W : (q + 1) * W].rearrange("p (n t) -> p n t", t=PACK),
+                    silus[h, b][:, q * W : (q + 1) * W].rearrange("p (n t) -> p n t", t=PACK),
+                    factor[:, b, :].unsqueeze(1).broadcast_to([P, P, PACK]),
                     ALU.mult,
                 )
             h_bf[h, b] = x
@@ -177,22 +188,35 @@ def tile_list_register_file_step_kernel(
         def quantize(x, name):
             codes = tile([P, W], U32, name + "_codes")
             scales = tile([P, W], U8, name + "_scales")
-            nc.vector.quantize_mx(out=codes[:].bitcast(FP8X4), scales=scales[:], in_=x[:])
+            nc.vector.quantize_mx(out=codes[:].bitcast(FP8X4), scales=scales[:], in_=x)
             return codes, scales
 
         w2_bf = {}
 
-        def round_w2(a, tag=None):
-            w2_bf[a] = tile([P, PACK * N], BF16, "w2_bf%d" % a, tag)
+        def round_w2(a):
+            w2_bf[a] = tile([P, PACK * N], BF16, "w2_bf%d" % a)
             for u in range(TILES):
                 nc.scalar.copy(
                     w2_bf[a][:, u * PACK * P : (u + 1) * PACK * P].rearrange("p (c i t) -> p c t i", t=PACK, i=4),
-                    w2_raw[a][:, :, u * P : (u + 1) * P].rearrange("p t (c i) -> p c t i", i=4),
+                    w2_raw[:, a, :, u * P : (u + 1) * P].rearrange("p t (c i) -> p c t i", i=4),
+                )
+
+        def round_w2_gpsimd(a, tag):
+            w2_bf[a] = tile([P, PACK * N], BF16, "w2_bf%d" % a, tag)
+            for c in range(0, N, N // 2):
+                nc.gpsimd.tensor_scalar(
+                    w2_bf[a][:, c * PACK : (c + N // 2) * PACK].rearrange("p (c t) -> p c t", t=PACK),
+                    w2_raw[:, a, :, c : c + N // 2].rearrange("p t c -> p c t"),
+                    1.0,
+                    0.0,
+                    ALU.mult,
+                    ALU.add,
                 )
 
         h_q = {}
         w2_q = {}
         diffs = {}
+        ys = {}
         tanhs = {}
 
         def output_diff(h, u):
@@ -211,6 +235,7 @@ def tile_list_register_file_step_kernel(
             d = tile([P, W], F32, "diff%d%d" % (h, u))
             nc.vector.tensor_tensor(d[:], bank[:], olds[h][:, u, :], ALU.subtract)
             diffs[h, u] = d
+            ys[h, u] = bank
 
         def gate(h, u):
             bank = psum.tile([P, W], F32, name="bank", tag="bank")
@@ -225,56 +250,65 @@ def tile_list_register_file_step_kernel(
                     **table_operand(a, h, 0, W),
                 )
             th = tile([P, W], F32, "tanh%d%d" % (h, u))
-            nc.scalar.activation(th[:], bank[:], ACT.Tanh, scale=0.5)
+            nc.scalar.activation(th[:], bank[:], ACT.Tanh, scale=-0.5)
+            if (h, u) in on_gpsimd:
+                stay = tile([P, W], F32, "stay%d%d" % (h, u))
+                nc.scalar.activation(stay[:], th[:], ACT.Copy, scale=0.5, bias=0.5)
+                th = stay
             tanhs[h, u] = th
 
         steps = {}
 
         def step(h, u):
             m = tile([P, W], F32, "step%d%d" % (h, u))
-            nc.vector.scalar_tensor_tensor(m[:], tanhs[h, u][:], 1.0, diffs[h, u][:], ALU.add, ALU.mult)
+            if (h, u) in on_gpsimd:
+                nc.gpsimd.tensor_tensor(m[:], tanhs[h, u][:], diffs[h, u][:], ALU.mult)
+            else:
+                nc.vector.scalar_tensor_tensor(m[:], tanhs[h, u][:], 1.0, diffs[h, u][:], ALU.add, ALU.mult)
             steps[h, u] = m
 
         def finish(h, u, c0, c1):
             r = tile([P, c1 - c0], F32, "result%d%d_%d" % (h, u, c0))
-            nc.vector.scalar_tensor_tensor(r[:], steps[h, u][:, c0:c1], 0.5, olds[h][:, u, c0:c1], ALU.mult, ALU.add)
+            factor = -1.0 if (h, u) in on_gpsimd else -0.5
+            nc.vector.scalar_tensor_tensor(r[:], steps[h, u][:, c0:c1], factor, ys[h, u][:, c0:c1], ALU.mult, ALU.add)
             nc.sync.dma_start(out[u * P : (u + 1) * P, h * W + c0 : h * W + c1], r[:])
+
+        units = [(h, u) for h in range(HALVES) for u in range(TILES)]
+        on_gpsimd = [unit for unit in units if unit[1] != TILES - 1]
 
         gather(0, 0)
         gather(1, 0)
         features(0, 0)
         order_w1(1)
         features(0, 1)
+        gather_rows(1, late_rows, "w1_raw1")
+        move_rows(nc.sync, late_planes, late_rows)
         gather(0, 1, "w1_raw1")
-        gather(1, 1)
-        features(1, 0)
-        w3 = tile([P, PASSES, N], U32, "w3", "w1_0")
+        gather(1, 1, "tab_rows")
+        w3 = tile([P, PASSES, N], U32, "w3", "late_rows")
         nc.sync.dma_start(w3[:].bitcast(I32), w3_words.rearrange("b p c i -> p b (c i)").bitcast(I32))
+        load_old(0, "table0")
+        round_w2(0)
+        round_w2_gpsimd(1, "table1")
+        load_old(1, "w1_raw0")
+        features(1, 0)
         features(1, 1)
-        round_w2(0, "w1_1")
-        round_w2(1)
-        apply_gain(0, 0)
-        apply_gain(0, 1)
-        h_q[0, 0] = quantize(h_bf[0, 0], "h00")
-        apply_gain(1, 0)
-        h_q[0, 1] = quantize(h_bf[0, 1], "h01")
-        apply_gain(1, 1)
-        h_q[1, 0] = quantize(h_bf[1, 0], "h10")
-        output_diff(0, 0)
-        h_q[1, 1] = quantize(h_bf[1, 1], "h11")
-        for u in range(1, TILES):
-            output_diff(0, u)
-        w2_q[0] = quantize(w2_bf[0], "w20")
-        w2_q[1] = quantize(w2_bf[1], "w21")
-        for u in range(TILES):
-            gate(0, u)
-            output_diff(1, u)
-        for u in range(TILES):
-            gate(1, u)
-        units = [(h, u) for h in range(HALVES) for u in range(TILES)]
-        for i in range(len(units)):
-            step(*units[i])
-            if i >= 1:
-                finish(*units[i - 1], 0, W)
+        apply_gain(0, 0, ())
+        apply_gain(0, 1, ())
+        h_q[0, 0] = quantize(h_bf[0, 0][:], "h00")
+        w2_q[0] = quantize(w2_bf[0][:], "w20")
+        h_q[0, 1] = quantize(h_bf[0, 1][:], "h01")
+        w2_q[1] = quantize(w2_bf[1][:], "w21")
+        apply_gain(1, 0, (0, 1, 2))
+        apply_gain(1, 1, (0, 1))
+        h_q[1, 0] = quantize(h_bf[1, 0][:], "h10")
+        h_q[1, 1] = quantize(h_bf[1, 1][:], "h11")
+        for i, unit in enumerate(units):
+            gate(*unit)
+            output_diff(*unit)
+            if i >= 2:
+                finish(*units[i - 2], 0, W)
+            step(*unit)
+        finish(*units[-2], 0, W)
         finish(*units[-1], 0, W // 2)
         finish(*units[-1], W // 2, W)

@@ -88,8 +88,8 @@ def tile_list_register_file_step_kernel(
         load_rows(late_rows[0:P:4, W:], w3_scales)
         gain_bank = psum.tile([P, PACK * P], F32, name="gain_bank", tag="bank")
         for t in range(PACK):
-            nc.tensor.transpose(gain_bank[:, t * P : (t + 1) * P], gain_rows[:, t:W:PACK], identity[:])
-        gains = gain_bank[:].rearrange("p (t b) -> p b t", t=PACK)
+            nc.tensor.transpose(gain_bank[:, t:W:PACK], gain_rows[:, t:W:PACK], identity[:])
+        gains = gain_bank[:].rearrange("p (b t) -> p b t", t=PACK)
 
         w1 = {}
 
@@ -168,13 +168,11 @@ def tile_list_register_file_step_kernel(
                 )
             silus[h, b] = s
 
-        h_bf = {}
 
         gain_copy = tile([P, PASSES, PACK], F32, "gain_copy")
         nc.scalar.copy(gain_copy[:], gains[:, 0:PASSES, :])
 
-        def apply_gain(h, b, shared, tag=None):
-            x = tile([P, PACK * W], BF16, "h_bf%d%d" % (h, b), tag)
+        def apply_gain(h, b, shared, x):
             for q in range(W // P):
                 engine, factor = (nc.gpsimd, gain_copy) if q in shared else (nc.vector, gains)
                 engine.tensor_tensor(
@@ -183,29 +181,24 @@ def tile_list_register_file_step_kernel(
                     factor[:, b, :].unsqueeze(1).broadcast_to([P, P, PACK]),
                     ALU.mult,
                 )
-            h_bf[h, b] = x
 
-        def quantize(x, name):
-            codes = tile([P, W], U32, name + "_codes")
-            scales = tile([P, W], U8, name + "_scales")
+        def quantize(x, passes, name, tag=None):
+            codes = tile([P, passes * W], U32, name + "_codes", tag)
+            scales = tile([P, passes * W], U8, name + "_scales")
             nc.vector.quantize_mx(out=codes[:].bitcast(FP8X4), scales=scales[:], in_=x)
-            return codes, scales
-
-        w2_bf = {}
+            return [(codes[:, a * W : (a + 1) * W], scales[:, a * W : (a + 1) * W]) for a in range(passes)]
 
         def round_w2(a):
-            w2_bf[a] = tile([P, PACK * N], BF16, "w2_bf%d" % a)
             for u in range(TILES):
                 nc.scalar.copy(
-                    w2_bf[a][:, u * PACK * P : (u + 1) * PACK * P].rearrange("p (c i t) -> p c t i", t=PACK, i=4),
+                    w2_bf[:, (a * N + u * P) * PACK : (a * N + (u + 1) * P) * PACK].rearrange("p (c i t) -> p c t i", t=PACK, i=4),
                     w2_raw[:, a, :, u * P : (u + 1) * P].rearrange("p t (c i) -> p c t i", i=4),
                 )
 
-        def round_w2_gpsimd(a, tag):
-            w2_bf[a] = tile([P, PACK * N], BF16, "w2_bf%d" % a, tag)
+        def round_w2_gpsimd(a):
             for c in range(0, N, N // 2):
                 nc.gpsimd.tensor_scalar(
-                    w2_bf[a][:, c * PACK : (c + N // 2) * PACK].rearrange("p (c t) -> p c t", t=PACK),
+                    w2_bf[:, (a * N + c) * PACK : (a * N + c + N // 2) * PACK].rearrange("p (c t) -> p c t", t=PACK),
                     w2_raw[:, a, :, c : c + N // 2].rearrange("p t c -> p c t"),
                     1.0,
                     0.0,
@@ -227,8 +220,8 @@ def tile_list_register_file_step_kernel(
                     bank[:],
                     lhsT=w3[:, b, u * P : (u + 1) * P].bitcast(FP8X4),
                     lhsT_scale=late_planes[:, b, W + u * P : W + (u + 1) * P],
-                    rhs=codes[:].bitcast(FP8X4),
-                    rhs_scale=scales[:],
+                    rhs=codes.bitcast(FP8X4),
+                    rhs_scale=scales,
                     start=(b == 0),
                     stop=(b == PASSES - 1),
                 )
@@ -260,11 +253,11 @@ def tile_list_register_file_step_kernel(
         steps = {}
 
         def step(h, u):
-            m = tile([P, W], F32, "step%d%d" % (h, u))
+            m = step_tiles[h][:, u * W : (u + 1) * W]
             if (h, u) in on_gpsimd:
-                nc.gpsimd.tensor_tensor(m[:], tanhs[h, u][:], diffs[h, u][:], ALU.mult)
+                nc.gpsimd.tensor_tensor(m, tanhs[h, u][:], diffs[h, u][:], ALU.mult)
             else:
-                nc.vector.scalar_tensor_tensor(m[:], tanhs[h, u][:], 1.0, diffs[h, u][:], ALU.add, ALU.mult)
+                nc.vector.scalar_tensor_tensor(m, tanhs[h, u][:], 1.0, diffs[h, u][:], ALU.add, ALU.mult)
             steps[h, u] = m
 
         def finish(h, u, c0, c1):
@@ -277,32 +270,33 @@ def tile_list_register_file_step_kernel(
         on_gpsimd = [unit for unit in units if unit[1] != TILES - 1]
 
         gather(0, 0)
+        gather(0, 1)
         gather(1, 0)
         features(0, 0)
         order_w1(1)
         features(0, 1)
         gather_rows(1, late_rows, "w1_raw1")
         move_rows(nc.sync, late_planes, late_rows)
-        gather(0, 1, "w1_raw1")
         gather(1, 1, "tab_rows")
         w3 = tile([P, PASSES, N], U32, "w3", "late_rows")
         nc.sync.dma_start(w3[:].bitcast(I32), w3_words.rearrange("b p c i -> p b (c i)").bitcast(I32))
-        load_old(0, "table0")
+        load_old(0, "table1")
+        w2_bf = tile([P, PASSES * PACK * N], BF16, "w2_bf", "table0")
         round_w2(0)
-        round_w2_gpsimd(1, "table1")
-        load_old(1, "w1_raw0")
+        round_w2_gpsimd(1)
         features(1, 0)
         features(1, 1)
-        apply_gain(0, 0, ())
-        apply_gain(0, 1, ())
-        h_q[0, 0] = quantize(h_bf[0, 0][:], "h00")
-        w2_q[0] = quantize(w2_bf[0][:], "w20")
-        h_q[0, 1] = quantize(h_bf[0, 1][:], "h01")
-        w2_q[1] = quantize(w2_bf[1][:], "w21")
-        apply_gain(1, 0, (0, 1, 2))
-        apply_gain(1, 1, (0, 1))
-        h_q[1, 0] = quantize(h_bf[1, 0][:], "h10")
-        h_q[1, 1] = quantize(h_bf[1, 1][:], "h11")
+        h0_bf = tile([P, PASSES * PACK * W], BF16, "h0_bf")
+        apply_gain(0, 0, (), h0_bf[:, 0 : PACK * W])
+        load_old(1, "silu00")
+        apply_gain(0, 1, (), h0_bf[:, PACK * W :])
+        h_q[0, 0], h_q[0, 1] = quantize(h0_bf[:], PASSES, "h0", "w1_raw0")
+        w2_q[0], w2_q[1] = quantize(w2_bf[:], PASSES, "w2")
+        h1_bf = tile([P, PASSES * PACK * W], BF16, "h1_bf", "table0")
+        apply_gain(1, 0, (0, 1, 2), h1_bf[:, 0 : PACK * W])
+        apply_gain(1, 1, (), h1_bf[:, PACK * W :])
+        h_q[1, 0], h_q[1, 1] = quantize(h1_bf[:], PASSES, "h1")
+        step_tiles = [tile([P, TILES * W], F32, "steps0", "table0"), tile([P, TILES * W], F32, "steps1")]
         for i, unit in enumerate(units):
             gate(*unit)
             output_diff(*unit)

@@ -58,10 +58,10 @@ def tile_list_register_file_step_kernel(
         planes = tile([P, PASSES, EARLY_ROW], U8, "planes")
         late_planes = tile([P, PASSES, LATE_ROW], U8, "late_planes")
         warm = tile([P, 2], F32, "warm")
-        nc.vector.memset(w1_rows[:].bitcast(I32), 0)
         nc.vector.memset(tab_rows[:].bitcast(I32), 0)
-        nc.vector.memset(warm[:, 0:1], 0.0)
+        nc.gpsimd.memset(w1_rows[:].bitcast(I32), 0)
         nc.vector.memset(late_rows[:, W:].bitcast(I32), 0)
+        nc.vector.memset(warm[:, 0:1], 0.0)
         nc.vector.memset(planes[:].rearrange("p a c -> p (a c)").bitcast(I32), 0)
         nc.vector.memset(late_planes[:].rearrange("p a c -> p (a c)").bitcast(I32), 0)
         gain_rows = tile([P, W], F32, "gain_rows")
@@ -73,8 +73,9 @@ def tile_list_register_file_step_kernel(
         def load_rows(dst, scales):
             nc.sync.dma_start(dst.bitcast(I32), scales.bitcast(I32).rearrange("a q c -> q a c"))
 
-        load_rows(w1_rows[0:P:4, :], w1_scales)
         load_rows(tab_rows[0:P:4, :], tab_scales)
+        load_rows(w1_rows[0:P:4, :], w1_scales)
+        load_rows(late_rows[0:P:4, W:], w3_scales)
         nc.sync.dma_start(gain_rows[0:PASSES, :], gain.rearrange("(b k) -> b k", b=PASSES))
 
         table = []
@@ -85,7 +86,6 @@ def tile_list_register_file_step_kernel(
 
 
         load_w1(1, [(0, 2)])
-        load_rows(late_rows[0:P:4, W:], w3_scales)
         gain_bank = psum.tile([P, PACK * P], F32, name="gain_bank", tag="bank")
         for t in range(PACK):
             nc.tensor.transpose(gain_bank[:, t:W:PACK], gain_rows[:, t:W:PACK], identity[:])
@@ -95,7 +95,7 @@ def tile_list_register_file_step_kernel(
 
         def order_w1(b, tag=None):
             w1[b] = tile([P, PASSES * 2 * W], U8, "w1_%d" % b, tag)
-            nc.vector.tensor_copy(
+            nc.gpsimd.tensor_copy(
                 w1[b][:].bitcast(U16).rearrange("p (a t m) -> p a t m", a=PASSES, t=PACK),
                 w1_raw[b][:].rearrange("p a c -> p (a c)").bitcast(U16).rearrange("p (a m t) -> p a t m", a=PASSES, t=PACK),
             )
@@ -112,15 +112,16 @@ def tile_list_register_file_step_kernel(
             for d in (0, 2, 1, 3):
                 queue.dma_start(dst[32 * d : 32 * d + 4, :, :].bitcast(I32), src[32 * d : 32 * d + 32 : 4, :].bitcast(I32))
 
-        nc.vector.tensor_copy(
+        nc.gpsimd.tensor_copy(
             rows[:, W:].rearrange("p (b t m) -> p b t m", b=2, t=PACK),
             w1_rows[:].rearrange("p (b m t) -> p b t m", b=2, t=PACK),
         )
         gather_rows(0, rows)
         move_rows(nc.scalar, planes, rows)
         order_w1(0, "picked_rows0")
+        gather_rows(1, late_rows, "w1_rows")
 
-        w2_raw = tile([P, PASSES, PACK, N], F32, "w2_raw", "w1_raw0")
+        w2_raw = tile([P, PASSES, PACK, N], F32, "w2_raw", "w1_rows")
 
         def load_w2(a):
             nc.sync.dma_start(w2_raw[:, a, :, :], w2[a * W : (a + 1) * W, :].rearrange("(p t) n -> p t n", t=PACK))
@@ -133,6 +134,7 @@ def tile_list_register_file_step_kernel(
 
         load_w2(0)
         load_w2(1)
+        move_rows(nc.sync, late_planes, late_rows)
 
         picked = {}
 
@@ -172,15 +174,14 @@ def tile_list_register_file_step_kernel(
         gain_copy = tile([P, PASSES, PACK], F32, "gain_copy")
         nc.scalar.copy(gain_copy[:], gains[:, 0:PASSES, :])
 
-        def apply_gain(h, b, shared, x):
-            for q in range(W // P):
-                engine, factor = (nc.gpsimd, gain_copy) if q in shared else (nc.vector, gains)
-                engine.tensor_tensor(
-                    x[:, q * W : (q + 1) * W].rearrange("p (n t) -> p n t", t=PACK),
-                    silus[h, b][:, q * W : (q + 1) * W].rearrange("p (n t) -> p n t", t=PACK),
-                    factor[:, b, :].unsqueeze(1).broadcast_to([P, P, PACK]),
-                    ALU.mult,
-                )
+        def apply_gain(engine, x, h, b, q0, q1):
+            factor = gain_copy if engine is nc.gpsimd else gains
+            engine.tensor_tensor(
+                x[:, (b * PACK + q0) * W : (b * PACK + q1) * W].rearrange("p (n t) -> p n t", t=PACK),
+                silus[h, b][:, q0 * W : q1 * W].rearrange("p (n t) -> p n t", t=PACK),
+                factor[:, b, :].unsqueeze(1).broadcast_to([P, (q1 - q0) * P, PACK]),
+                ALU.mult,
+            )
 
         def quantize(x, passes, name, tag=None):
             codes = tile([P, passes * W], U32, name + "_codes", tag)
@@ -225,8 +226,8 @@ def tile_list_register_file_step_kernel(
                     start=(b == 0),
                     stop=(b == PASSES - 1),
                 )
-            d = tile([P, W], F32, "diff%d%d" % (h, u))
-            nc.vector.tensor_tensor(d[:], bank[:], olds[h][:, u, :], ALU.subtract)
+            d = diff_room(h, u)
+            nc.vector.tensor_tensor(d, bank[:], olds[h][:, u, :], ALU.subtract)
             diffs[h, u] = d
             ys[h, u] = bank
 
@@ -255,48 +256,71 @@ def tile_list_register_file_step_kernel(
         def step(h, u):
             m = step_tiles[h][:, u * W : (u + 1) * W]
             if (h, u) in on_gpsimd:
-                nc.gpsimd.tensor_tensor(m, tanhs[h, u][:], diffs[h, u][:], ALU.mult)
+                nc.gpsimd.tensor_tensor(m, tanhs[h, u][:], diffs[h, u], ALU.mult)
             else:
-                nc.vector.scalar_tensor_tensor(m, tanhs[h, u][:], 1.0, diffs[h, u][:], ALU.add, ALU.mult)
+                nc.vector.scalar_tensor_tensor(m, tanhs[h, u][:], 1.0, diffs[h, u], ALU.add, ALU.mult)
             steps[h, u] = m
 
         def finish(h, u, c0, c1):
-            r = tile([P, c1 - c0], F32, "result%d%d_%d" % (h, u, c0))
+            room = units[(units.index((h, u)) + 2) % len(units)]
+            r = olds[room[0]][:, room[1], c0:c1]
             factor = -1.0 if (h, u) in on_gpsimd else -0.5
-            nc.vector.scalar_tensor_tensor(r[:], steps[h, u][:, c0:c1], factor, ys[h, u][:, c0:c1], ALU.mult, ALU.add)
-            nc.sync.dma_start(out[u * P : (u + 1) * P, h * W + c0 : h * W + c1], r[:])
+            nc.vector.scalar_tensor_tensor(r, steps[h, u][:, c0:c1], factor, ys[h, u][:, c0:c1], ALU.mult, ALU.add)
+            nc.sync.dma_start(out[u * P : (u + 1) * P, h * W + c0 : h * W + c1], r)
 
         units = [(h, u) for h in range(HALVES) for u in range(TILES)]
         on_gpsimd = [unit for unit in units if unit[1] != TILES - 1]
 
         gather(0, 0)
-        gather(0, 1)
+        warm_bank = psum.tile([P, W], F32, name="bank", tag="bank")
+        for i in range(3):
+            nc.tensor.matmul_mx(
+                warm_bank[:],
+                lhsT=w1[0][:, 0 : 2 * P].bitcast(FP4X4),
+                lhsT_scale=rows[:, W : W + P],
+                rhs=picked[0, 0][:].bitcast(FP8X4),
+                rhs_scale=rows[:, 0:W],
+                start=(i == 0),
+                stop=(i == 2),
+            )
         gather(1, 0)
         features(0, 0)
         order_w1(1)
+        gather(1, 1)
+        gather(0, 1, "w1_raw1")
         features(0, 1)
-        gather_rows(1, late_rows, "w1_raw1")
-        move_rows(nc.sync, late_planes, late_rows)
-        gather(1, 1, "tab_rows")
         w3 = tile([P, PASSES, N], U32, "w3", "late_rows")
         nc.sync.dma_start(w3[:].bitcast(I32), w3_words.rearrange("b p c i -> p b (c i)").bitcast(I32))
         load_old(0, "table1")
-        w2_bf = tile([P, PASSES * PACK * N], BF16, "w2_bf", "table0")
+        h0_bf = tile([P, PASSES * PACK * W], BF16, "h0_bf")
+        apply_gain(nc.gpsimd, h0_bf, 0, 0, 0, 1)
+        apply_gain(nc.gpsimd, h0_bf, 0, 0, 1, 2)
+        apply_gain(nc.vector, h0_bf, 0, 0, 2, 4)
+        w2_bf = tile([P, PASSES * PACK * N], BF16, "w2_bf", "silu00")
         round_w2(0)
         round_w2_gpsimd(1)
         features(1, 0)
         features(1, 1)
-        h0_bf = tile([P, PASSES * PACK * W], BF16, "h0_bf")
-        apply_gain(0, 0, (), h0_bf[:, 0 : PACK * W])
-        load_old(1, "silu00")
-        apply_gain(0, 1, (), h0_bf[:, PACK * W :])
-        h_q[0, 0], h_q[0, 1] = quantize(h0_bf[:], PASSES, "h0", "w1_raw0")
-        w2_q[0], w2_q[1] = quantize(w2_bf[:], PASSES, "w2")
-        h1_bf = tile([P, PASSES * PACK * W], BF16, "h1_bf", "table0")
-        apply_gain(1, 0, (0, 1, 2), h1_bf[:, 0 : PACK * W])
-        apply_gain(1, 1, (), h1_bf[:, PACK * W :])
+        apply_gain(nc.vector, h0_bf, 0, 1, 0, 2)
+        apply_gain(nc.vector, h0_bf, 0, 1, 2, 4)
+        h_q[0, 0], h_q[0, 1] = quantize(h0_bf[:], PASSES, "h0", "w1_rows")
+        load_old(1, "h0_bf")
+        w2_q[0], w2_q[1] = quantize(w2_bf[:], PASSES, "w2", "silu01")
+        h1_bf = tile([P, PASSES * PACK * W], BF16, "h1_bf", "silu00")
+        apply_gain(nc.gpsimd, h1_bf, 1, 0, 0, 3)
+        apply_gain(nc.vector, h1_bf, 1, 0, 3, 4)
+        apply_gain(nc.vector, h1_bf, 1, 1, 0, 2)
+        apply_gain(nc.vector, h1_bf, 1, 1, 2, 3)
+        apply_gain(nc.vector, h1_bf, 1, 1, 3, 4)
         h_q[1, 0], h_q[1, 1] = quantize(h1_bf[:], PASSES, "h1")
-        step_tiles = [tile([P, TILES * W], F32, "steps0", "table0"), tile([P, TILES * W], F32, "steps1")]
+        behind = tile([P, 2 * TILES * W], F32, "behind", "silu00")
+        step_tiles = [behind[:, 0 : TILES * W], tile([P, TILES * W], F32, "steps1")[:]]
+
+        def diff_room(h, u):
+            if h == 0 and u > 1:
+                return behind[:, (TILES + u) * W : (TILES + u + 1) * W]
+            return tile([P, W], F32, "diff%d%d" % (h, u))[:]
+
         for i, unit in enumerate(units):
             gate(*unit)
             output_diff(*unit)

@@ -121,10 +121,11 @@ def tile_list_register_file_step_kernel(
         order_w1(0, "picked_rows0")
         gather_rows(1, late_rows, "w1_rows")
 
-        w2_raw = tile([P, PASSES, PACK, N], F32, "w2_raw", "w1_rows")
+        w2_raw = {}
 
-        def load_w2(a):
-            nc.sync.dma_start(w2_raw[:, a, :, :], w2[a * W : (a + 1) * W, :].rearrange("(p t) n -> p t n", t=PACK))
+        def load_w2(a, tag):
+            w2_raw[a] = tile([P, PACK, N], F32, "w2_raw%d" % a, tag)
+            nc.sync.dma_start(w2_raw[a][:], w2[a * W : (a + 1) * W, :].rearrange("(p t) n -> p t n", t=PACK))
 
         olds = {}
 
@@ -132,16 +133,17 @@ def tile_list_register_file_step_kernel(
             olds[h] = tile([P, TILES, W], F32, "old%d" % h, tag)
             nc.sync.dma_start(olds[h][:], old[:, h * W : (h + 1) * W].rearrange("(u p) j -> p u j", p=P))
 
-        load_w2(0)
-        load_w2(1)
+        load_w2(0, "w1_rows")
         move_rows(nc.sync, late_planes, late_rows)
+        load_w2(1, "w1_raw0")
 
         picked = {}
 
-        def gather(a, h, tag=None):
-            v = tile([P, W], U32, "picked%d%d" % (a, h), tag)
-            nc.vector.tensor_copy(v[:], table[a][:].indirect(offsets_of(h)))
-            picked[a, h] = v
+        def gather(a, h, c0=0, c1=W, tag=None):
+            if c0 == 0:
+                picked[a, h] = tile([P, W], U32, "picked%d%d" % (a, h), tag)
+            listed = offsets_of(h)[:, c0 // 16 : c1 // 16]
+            nc.vector.tensor_copy(picked[a, h][:, c0:c1], table[a][:].indirect(listed))
 
         def table_operand(a, h, c0, c1):
             return {"rhs": picked[a, h][:, c0:c1].bitcast(FP8X4), "rhs_scale": (planes, late_planes)[h][:, a, c0:c1]}
@@ -171,15 +173,20 @@ def tile_list_register_file_step_kernel(
             silus[h, b] = s
 
 
-        gain_copy = tile([P, PASSES, PACK], F32, "gain_copy")
-        nc.scalar.copy(gain_copy[:], gains[:, 0:PASSES, :])
+        gain_copy = {}
+
+        def copy_gains(copy, b, tag=None):
+            gain_copy[b] = tile([P, PACK], F32, "gain_copy%d" % b, tag)
+            copy(gain_copy[b][:], gains[:, b, :])
+
+        copy_gains(nc.scalar.copy, 0)
 
         def apply_gain(engine, x, h, b, q0, q1):
-            factor = gain_copy if engine is nc.gpsimd else gains
+            factor = gain_copy[b][:] if engine is nc.gpsimd else gains[:, b, :]
             engine.tensor_tensor(
-                x[:, (b * PACK + q0) * W : (b * PACK + q1) * W].rearrange("p (n t) -> p n t", t=PACK),
+                x[:, q0 * W : q1 * W].rearrange("p (n t) -> p n t", t=PACK),
                 silus[h, b][:, q0 * W : q1 * W].rearrange("p (n t) -> p n t", t=PACK),
-                factor[:, b, :].unsqueeze(1).broadcast_to([P, (q1 - q0) * P, PACK]),
+                factor.unsqueeze(1).broadcast_to([P, (q1 - q0) * P, PACK]),
                 ALU.mult,
             )
 
@@ -189,22 +196,14 @@ def tile_list_register_file_step_kernel(
             nc.vector.quantize_mx(out=codes[:].bitcast(FP8X4), scales=scales[:], in_=x)
             return [(codes[:, a * W : (a + 1) * W], scales[:, a * W : (a + 1) * W]) for a in range(passes)]
 
-        def round_w2(a):
-            for u in range(TILES):
-                nc.scalar.copy(
-                    w2_bf[:, (a * N + u * P) * PACK : (a * N + (u + 1) * P) * PACK].rearrange("p (c i t) -> p c t i", t=PACK, i=4),
-                    w2_raw[:, a, :, u * P : (u + 1) * P].rearrange("p t (c i) -> p c t i", i=4),
-                )
+        w2_bf = {}
 
-        def round_w2_gpsimd(a):
-            for c in range(0, N, N // 2):
-                nc.gpsimd.tensor_scalar(
-                    w2_bf[:, (a * N + c) * PACK : (a * N + c + N // 2) * PACK].rearrange("p (c t) -> p c t", t=PACK),
-                    w2_raw[:, a, :, c : c + N // 2].rearrange("p t c -> p c t"),
-                    1.0,
-                    0.0,
-                    ALU.mult,
-                    ALU.add,
+        def round_w2(copy, a, pieces, tag):
+            w2_bf[a] = tile([P, PACK * N], BF16, "w2_bf%d" % a, tag)
+            for c in range(0, N, N // pieces):
+                copy(
+                    w2_bf[a][:, c * PACK : (c + N // pieces) * PACK].rearrange("p (c i t) -> p c t i", t=PACK, i=4),
+                    w2_raw[a][:, :, c : c + N // pieces].rearrange("p t (c i) -> p c t i", i=4),
                 )
 
         h_q = {}
@@ -283,37 +282,42 @@ def tile_list_register_file_step_kernel(
                 start=(i == 0),
                 stop=(i == 2),
             )
-        gather(1, 0)
+        gather(1, 0, 0, W // 2)
+        gather(1, 0, W // 2, W)
         features(0, 0)
         order_w1(1)
         gather(1, 1)
-        gather(0, 1, "w1_raw1")
+        gather(0, 1, tag="w1_raw1")
         features(0, 1)
         w3 = tile([P, PASSES, N], U32, "w3", "late_rows")
         nc.sync.dma_start(w3[:].bitcast(I32), w3_words.rearrange("b p c i -> p b (c i)").bitcast(I32))
         load_old(0, "table1")
-        h0_bf = tile([P, PASSES * PACK * W], BF16, "h0_bf")
-        apply_gain(nc.gpsimd, h0_bf, 0, 0, 0, 1)
-        apply_gain(nc.gpsimd, h0_bf, 0, 0, 1, 2)
-        apply_gain(nc.vector, h0_bf, 0, 0, 2, 4)
-        w2_bf = tile([P, PASSES * PACK * N], BF16, "w2_bf", "silu00")
-        round_w2(0)
-        round_w2_gpsimd(1)
+        h00_bf = tile([P, PACK * W], BF16, "h00_bf")
+        apply_gain(nc.gpsimd, h00_bf, 0, 0, 0, 1)
+        apply_gain(nc.gpsimd, h00_bf, 0, 0, 1, 2)
+        apply_gain(nc.vector, h00_bf, 0, 0, 2, 3)
+        apply_gain(nc.vector, h00_bf, 0, 0, 3, 4)
+        round_w2(nc.scalar.copy, 0, TILES, "silu00")
+        h_q[0, 0] = quantize(h00_bf[:], 1, "h00")[0]
+        load_old(1, "w1_rows")
         features(1, 0)
         features(1, 1)
-        apply_gain(nc.vector, h0_bf, 0, 1, 0, 2)
-        apply_gain(nc.vector, h0_bf, 0, 1, 2, 4)
-        h_q[0, 0], h_q[0, 1] = quantize(h0_bf[:], PASSES, "h0", "w1_rows")
-        load_old(1, "h0_bf")
-        w2_q[0], w2_q[1] = quantize(w2_bf[:], PASSES, "w2", "silu01")
-        h1_bf = tile([P, PASSES * PACK * W], BF16, "h1_bf", "silu00")
-        apply_gain(nc.gpsimd, h1_bf, 1, 0, 0, 3)
-        apply_gain(nc.vector, h1_bf, 1, 0, 3, 4)
-        apply_gain(nc.vector, h1_bf, 1, 1, 0, 2)
-        apply_gain(nc.vector, h1_bf, 1, 1, 2, 3)
-        apply_gain(nc.vector, h1_bf, 1, 1, 3, 4)
+        h01_bf = tile([P, PACK * W], BF16, "h01_bf")
+        apply_gain(nc.vector, h01_bf, 0, 1, 0, 2)
+        apply_gain(nc.vector, h01_bf, 0, 1, 2, 4)
+        round_w2(nc.vector.tensor_copy, 1, 1, "silu01")
+        h_q[0, 1] = quantize(h01_bf[:], 1, "h01")[0]
+        h1_bf = tile([P, PASSES * PACK * W], BF16, "h1_bf")
+        w2_q[0] = quantize(w2_bf[0][:], 1, "w20", "h01_bf")[0]
+        w2_q[1] = quantize(w2_bf[1][:], 1, "w21")[0]
+        apply_gain(nc.vector, h1_bf, 1, 0, 0, 2)
+        apply_gain(nc.gpsimd, h1_bf, 1, 0, 2, 3)
+        apply_gain(nc.gpsimd, h1_bf, 1, 0, 3, 4)
+        apply_gain(nc.vector, h1_bf[:, PACK * W :], 1, 1, 0, 2)
+        apply_gain(nc.vector, h1_bf[:, PACK * W :], 1, 1, 2, 3)
+        apply_gain(nc.vector, h1_bf[:, PACK * W :], 1, 1, 3, 4)
         h_q[1, 0], h_q[1, 1] = quantize(h1_bf[:], PASSES, "h1")
-        behind = tile([P, 2 * TILES * W], F32, "behind", "silu00")
+        behind = tile([P, 2 * TILES * W], F32, "behind", "h1_bf")
         step_tiles = [behind[:, 0 : TILES * W], tile([P, TILES * W], F32, "steps1")[:]]
 
         def diff_room(h, u):

@@ -151,8 +151,10 @@ def tile_list_register_file_step_kernel(
         silus = {}
 
         def features(h, b):
-            s = tile([P, W * PACK], F32, "silu%d%d" % (h, b))
             for q in range(W // P):
+                if q % 2 == 0:
+                    silus[h, b, q // 2] = tile([P, 2 * W], F32, "silu%d%d%d" % (h, b, q // 2))
+                s = silus[h, b, q // 2]
                 bank = psum.tile([P, PACK * P], F32, name="bank", tag="bank")
                 for t in range(PACK):
                     for a in range(PASSES):
@@ -166,11 +168,10 @@ def tile_list_register_file_step_kernel(
                             **table_operand(a, h, q * P, (q + 1) * P),
                         )
                 nc.scalar.activation(
-                    s[:, q * W : (q + 1) * W].rearrange("p (n t) -> p n t", t=PACK),
+                    s[:, q % 2 * W : (q % 2 + 1) * W].rearrange("p (n t) -> p n t", t=PACK),
                     bank[:].rearrange("p (t n) -> p n t", t=PACK),
                     ACT.Silu,
                 )
-            silus[h, b] = s
 
 
         gain_copy = {}
@@ -180,12 +181,13 @@ def tile_list_register_file_step_kernel(
             copy(gain_copy[b][:], gains[:, b, :])
 
         copy_gains(nc.scalar.copy, 0)
+        copy_gains(nc.scalar.copy, 1)
 
         def apply_gain(engine, x, h, b, q0, q1):
             factor = gain_copy[b][:] if engine is nc.gpsimd else gains[:, b, :]
             engine.tensor_tensor(
                 x[:, q0 * W : q1 * W].rearrange("p (n t) -> p n t", t=PACK),
-                silus[h, b][:, q0 * W : q1 * W].rearrange("p (n t) -> p n t", t=PACK),
+                silus[h, b, q0 // 2][:, q0 % 2 * W : (q0 % 2 + q1 - q0) * W].rearrange("p (n t) -> p n t", t=PACK),
                 factor.unsqueeze(1).broadcast_to([P, (q1 - q0) * P, PACK]),
                 ALU.mult,
             )
@@ -261,7 +263,7 @@ def tile_list_register_file_step_kernel(
             steps[h, u] = m
 
         def finish(h, u, c0, c1):
-            room = units[(units.index((h, u)) + 2) % len(units)]
+            room = units[(units.index((h, u)) + 3) % len(units)]
             r = olds[room[0]][:, room[1], c0:c1]
             factor = -1.0 if (h, u) in on_gpsimd else -0.5
             nc.vector.scalar_tensor_tensor(r, steps[h, u][:, c0:c1], factor, ys[h, u][:, c0:c1], ALU.mult, ALU.add)
@@ -297,27 +299,30 @@ def tile_list_register_file_step_kernel(
         apply_gain(nc.gpsimd, h00_bf, 0, 0, 1, 2)
         apply_gain(nc.vector, h00_bf, 0, 0, 2, 3)
         apply_gain(nc.vector, h00_bf, 0, 0, 3, 4)
-        round_w2(nc.scalar.copy, 0, TILES, "silu00")
+        round_w2(nc.scalar.copy, 0, TILES, "silu001")
         h_q[0, 0] = quantize(h00_bf[:], 1, "h00")[0]
         load_old(1, "w1_rows")
         features(1, 0)
         features(1, 1)
         h01_bf = tile([P, PACK * W], BF16, "h01_bf")
-        apply_gain(nc.vector, h01_bf, 0, 1, 0, 2)
+        apply_gain(nc.vector, h01_bf, 0, 1, 0, 1)
+        apply_gain(nc.gpsimd, h01_bf, 0, 1, 1, 2)
         apply_gain(nc.vector, h01_bf, 0, 1, 2, 4)
-        round_w2(nc.vector.tensor_copy, 1, 1, "silu01")
+        round_w2(nc.vector.tensor_copy, 1, 1, "silu011")
         h_q[0, 1] = quantize(h01_bf[:], 1, "h01")[0]
-        h1_bf = tile([P, PASSES * PACK * W], BF16, "h1_bf")
         w2_q[0] = quantize(w2_bf[0][:], 1, "w20", "h01_bf")[0]
         w2_q[1] = quantize(w2_bf[1][:], 1, "w21")[0]
-        apply_gain(nc.vector, h1_bf, 1, 0, 0, 2)
-        apply_gain(nc.gpsimd, h1_bf, 1, 0, 2, 3)
-        apply_gain(nc.gpsimd, h1_bf, 1, 0, 3, 4)
-        apply_gain(nc.vector, h1_bf[:, PACK * W :], 1, 1, 0, 2)
-        apply_gain(nc.vector, h1_bf[:, PACK * W :], 1, 1, 2, 3)
-        apply_gain(nc.vector, h1_bf[:, PACK * W :], 1, 1, 3, 4)
-        h_q[1, 0], h_q[1, 1] = quantize(h1_bf[:], PASSES, "h1")
-        behind = tile([P, 2 * TILES * W], F32, "behind", "h1_bf")
+        h10_bf = tile([P, PACK * W], BF16, "h10_bf")
+        h11_bf = tile([P, PACK * W], BF16, "h11_bf")
+        apply_gain(nc.vector, h10_bf, 1, 0, 0, 2)
+        apply_gain(nc.gpsimd, h10_bf, 1, 0, 2, 3)
+        apply_gain(nc.gpsimd, h10_bf, 1, 0, 3, 4)
+        apply_gain(nc.vector, h11_bf, 1, 1, 0, 2)
+        apply_gain(nc.vector, h11_bf, 1, 1, 2, 3)
+        apply_gain(nc.vector, h11_bf, 1, 1, 3, 4)
+        h_q[1, 0] = quantize(h10_bf[:], 1, "h10", "silu110")[0]
+        h_q[1, 1] = quantize(h11_bf[:], 1, "h11")[0]
+        behind = tile([P, 2 * TILES * W], F32, "behind", "h11_bf")
         step_tiles = [behind[:, 0 : TILES * W], tile([P, TILES * W], F32, "steps1")[:]]
 
         def diff_room(h, u):
@@ -328,9 +333,10 @@ def tile_list_register_file_step_kernel(
         for i, unit in enumerate(units):
             gate(*unit)
             output_diff(*unit)
-            if i >= 2:
-                finish(*units[i - 2], 0, W)
             step(*unit)
-        finish(*units[-2], 0, W)
-        finish(*units[-1], 0, W // 2)
-        finish(*units[-1], W // 2, W)
+            if i >= 3:
+                finish(*units[i - 3], 0, W)
+        finish(*units[-3], 0, W)
+        finish(*units[-1], 0, W)
+        finish(*units[-2], 0, W // 2)
+        finish(*units[-2], W // 2, W)

@@ -181,7 +181,6 @@ def tile_list_register_file_step_kernel(
             copy(gain_copy[b][:], gains[:, b, :])
 
         copy_gains(nc.scalar.copy, 0)
-        copy_gains(nc.scalar.copy, 1)
 
         def apply_gain(engine, x, h, b, q0, q1):
             factor = gain_copy[b][:] if engine is nc.gpsimd else gains[:, b, :]
@@ -256,6 +255,8 @@ def tile_list_register_file_step_kernel(
 
         def step(h, u):
             m = step_tiles[h][:, u * W : (u + 1) * W]
+            if (h, u) == on_gpsimd[0]:
+                m = tile([P, W], F32, "step02", "tanh01")[:]
             if (h, u) in on_gpsimd:
                 nc.gpsimd.tensor_tensor(m, tanhs[h, u][:], diffs[h, u], ALU.mult)
             else:
@@ -270,7 +271,7 @@ def tile_list_register_file_step_kernel(
             nc.sync.dma_start(out[u * P : (u + 1) * P, h * W + c0 : h * W + c1], r)
 
         units = [(h, u) for h in range(HALVES) for u in range(TILES)]
-        on_gpsimd = [unit for unit in units if unit[1] != TILES - 1]
+        on_gpsimd = units[2:]
 
         gather(0, 0)
         warm_bank = psum.tile([P, W], F32, name="bank", tag="bank")
@@ -305,8 +306,7 @@ def tile_list_register_file_step_kernel(
         features(1, 0)
         features(1, 1)
         h01_bf = tile([P, PACK * W], BF16, "h01_bf")
-        apply_gain(nc.vector, h01_bf, 0, 1, 0, 1)
-        apply_gain(nc.gpsimd, h01_bf, 0, 1, 1, 2)
+        apply_gain(nc.vector, h01_bf, 0, 1, 0, 2)
         apply_gain(nc.vector, h01_bf, 0, 1, 2, 4)
         round_w2(nc.vector.tensor_copy, 1, 1, "silu011")
         h_q[0, 1] = quantize(h01_bf[:], 1, "h01")[0]
@@ -326,7 +326,7 @@ def tile_list_register_file_step_kernel(
         step_tiles = [behind[:, 0 : TILES * W], tile([P, TILES * W], F32, "steps1")[:]]
 
         def diff_room(h, u):
-            if h == 0 and u > 1:
+            if h == 0 and u > 2:
                 return behind[:, (TILES + u) * W : (TILES + u + 1) * W]
             return tile([P, W], F32, "diff%d%d" % (h, u))[:]
 
@@ -337,6 +337,6 @@ def tile_list_register_file_step_kernel(
             if i >= 3:
                 finish(*units[i - 3], 0, W)
         finish(*units[-3], 0, W)
-        finish(*units[-1], 0, W)
-        finish(*units[-2], 0, W // 2)
-        finish(*units[-2], W // 2, W)
+        finish(*units[-2], 0, W)
+        finish(*units[-1], 0, W // 2)
+        finish(*units[-1], W // 2, W)

@@ -23,8 +23,7 @@ PASSES = 2
 W = 512
 HALVES = S // W
 TILES = N // P
-EARLY_ROW = W + H
-LATE_ROW = W + N
+EARLY_ROW = W + H + N
 
 
 def tile_list_register_file_step_kernel(
@@ -33,6 +32,7 @@ def tile_list_register_file_step_kernel(
     nc = tc.nc
     with ExitStack() as ctx:
         keep = ctx.enter_context(tc.tile_pool(name="keep", bufs=1))
+        shared = ctx.enter_context(tc.tile_pool(name="shared", bufs=1))
         psum = ctx.enter_context(tc.psum_pool(name="psum", bufs=8))
 
         def tile(shape, dtype, name, tag=None):
@@ -43,49 +43,48 @@ def tile_list_register_file_step_kernel(
 
         w1_raw = {}
 
-        def load_w1(b, pieces):
-            w1_raw[b] = tile([P, PASSES, 2 * W], U8, "w1_raw%d" % b)
+        def load_w1(b, a0, a1):
+            if a0 == 0:
+                w1_raw[b] = tile([P, PASSES, 2 * W], U8, "w1_raw%d" % b)
             src = w1_words[:, :, 2 * W * b : 2 * W * (b + 1)].bitcast(I32).rearrange("a p c -> p a c")
-            for a0, a1 in pieces:
-                nc.sync.dma_start(w1_raw[b][:, a0:a1, :].bitcast(I32), src[:, a0:a1, :])
+            nc.sync.dma_start(w1_raw[b][:, a0:a1, :].bitcast(I32), src[:, a0:a1, :])
 
-        load_w1(0, [(0, 1), (1, 2)])
+        load_w1(0, 0, 1)
 
         tab_rows = tile([P, T], U8, "tab_rows")
-        w1_rows = tile([P, H], U8, "w1_rows")
-        rows = tile([P, EARLY_ROW], U8, "rows")
-        late_rows = tile([P, LATE_ROW], U8, "late_rows")
+        w1_rows = shared.tile([P, H], U8, name="w1_rows", offset=EARLY_ROW + W, align_bytes=64)
+        rows = shared.tile([P, EARLY_ROW], U8, name="rows", offset=0, align_bytes=64)
         planes = tile([P, PASSES, EARLY_ROW], U8, "planes")
-        late_planes = tile([P, PASSES, LATE_ROW], U8, "late_planes")
         warm = tile([P, 2], F32, "warm")
-        nc.vector.memset(tab_rows[:].bitcast(I32), 0)
-        nc.gpsimd.memset(w1_rows[:].bitcast(I32), 0)
-        nc.vector.memset(late_rows[:, W:].bitcast(I32), 0)
-        nc.vector.memset(warm[:, 0:1], 0.0)
+        nc.gpsimd.memset(tab_rows[:].bitcast(I32), 0)
+        nc.vector.memset(w1_rows[:].bitcast(I32), 0)
         nc.vector.memset(planes[:].rearrange("p a c -> p (a c)").bitcast(I32), 0)
-        nc.vector.memset(late_planes[:].rearrange("p a c -> p (a c)").bitcast(I32), 0)
+        nc.vector.memset(warm[:, 0:1], 0.0)
         gain_rows = tile([P, W], F32, "gain_rows")
         identity = tile([P, P], F32, "identity")
         nc.gpsimd.memset(gain_rows[:], 0.0)
         make_identity(nc, identity[:])
+
+        def load_rows(queue, dst, scales):
+            queue.dma_start(dst.bitcast(I32), scales.bitcast(I32).rearrange("a q c -> q a c"))
+
+        load_rows(nc.sync, tab_rows[0:P:4, :], tab_scales)
+        load_rows(nc.sync, w1_rows[0:P:4, :], w1_scales)
+        load_rows(nc.scalar, rows[0:P:4, W + H :], w3_scales)
+
         nc.scalar.activation(warm[:, 1:2], warm[:, 0:1], ACT.Silu)
-
-        def load_rows(dst, scales):
-            nc.sync.dma_start(dst.bitcast(I32), scales.bitcast(I32).rearrange("a q c -> q a c"))
-
-        load_rows(tab_rows[0:P:4, :], tab_scales)
-        load_rows(w1_rows[0:P:4, :], w1_scales)
-        load_rows(late_rows[0:P:4, W:], w3_scales)
-        nc.sync.dma_start(gain_rows[0:PASSES, :], gain.rearrange("(b k) -> b k", b=PASSES))
 
         table = []
         for a in range(PASSES):
             words = tile([P, T], U32, "table%d" % a)
             nc.sync.dma_start(words[:].bitcast(I32), tab_words[a].rearrange("p t i -> p (t i)").bitcast(I32))
             table.append(words)
+            if a == 0:
+                load_w1(0, 1, 2)
+                nc.sync.dma_start(gain_rows[0:PASSES, :], gain.rearrange("(b k) -> b k", b=PASSES))
 
 
-        load_w1(1, [(0, 2)])
+        load_w1(1, 0, 2)
         gain_bank = psum.tile([P, PACK * P], F32, name="gain_bank", tag="bank")
         for t in range(PACK):
             nc.tensor.transpose(gain_bank[:, t:W:PACK], gain_rows[:, t:W:PACK], identity[:])
@@ -103,39 +102,36 @@ def tile_list_register_file_step_kernel(
         def offsets_of(h):
             return offsets[:, h * (W // 16) : (h + 1) * (W // 16)]
 
-        def gather_rows(h, dst, tag=None):
+        def gather_rows(h, tag=None):
             picked_rows = tile([P, W], U8, "picked_rows%d" % h, tag)
             nc.vector.tensor_copy(picked_rows[:], tab_rows[:].indirect(offsets_of(h)))
-            nc.vector.tensor_copy(dst[:, 0:W].bitcast(I32), picked_rows[:].bitcast(I32))
+            return picked_rows
 
-        def move_rows(queue, dst, src):
-            for d in (0, 2, 1, 3):
+        def move_rows(queues, dst, src):
+            for queue, d in zip(queues, (0, 2, 1, 3)):
                 queue.dma_start(dst[32 * d : 32 * d + 4, :, :].bitcast(I32), src[32 * d : 32 * d + 32 : 4, :].bitcast(I32))
 
         nc.gpsimd.tensor_copy(
-            rows[:, W:].rearrange("p (b t m) -> p b t m", b=2, t=PACK),
+            rows[:, W : W + H].rearrange("p (b t m) -> p b t m", b=2, t=PACK),
             w1_rows[:].rearrange("p (b m t) -> p b t m", b=2, t=PACK),
         )
-        gather_rows(0, rows)
-        move_rows(nc.scalar, planes, rows)
-        order_w1(0, "picked_rows0")
-        gather_rows(1, late_rows, "w1_rows")
+        nc.vector.tensor_copy(rows[:, 0:W].bitcast(I32), gather_rows(0)[:].bitcast(I32))
+        move_rows((nc.scalar, nc.sync, nc.scalar, nc.sync), planes, rows)
+        order_w1(0)
+        late_rows = gather_rows(1)
 
         w2_raw = {}
 
-        def load_w2(a, tag):
-            w2_raw[a] = tile([P, PACK, N], F32, "w2_raw%d" % a, tag)
-            nc.sync.dma_start(w2_raw[a][:], w2[a * W : (a + 1) * W, :].rearrange("(p t) n -> p t n", t=PACK))
+        def load_w2(a, room):
+            w2_raw[a] = room.rearrange("p (t n) -> p t n", t=PACK)
+            nc.sync.dma_start(w2_raw[a], w2[a * W : (a + 1) * W, :].rearrange("(p t) n -> p t n", t=PACK))
 
         olds = {}
 
-        def load_old(h, tag):
-            olds[h] = tile([P, TILES, W], F32, "old%d" % h, tag)
-            nc.sync.dma_start(olds[h][:], old[:, h * W : (h + 1) * W].rearrange("(u p) j -> p u j", p=P))
+        def load_old(h, both):
+            olds[h] = both[:, (2 + h) * PACK * N : (3 + h) * PACK * N].rearrange("p (u j) -> p u j", u=TILES)
+            nc.sync.dma_start(olds[h], old[:, h * W : (h + 1) * W].rearrange("(u p) j -> p u j", p=P))
 
-        load_w2(0, "w1_rows")
-        move_rows(nc.sync, late_planes, late_rows)
-        load_w2(1, "w1_raw0")
 
         picked = {}
 
@@ -150,44 +146,32 @@ def tile_list_register_file_step_kernel(
 
         silus = {}
 
-        def features(h, b):
-            for q in range(W // P):
-                if q % 2 == 0:
-                    silus[h, b, q // 2] = tile([P, 2 * W], F32, "silu%d%d%d" % (h, b, q // 2))
-                s = silus[h, b, q // 2]
-                bank = psum.tile([P, PACK * P], F32, name="bank", tag="bank")
-                for t in range(PACK):
-                    for a in range(PASSES):
-                        c = W + b * W + t * P
-                        nc.tensor.matmul_mx(
-                            bank[:, t * P : (t + 1) * P],
-                            lhsT=w1[b][:, 2 * (a * W + t * P) : 2 * (a * W + (t + 1) * P)].bitcast(FP4X4),
-                            lhsT_scale=planes[:, a, c : c + P],
-                            start=(a == 0),
-                            stop=(a == PASSES - 1),
-                            **table_operand(a, h, q * P, (q + 1) * P),
-                        )
-                nc.scalar.activation(
-                    s[:, q % 2 * W : (q % 2 + 1) * W].rearrange("p (n t) -> p n t", t=PACK),
-                    bank[:].rearrange("p (t n) -> p n t", t=PACK),
-                    ACT.Silu,
-                )
+        def feature_bank(h, b, q):
+            silus[h, b, q] = tile([P, W], F32, "silu%d%d%d" % (h, b, q))
+            bank = psum.tile([P, PACK * P], F32, name="bank", tag="bank")
+            for t in range(PACK):
+                for a in range(PASSES):
+                    c = W + b * W + t * P
+                    nc.tensor.matmul_mx(
+                        bank[:, t * P : (t + 1) * P],
+                        lhsT=w1[b][:, 2 * (a * W + t * P) : 2 * (a * W + (t + 1) * P)].bitcast(FP4X4),
+                        lhsT_scale=planes[:, a, c : c + P],
+                        start=(a == 0),
+                        stop=(a == PASSES - 1),
+                        **table_operand(a, h, q * P, (q + 1) * P),
+                    )
+            nc.scalar.activation(
+                silus[h, b, q][:].rearrange("p (n t) -> p n t", t=PACK),
+                bank[:].rearrange("p (t n) -> p n t", t=PACK),
+                ACT.Silu,
+            )
 
-
-        gain_copy = {}
-
-        def copy_gains(copy, b, tag=None):
-            gain_copy[b] = tile([P, PACK], F32, "gain_copy%d" % b, tag)
-            copy(gain_copy[b][:], gains[:, b, :])
-
-        copy_gains(nc.scalar.copy, 0)
-
-        def apply_gain(engine, x, h, b, q0, q1):
-            factor = gain_copy[b][:] if engine is nc.gpsimd else gains[:, b, :]
+        def apply_gain(engine, x, h, b, q):
+            factor = gain_copy[:, b, :] if engine is nc.gpsimd else gains[:, b, :]
             engine.tensor_tensor(
-                x[:, q0 * W : q1 * W].rearrange("p (n t) -> p n t", t=PACK),
-                silus[h, b, q0 // 2][:, q0 % 2 * W : (q0 % 2 + q1 - q0) * W].rearrange("p (n t) -> p n t", t=PACK),
-                factor.unsqueeze(1).broadcast_to([P, (q1 - q0) * P, PACK]),
+                x[:, q * W : (q + 1) * W].rearrange("p (n t) -> p n t", t=PACK),
+                silus[h, b, q][:].rearrange("p (n t) -> p n t", t=PACK),
+                factor.unsqueeze(1).broadcast_to([P, P, PACK]),
                 ALU.mult,
             )
 
@@ -199,13 +183,13 @@ def tile_list_register_file_step_kernel(
 
         w2_bf = {}
 
-        def round_w2(copy, a, pieces, tag):
-            w2_bf[a] = tile([P, PACK * N], BF16, "w2_bf%d" % a, tag)
-            for c in range(0, N, N // pieces):
-                copy(
-                    w2_bf[a][:, c * PACK : (c + N // pieces) * PACK].rearrange("p (c i t) -> p c t i", t=PACK, i=4),
-                    w2_raw[a][:, :, c : c + N // pieces].rearrange("p t (c i) -> p c t i", i=4),
-                )
+        def round_w2(copy, a, c0, c1, tag=None):
+            if c0 == 0:
+                w2_bf[a] = tile([P, PACK * N], BF16, "w2_bf%d" % a, tag)
+            copy(
+                w2_bf[a][:, c0 * PACK : c1 * PACK].rearrange("p (c i t) -> p c t i", t=PACK, i=4),
+                w2_raw[a][:, :, c0:c1].rearrange("p t (c i) -> p c t i", i=4),
+            )
 
         h_q = {}
         w2_q = {}
@@ -220,7 +204,7 @@ def tile_list_register_file_step_kernel(
                 nc.tensor.matmul_mx(
                     bank[:],
                     lhsT=w3[:, b, u * P : (u + 1) * P].bitcast(FP8X4),
-                    lhsT_scale=late_planes[:, b, W + u * P : W + (u + 1) * P],
+                    lhsT_scale=planes[:, b, W + H + u * P : W + H + (u + 1) * P],
                     rhs=codes.bitcast(FP8X4),
                     rhs_scale=scales,
                     start=(b == 0),
@@ -285,44 +269,66 @@ def tile_list_register_file_step_kernel(
                 start=(i == 0),
                 stop=(i == 2),
             )
+        gain_copy = shared.tile([P, PASSES, PACK], F32, name="gain_copy", offset=0, align_bytes=64)
+        nc.scalar.copy(gain_copy[:], gains[:, 0:PASSES, :])
+        late_planes = shared.tile([P, PASSES, W], U8, name="late_planes", offset=EARLY_ROW, align_bytes=64)
+        nc.gpsimd.memset(late_planes[:].rearrange("p a c -> p (a c)").bitcast(I32), 0)
+        w2_both = shared.tile([P, (PASSES + HALVES) * PACK * N], F32, name="w2_both", offset=EARLY_ROW + PASSES * W, align_bytes=64)
+        load_w2(0, w2_both[:, 0 : PACK * N])
+        move_rows((nc.sync,) * 4, late_planes, late_rows)
+        load_w2(1, w2_both[:, PACK * N : 2 * PACK * N])
+        gather(0, 1)
         gather(1, 0, 0, W // 2)
         gather(1, 0, W // 2, W)
-        features(0, 0)
+        for q in range(PACK):
+            feature_bank(0, 0, q)
         order_w1(1)
         gather(1, 1)
-        gather(0, 1, tag="w1_raw1")
-        features(0, 1)
-        w3 = tile([P, PASSES, N], U32, "w3", "late_rows")
+        w3 = tile([P, PASSES, N], U32, "w3", "w1_raw0")
         nc.sync.dma_start(w3[:].bitcast(I32), w3_words.rearrange("b p c i -> p b (c i)").bitcast(I32))
-        load_old(0, "table1")
-        h00_bf = tile([P, PACK * W], BF16, "h00_bf")
-        apply_gain(nc.gpsimd, h00_bf, 0, 0, 0, 1)
-        apply_gain(nc.gpsimd, h00_bf, 0, 0, 1, 2)
-        apply_gain(nc.vector, h00_bf, 0, 0, 2, 3)
-        apply_gain(nc.vector, h00_bf, 0, 0, 3, 4)
-        round_w2(nc.scalar.copy, 0, TILES, "silu001")
-        h_q[0, 0] = quantize(h00_bf[:], 1, "h00")[0]
-        load_old(1, "w1_rows")
-        features(1, 0)
-        features(1, 1)
-        h01_bf = tile([P, PACK * W], BF16, "h01_bf")
-        apply_gain(nc.vector, h01_bf, 0, 1, 0, 2)
-        apply_gain(nc.vector, h01_bf, 0, 1, 2, 4)
-        round_w2(nc.vector.tensor_copy, 1, 1, "silu011")
-        h_q[0, 1] = quantize(h01_bf[:], 1, "h01")[0]
-        w2_q[0] = quantize(w2_bf[0][:], 1, "w20", "h01_bf")[0]
+        load_old(0, w2_both)
+        load_old(1, w2_both)
+
+        h_room = tile([P, (PACK + 3 * (PACK - 1)) * W], BF16, "h_room")
+
+        def h_bf(h, b):
+            c = (PASSES * h + b) * (PACK - 1) * W
+            return h_room[:, c : c + PACK * W]
+
+        def gains_of(h, b, on_pool, q0=0, q1=PACK):
+            for q in range(q0, q1):
+                apply_gain(nc.gpsimd if q in on_pool else nc.vector, h_bf(h, b), h, b, q)
+
+        def quantize_h(h, b):
+            h_q[h, b] = quantize(h_bf(h, b), 1, "h%d%d" % (h, b))[0]
+
+        gains_of(0, 0, (0,))
+        quantize_h(0, 0)
+        round_w2(nc.scalar.copy, 0, 0, P, "silu000")
+        feature_bank(0, 1, 0)
+        feature_bank(0, 1, 1)
+        round_w2(nc.scalar.copy, 0, P, 2 * P)
+        feature_bank(0, 1, 2)
+        feature_bank(0, 1, 3)
+        round_w2(nc.scalar.copy, 0, 2 * P, 3 * P)
+        gains_of(0, 1, (0,), 0, 3)
+        round_w2(nc.vector.tensor_copy, 1, 0, N, "silu010")
+        gains_of(0, 1, (0,), 3, 4)
         w2_q[1] = quantize(w2_bf[1][:], 1, "w21")[0]
-        h10_bf = tile([P, PACK * W], BF16, "h10_bf")
-        h11_bf = tile([P, PACK * W], BF16, "h11_bf")
-        apply_gain(nc.vector, h10_bf, 1, 0, 0, 2)
-        apply_gain(nc.gpsimd, h10_bf, 1, 0, 2, 3)
-        apply_gain(nc.gpsimd, h10_bf, 1, 0, 3, 4)
-        apply_gain(nc.vector, h11_bf, 1, 1, 0, 2)
-        apply_gain(nc.vector, h11_bf, 1, 1, 2, 3)
-        apply_gain(nc.vector, h11_bf, 1, 1, 3, 4)
-        h_q[1, 0] = quantize(h10_bf[:], 1, "h10", "silu110")[0]
-        h_q[1, 1] = quantize(h11_bf[:], 1, "h11")[0]
-        behind = tile([P, 2 * TILES * W], F32, "behind", "h11_bf")
+        quantize_h(0, 1)
+        feature_bank(1, 0, 0)
+        round_w2(nc.scalar.copy, 0, 3 * P, 4 * P)
+        feature_bank(1, 0, 1)
+        feature_bank(1, 0, 2)
+        feature_bank(1, 0, 3)
+        gains_of(1, 0, (0,))
+        w2_q[0] = quantize(w2_bf[0][:], 1, "w20", "silu100")[0]
+        quantize_h(1, 0)
+        for q in range(PACK):
+            feature_bank(1, 1, q)
+        gains_of(1, 1, (0,))
+        quantize_h(1, 1)
+        behind = tile([P, 2 * TILES * W], F32, "behind", "h_room")
         step_tiles = [behind[:, 0 : TILES * W], tile([P, TILES * W], F32, "steps1")[:]]
 
         def diff_room(h, u):

@@ -23,7 +23,8 @@ PASSES = 2
 W = 512
 HALVES = S // W
 TILES = N // P
-EARLY_ROW = W + H + N
+EARLY_ROW = W + W
+LATE_ROW = W + W + N
 
 
 def tile_list_register_file_step_kernel(
@@ -52,13 +53,16 @@ def tile_list_register_file_step_kernel(
         load_w1(0, 0, 1)
 
         tab_rows = tile([P, T], U8, "tab_rows")
-        w1_rows = shared.tile([P, H], U8, name="w1_rows", offset=EARLY_ROW + W, align_bytes=64)
+        w1_rows = tile([P, H], U8, "w1_rows")
+        late_rows = tile([P, LATE_ROW], U8, "late_rows")
+        late_planes = tile([P, PASSES, LATE_ROW], U8, "late_planes")
         rows = shared.tile([P, EARLY_ROW], U8, name="rows", offset=0, align_bytes=64)
         planes = tile([P, PASSES, EARLY_ROW], U8, "planes")
         warm = tile([P, 2], F32, "warm")
         nc.gpsimd.memset(tab_rows[:].bitcast(I32), 0)
         nc.vector.memset(w1_rows[:].bitcast(I32), 0)
         nc.vector.memset(planes[:].rearrange("p a c -> p (a c)").bitcast(I32), 0)
+        nc.vector.memset(late_planes[:].rearrange("p a c -> p (a c)").bitcast(I32), 0)
         nc.vector.memset(warm[:, 0:1], 0.0)
         gain_rows = tile([P, W], F32, "gain_rows")
         identity = tile([P, P], F32, "identity")
@@ -70,7 +74,7 @@ def tile_list_register_file_step_kernel(
 
         load_rows(nc.sync, tab_rows[0:P:4, :], tab_scales)
         load_rows(nc.sync, w1_rows[0:P:4, :], w1_scales)
-        load_rows(nc.scalar, rows[0:P:4, W + H :], w3_scales)
+        load_rows(nc.scalar, late_rows[0:P:4, 2 * W :], w3_scales)
 
         nc.scalar.activation(warm[:, 1:2], warm[:, 0:1], ACT.Silu)
 
@@ -107,18 +111,24 @@ def tile_list_register_file_step_kernel(
             nc.vector.tensor_copy(picked_rows[:], tab_rows[:].indirect(offsets_of(h)))
             return picked_rows
 
-        def move_rows(queues, dst, src):
-            for queue, d in zip(queues, (0, 2, 1, 3)):
+        def move_rows(queue, dst, src):
+            for d in (0, 2, 1, 3):
                 queue.dma_start(dst[32 * d : 32 * d + 4, :, :].bitcast(I32), src[32 * d : 32 * d + 32 : 4, :].bitcast(I32))
 
-        nc.gpsimd.tensor_copy(
-            rows[:, W : W + H].rearrange("p (b t m) -> p b t m", b=2, t=PACK),
-            w1_rows[:].rearrange("p (b m t) -> p b t m", b=2, t=PACK),
-        )
-        nc.vector.tensor_copy(rows[:, 0:W].bitcast(I32), gather_rows(0)[:].bitcast(I32))
-        move_rows((nc.scalar, nc.sync, nc.scalar, nc.sync), planes, rows)
+        def order_w1_scales(b, dst):
+            nc.gpsimd.tensor_copy(
+                dst[:, W : 2 * W].rearrange("p (t m) -> p t m", t=PACK),
+                w1_rows[:, b * W : (b + 1) * W].rearrange("p (m t) -> p t m", t=PACK),
+            )
+
+        order_w1_scales(0, rows)
+        first_rows = gather_rows(0)
+        nc.vector.tensor_copy(rows[:, 0:W].bitcast(I32), first_rows[:].bitcast(I32))
+        move_rows(nc.scalar, planes, rows)
+        order_w1_scales(1, late_rows)
         order_w1(0)
-        late_rows = gather_rows(1)
+        nc.vector.tensor_copy(late_rows[:, 0:W].bitcast(I32), gather_rows(1)[:].bitcast(I32))
+        move_rows(nc.scalar, late_planes, late_rows)
 
         w2_raw = {}
 
@@ -151,11 +161,11 @@ def tile_list_register_file_step_kernel(
             bank = psum.tile([P, PACK * P], F32, name="bank", tag="bank")
             for t in range(PACK):
                 for a in range(PASSES):
-                    c = W + b * W + t * P
+                    c = W + t * P
                     nc.tensor.matmul_mx(
                         bank[:, t * P : (t + 1) * P],
                         lhsT=w1[b][:, 2 * (a * W + t * P) : 2 * (a * W + (t + 1) * P)].bitcast(FP4X4),
-                        lhsT_scale=planes[:, a, c : c + P],
+                        lhsT_scale=(planes, late_planes)[b][:, a, c : c + P],
                         start=(a == 0),
                         stop=(a == PASSES - 1),
                         **table_operand(a, h, q * P, (q + 1) * P),
@@ -204,7 +214,7 @@ def tile_list_register_file_step_kernel(
                 nc.tensor.matmul_mx(
                     bank[:],
                     lhsT=w3[:, b, u * P : (u + 1) * P].bitcast(FP8X4),
-                    lhsT_scale=planes[:, b, W + H + u * P : W + H + (u + 1) * P],
+                    lhsT_scale=late_planes[:, b, 2 * W + u * P : 2 * W + (u + 1) * P],
                     rhs=codes.bitcast(FP8X4),
                     rhs_scale=scales,
                     start=(b == 0),
@@ -263,19 +273,16 @@ def tile_list_register_file_step_kernel(
             nc.tensor.matmul_mx(
                 warm_bank[:],
                 lhsT=w1[0][:, 0 : 2 * P].bitcast(FP4X4),
-                lhsT_scale=rows[:, W : W + P],
+                lhsT_scale=first_rows[:, 0:P],
                 rhs=picked[0, 0][:].bitcast(FP8X4),
-                rhs_scale=rows[:, 0:W],
+                rhs_scale=first_rows[:],
                 start=(i == 0),
                 stop=(i == 2),
             )
         gain_copy = shared.tile([P, PASSES, PACK], F32, name="gain_copy", offset=0, align_bytes=64)
         nc.scalar.copy(gain_copy[:], gains[:, 0:PASSES, :])
-        late_planes = shared.tile([P, PASSES, W], U8, name="late_planes", offset=EARLY_ROW, align_bytes=64)
-        nc.gpsimd.memset(late_planes[:].rearrange("p a c -> p (a c)").bitcast(I32), 0)
-        w2_both = shared.tile([P, (PASSES + HALVES) * PACK * N], F32, name="w2_both", offset=EARLY_ROW + PASSES * W, align_bytes=64)
+        w2_both = shared.tile([P, (PASSES + HALVES) * PACK * N], F32, name="w2_both", offset=W, align_bytes=64)
         load_w2(0, w2_both[:, 0 : PACK * N])
-        move_rows((nc.sync,) * 4, late_planes, late_rows)
         load_w2(1, w2_both[:, PACK * N : 2 * PACK * N])
         gather(0, 1)
         gather(1, 0, 0, W // 2)
@@ -284,7 +291,7 @@ def tile_list_register_file_step_kernel(
             feature_bank(0, 0, q)
         order_w1(1)
         gather(1, 1)
-        w3 = tile([P, PASSES, N], U32, "w3", "w1_raw0")
+        w3 = tile([P, PASSES, N], U32, "w3", "table0")
         nc.sync.dma_start(w3[:].bitcast(I32), w3_words.rearrange("b p c i -> p b (c i)").bitcast(I32))
         load_old(0, w2_both)
         load_old(1, w2_both)

@@ -98,7 +98,7 @@ def tile_list_register_file_step_kernel(
 
         def order_w1(b, tag=None):
             w1[b] = tile([P, PASSES * 2 * W], U8, "w1_%d" % b, tag)
-            nc.gpsimd.tensor_copy(
+            nc.vector.tensor_copy(
                 w1[b][:].bitcast(U16).rearrange("p (a t m) -> p a t m", a=PASSES, t=PACK),
                 w1_raw[b][:].rearrange("p a c -> p (a c)").bitcast(U16).rearrange("p (a m t) -> p a t m", a=PASSES, t=PACK),
             )
@@ -116,7 +116,7 @@ def tile_list_register_file_step_kernel(
                 queue.dma_start(dst[32 * d : 32 * d + 4, :, :].bitcast(I32), src[32 * d : 32 * d + 32 : 4, :].bitcast(I32))
 
         def order_w1_scales(b, dst):
-            nc.gpsimd.tensor_copy(
+            nc.vector.tensor_copy(
                 dst[:, W : 2 * W].rearrange("p (t m) -> p t m", t=PACK),
                 w1_rows[:, b * W : (b + 1) * W].rearrange("p (m t) -> p t m", t=PACK),
             )
@@ -296,7 +296,7 @@ def tile_list_register_file_step_kernel(
         load_old(0, w2_both)
         load_old(1, w2_both)
 
-        h_room = tile([P, (PACK + 3 * (PACK - 1)) * W], BF16, "h_room")
+        h_room = tile([P, (PACK + 3 * (PACK - 1)) * W], BF16, "h_room", "table1")
 
         def h_bf(h, b):
             c = (PASSES * h + b) * (PACK - 1) * W
@@ -335,7 +335,7 @@ def tile_list_register_file_step_kernel(
             feature_bank(1, 1, q)
         gains_of(1, 1, (0,))
         quantize_h(1, 1)
-        behind = tile([P, 2 * TILES * W], F32, "behind", "h_room")
+        behind = tile([P, 2 * TILES * W], F32, "behind", "table1")
         step_tiles = [behind[:, 0 : TILES * W], tile([P, TILES * W], F32, "steps1")[:]]
 
         def diff_room(h, u):

@@ -23,8 +23,8 @@ PASSES = 2
 W = 512
 HALVES = S // W
 TILES = N // P
-EARLY_ROW = W + W
-LATE_ROW = W + W + N
+EARLY_ROW = W + H
+LATE_ROW = W + N
 
 
 def tile_list_register_file_step_kernel(
@@ -74,7 +74,7 @@ def tile_list_register_file_step_kernel(
 
         load_rows(nc.sync, tab_rows[0:P:4, :], tab_scales)
         load_rows(nc.sync, w1_rows[0:P:4, :], w1_scales)
-        load_rows(nc.scalar, late_rows[0:P:4, 2 * W :], w3_scales)
+        load_rows(nc.scalar, late_rows[0:P:4, W:], w3_scales)
 
         nc.scalar.activation(warm[:, 1:2], warm[:, 0:1], ACT.Silu)
 
@@ -98,7 +98,7 @@ def tile_list_register_file_step_kernel(
 
         def order_w1(b, tag=None):
             w1[b] = tile([P, PASSES * 2 * W], U8, "w1_%d" % b, tag)
-            nc.vector.tensor_copy(
+            nc.gpsimd.tensor_copy(
                 w1[b][:].bitcast(U16).rearrange("p (a t m) -> p a t m", a=PASSES, t=PACK),
                 w1_raw[b][:].rearrange("p a c -> p (a c)").bitcast(U16).rearrange("p (a m t) -> p a t m", a=PASSES, t=PACK),
             )
@@ -115,20 +115,14 @@ def tile_list_register_file_step_kernel(
             for d in (0, 2, 1, 3):
                 queue.dma_start(dst[32 * d : 32 * d + 4, :, :].bitcast(I32), src[32 * d : 32 * d + 32 : 4, :].bitcast(I32))
 
-        def order_w1_scales(b, dst):
-            nc.vector.tensor_copy(
-                dst[:, W : 2 * W].rearrange("p (t m) -> p t m", t=PACK),
-                w1_rows[:, b * W : (b + 1) * W].rearrange("p (m t) -> p t m", t=PACK),
-            )
-
-        order_w1_scales(0, rows)
         first_rows = gather_rows(0)
+        nc.vector.tensor_copy(
+            rows[:, W:].rearrange("p (b t m) -> p b t m", b=2, t=PACK),
+            w1_rows[:].rearrange("p (b m t) -> p b t m", b=2, t=PACK),
+        )
         nc.vector.tensor_copy(rows[:, 0:W].bitcast(I32), first_rows[:].bitcast(I32))
         move_rows(nc.scalar, planes, rows)
-        order_w1_scales(1, late_rows)
         order_w1(0)
-        nc.vector.tensor_copy(late_rows[:, 0:W].bitcast(I32), gather_rows(1)[:].bitcast(I32))
-        move_rows(nc.scalar, late_planes, late_rows)
 
         w2_raw = {}
 
@@ -139,7 +133,7 @@ def tile_list_register_file_step_kernel(
         olds = {}
 
         def load_old(h, both):
-            olds[h] = both[:, (2 + h) * PACK * N : (3 + h) * PACK * N].rearrange("p (u j) -> p u j", u=TILES)
+            olds[h] = both[:, h * PACK * N : (h + 1) * PACK * N].rearrange("p (u j) -> p u j", u=TILES)
             nc.sync.dma_start(olds[h], old[:, h * W : (h + 1) * W].rearrange("(u p) j -> p u j", p=P))
 
 
@@ -161,11 +155,11 @@ def tile_list_register_file_step_kernel(
             bank = psum.tile([P, PACK * P], F32, name="bank", tag="bank")
             for t in range(PACK):
                 for a in range(PASSES):
-                    c = W + t * P
+                    c = W + b * W + t * P
                     nc.tensor.matmul_mx(
                         bank[:, t * P : (t + 1) * P],
                         lhsT=w1[b][:, 2 * (a * W + t * P) : 2 * (a * W + (t + 1) * P)].bitcast(FP4X4),
-                        lhsT_scale=(planes, late_planes)[b][:, a, c : c + P],
+                        lhsT_scale=planes[:, a, c : c + P],
                         start=(a == 0),
                         stop=(a == PASSES - 1),
                         **table_operand(a, h, q * P, (q + 1) * P),
@@ -214,7 +208,7 @@ def tile_list_register_file_step_kernel(
                 nc.tensor.matmul_mx(
                     bank[:],
                     lhsT=w3[:, b, u * P : (u + 1) * P].bitcast(FP8X4),
-                    lhsT_scale=late_planes[:, b, 2 * W + u * P : 2 * W + (u + 1) * P],
+                    lhsT_scale=late_planes[:, b, W + u * P : W + (u + 1) * P],
                     rhs=codes.bitcast(FP8X4),
                     rhs_scale=scales,
                     start=(b == 0),
@@ -281,7 +275,7 @@ def tile_list_register_file_step_kernel(
             )
         gain_copy = shared.tile([P, PASSES, PACK], F32, name="gain_copy", offset=0, align_bytes=64)
         nc.scalar.copy(gain_copy[:], gains[:, 0:PASSES, :])
-        w2_both = shared.tile([P, (PASSES + HALVES) * PACK * N], F32, name="w2_both", offset=W, align_bytes=64)
+        w2_both = tile([P, PASSES * PACK * N], F32, "w2_both", "w1_raw0")
         load_w2(0, w2_both[:, 0 : PACK * N])
         load_w2(1, w2_both[:, PACK * N : 2 * PACK * N])
         gather(0, 1)
@@ -290,11 +284,14 @@ def tile_list_register_file_step_kernel(
         for q in range(PACK):
             feature_bank(0, 0, q)
         order_w1(1)
+        nc.vector.tensor_copy(late_rows[:, 0:W].bitcast(I32), gather_rows(1, "w1_raw1")[:].bitcast(I32))
+        move_rows(nc.sync, late_planes, late_rows)
         gather(1, 1)
-        w3 = tile([P, PASSES, N], U32, "w3", "table0")
+        w3 = tile([P, PASSES, N], U32, "w3", "late_rows")
         nc.sync.dma_start(w3[:].bitcast(I32), w3_words.rearrange("b p c i -> p b (c i)").bitcast(I32))
-        load_old(0, w2_both)
-        load_old(1, w2_both)
+        old_both = tile([P, HALVES * TILES * W], F32, "old_both", "w1_raw1")
+        load_old(0, old_both)
+        load_old(1, old_both)
 
         h_room = tile([P, (PACK + 3 * (PACK - 1)) * W], BF16, "h_room", "table1")
 

@@ -25,6 +25,7 @@ HALVES = S // W
 TILES = N // P
 EARLY_ROW = W + H
 LATE_ROW = W + N
+HOLD = 2048
 
 
 def tile_list_register_file_step_kernel(
@@ -51,6 +52,7 @@ def tile_list_register_file_step_kernel(
             nc.sync.dma_start(w1_raw[b][:, a0:a1, :].bitcast(I32), src[:, a0:a1, :])
 
         load_w1(0, 0, 1)
+        load_w1(0, 1, 2)
 
         tab_rows = tile([P, T], U8, "tab_rows")
         w1_rows = tile([P, H], U8, "w1_rows")
@@ -84,7 +86,6 @@ def tile_list_register_file_step_kernel(
             nc.sync.dma_start(words[:].bitcast(I32), tab_words[a].rearrange("p t i -> p (t i)").bitcast(I32))
             table.append(words)
             if a == 0:
-                load_w1(0, 1, 2)
                 nc.sync.dma_start(gain_rows[0:PASSES, :], gain.rearrange("(b k) -> b k", b=PASSES))
 
 
@@ -116,13 +117,13 @@ def tile_list_register_file_step_kernel(
                 queue.dma_start(dst[32 * d : 32 * d + 4, :, :].bitcast(I32), src[32 * d : 32 * d + 32 : 4, :].bitcast(I32))
 
         first_rows = gather_rows(0)
+        nc.vector.tensor_copy(rows[:, 0:W].bitcast(I32), first_rows[:].bitcast(I32))
         nc.vector.tensor_copy(
             rows[:, W:].rearrange("p (b t m) -> p b t m", b=2, t=PACK),
             w1_rows[:].rearrange("p (b m t) -> p b t m", b=2, t=PACK),
         )
-        nc.vector.tensor_copy(rows[:, 0:W].bitcast(I32), first_rows[:].bitcast(I32))
         move_rows(nc.scalar, planes, rows)
-        order_w1(0)
+        order_w1(0, "w1_rows")
 
         w2_raw = {}
 
@@ -151,7 +152,10 @@ def tile_list_register_file_step_kernel(
         silus = {}
 
         def feature_bank(h, b, q):
-            silus[h, b, q] = tile([P, W], F32, "silu%d%d%d" % (h, b, q))
+            if (h, b, q) == (1, 0, 0):
+                silus[h, b, q] = shared.tile([P, W], F32, name="silu100", offset=HOLD, align_bytes=64)
+            else:
+                silus[h, b, q] = tile([P, W], F32, "silu%d%d%d" % (h, b, q))
             bank = psum.tile([P, PACK * P], F32, name="bank", tag="bank")
             for t in range(PACK):
                 for a in range(PASSES):
@@ -179,9 +183,12 @@ def tile_list_register_file_step_kernel(
                 ALU.mult,
             )
 
-        def quantize(x, passes, name, tag=None):
-            codes = tile([P, passes * W], U32, name + "_codes", tag)
-            scales = tile([P, passes * W], U8, name + "_scales")
+        def quantize(x, passes, name, held=None):
+            codes = tile([P, passes * W], U32, name + "_codes")
+            if held is None:
+                scales = tile([P, passes * W], U8, name + "_scales")
+            else:
+                scales = shared.tile([P, passes * W], U8, name=name + "_scales", offset=HOLD + held * W, align_bytes=64)
             nc.vector.quantize_mx(out=codes[:].bitcast(FP8X4), scales=scales[:], in_=x)
             return [(codes[:, a * W : (a + 1) * W], scales[:, a * W : (a + 1) * W]) for a in range(passes)]
 
@@ -266,7 +273,7 @@ def tile_list_register_file_step_kernel(
         for i in range(3):
             nc.tensor.matmul_mx(
                 warm_bank[:],
-                lhsT=w1[0][:, 0 : 2 * P].bitcast(FP4X4),
+                lhsT=w1_raw[0][:, 0, 0 : 2 * P].bitcast(FP4X4),
                 lhsT_scale=first_rows[:, 0:P],
                 rhs=picked[0, 0][:].bitcast(FP8X4),
                 rhs_scale=first_rows[:],
@@ -275,10 +282,10 @@ def tile_list_register_file_step_kernel(
             )
         gain_copy = shared.tile([P, PASSES, PACK], F32, name="gain_copy", offset=0, align_bytes=64)
         nc.scalar.copy(gain_copy[:], gains[:, 0:PASSES, :])
-        w2_both = tile([P, PASSES * PACK * N], F32, "w2_both", "w1_raw0")
+        gather(0, 1)
+        w2_both = tile([P, PASSES * PACK * N], F32, "w2_both", "table0")
         load_w2(0, w2_both[:, 0 : PACK * N])
         load_w2(1, w2_both[:, PACK * N : 2 * PACK * N])
-        gather(0, 1)
         gather(1, 0, 0, W // 2)
         gather(1, 0, W // 2, W)
         for q in range(PACK):
@@ -293,40 +300,35 @@ def tile_list_register_file_step_kernel(
         load_old(0, old_both)
         load_old(1, old_both)
 
-        h_room = tile([P, (PACK + 3 * (PACK - 1)) * W], BF16, "h_room", "table1")
+        h_room = tile([P, 14 * W], BF16, "h_room", "table1")
 
         def h_bf(h, b):
-            c = (PASSES * h + b) * (PACK - 1) * W
+            c = (3, 0, 7, 10)[PASSES * h + b] * W
             return h_room[:, c : c + PACK * W]
 
         def gains_of(h, b, on_pool, q0=0, q1=PACK):
             for q in range(q0, q1):
                 apply_gain(nc.gpsimd if q in on_pool else nc.vector, h_bf(h, b), h, b, q)
 
-        def quantize_h(h, b):
-            h_q[h, b] = quantize(h_bf(h, b), 1, "h%d%d" % (h, b))[0]
+        def quantize_h(h, b, held=None):
+            h_q[h, b] = quantize(h_bf(h, b), 1, "h%d%d" % (h, b), held)[0]
 
         gains_of(0, 0, (0,))
-        quantize_h(0, 0)
-        round_w2(nc.scalar.copy, 0, 0, P, "silu000")
-        feature_bank(0, 1, 0)
-        feature_bank(0, 1, 1)
-        round_w2(nc.scalar.copy, 0, P, 2 * P)
-        feature_bank(0, 1, 2)
-        feature_bank(0, 1, 3)
-        round_w2(nc.scalar.copy, 0, 2 * P, 3 * P)
-        gains_of(0, 1, (0,), 0, 3)
+        round_w2(nc.scalar.copy, 0, 0, P, "silu001")
+        for q in range(PACK):
+            feature_bank(0, 1, q)
+            if q > 0:
+                round_w2(nc.scalar.copy, 0, q * P, (q + 1) * P)
+        gains_of(0, 1, (0,), 0, 2)
         round_w2(nc.vector.tensor_copy, 1, 0, N, "silu010")
-        gains_of(0, 1, (0,), 3, 4)
-        w2_q[1] = quantize(w2_bf[1][:], 1, "w21")[0]
-        quantize_h(0, 1)
-        feature_bank(1, 0, 0)
-        round_w2(nc.scalar.copy, 0, 3 * P, 4 * P)
-        feature_bank(1, 0, 1)
-        feature_bank(1, 0, 2)
-        feature_bank(1, 0, 3)
+        quantize_h(0, 0)
+        for q in range(PACK):
+            feature_bank(1, 0, q)
+        gains_of(0, 1, (3,), 2, 4)
         gains_of(1, 0, (0,))
-        w2_q[0] = quantize(w2_bf[0][:], 1, "w20", "silu100")[0]
+        quantize_h(0, 1, 0)
+        w2_q[0] = quantize(w2_bf[0][:], 1, "w20", 1)[0]
+        w2_q[1] = quantize(w2_bf[1][:], 1, "w21", 2)[0]
         quantize_h(1, 0)
         for q in range(PACK):
             feature_bank(1, 1, q)

@@ -23,8 +23,7 @@ PASSES = 2
 W = 512
 HALVES = S // W
 TILES = N // P
-EARLY_ROW = W + H
-LATE_ROW = W + N
+EARLY_ROW = W + H + N
 HOLD = 2048
 
 
@@ -56,8 +55,7 @@ def tile_list_register_file_step_kernel(
 
         tab_rows = tile([P, T], U8, "tab_rows")
         w1_rows = tile([P, H], U8, "w1_rows")
-        late_rows = tile([P, LATE_ROW], U8, "late_rows")
-        late_planes = tile([P, PASSES, LATE_ROW], U8, "late_planes")
+        late_planes = tile([P, PASSES, W], U8, "late_planes")
         rows = shared.tile([P, EARLY_ROW], U8, name="rows", offset=0, align_bytes=64)
         planes = tile([P, PASSES, EARLY_ROW], U8, "planes")
         warm = tile([P, 2], F32, "warm")
@@ -76,7 +74,7 @@ def tile_list_register_file_step_kernel(
 
         load_rows(nc.sync, tab_rows[0:P:4, :], tab_scales)
         load_rows(nc.sync, w1_rows[0:P:4, :], w1_scales)
-        load_rows(nc.scalar, late_rows[0:P:4, W:], w3_scales)
+        load_rows(nc.scalar, rows[0:P:4, W + H :], w3_scales)
 
         nc.scalar.activation(warm[:, 1:2], warm[:, 0:1], ACT.Silu)
 
@@ -97,9 +95,9 @@ def tile_list_register_file_step_kernel(
 
         w1 = {}
 
-        def order_w1(b, tag=None):
+        def order_w1(engine, b, tag=None):
             w1[b] = tile([P, PASSES * 2 * W], U8, "w1_%d" % b, tag)
-            nc.gpsimd.tensor_copy(
+            engine.tensor_copy(
                 w1[b][:].bitcast(U16).rearrange("p (a t m) -> p a t m", a=PASSES, t=PACK),
                 w1_raw[b][:].rearrange("p a c -> p (a c)").bitcast(U16).rearrange("p (a m t) -> p a t m", a=PASSES, t=PACK),
             )
@@ -119,11 +117,11 @@ def tile_list_register_file_step_kernel(
         first_rows = gather_rows(0)
         nc.vector.tensor_copy(rows[:, 0:W].bitcast(I32), first_rows[:].bitcast(I32))
         nc.vector.tensor_copy(
-            rows[:, W:].rearrange("p (b t m) -> p b t m", b=2, t=PACK),
+            rows[:, W : W + H].rearrange("p (b t m) -> p b t m", b=2, t=PACK),
             w1_rows[:].rearrange("p (b m t) -> p b t m", b=2, t=PACK),
         )
         move_rows(nc.scalar, planes, rows)
-        order_w1(0, "w1_rows")
+        order_w1(nc.gpsimd, 0, "w1_rows")
 
         w2_raw = {}
 
@@ -152,8 +150,10 @@ def tile_list_register_file_step_kernel(
         silus = {}
 
         def feature_bank(h, b, q):
-            if (h, b, q) == (1, 0, 0):
-                silus[h, b, q] = shared.tile([P, W], F32, name="silu100", offset=HOLD, align_bytes=64)
+            if (h, b, q) == (0, 1, 0):
+                silus[h, b, q] = shared.tile([P, W], F32, name="silu010", offset=HOLD, align_bytes=64)
+            elif (h, b, q) == (1, 0, 1):
+                silus[h, b, q] = w2_both[:, PACK * N : PACK * N + W]
             else:
                 silus[h, b, q] = tile([P, W], F32, "silu%d%d%d" % (h, b, q))
             bank = psum.tile([P, PACK * P], F32, name="bank", tag="bank")
@@ -183,24 +183,26 @@ def tile_list_register_file_step_kernel(
                 ALU.mult,
             )
 
-        def quantize(x, passes, name, held=None):
-            codes = tile([P, passes * W], U32, name + "_codes")
+        def quantize(x, width, name, held=None):
+            codes = tile([P, width], U32, name + "_codes")
             if held is None:
-                scales = tile([P, passes * W], U8, name + "_scales")
+                scales = tile([P, width], U8, name + "_scales")
             else:
-                scales = shared.tile([P, passes * W], U8, name=name + "_scales", offset=HOLD + held * W, align_bytes=64)
+                scales = shared.tile([P, width], U8, name=name + "_scales", offset=HOLD + held * W, align_bytes=64)
             nc.vector.quantize_mx(out=codes[:].bitcast(FP8X4), scales=scales[:], in_=x)
-            return [(codes[:, a * W : (a + 1) * W], scales[:, a * W : (a + 1) * W]) for a in range(passes)]
+            return codes[:], scales[:]
 
-        w2_bf = {}
 
-        def round_w2(copy, a, c0, c1, tag=None):
-            if c0 == 0:
-                w2_bf[a] = tile([P, PACK * N], BF16, "w2_bf%d" % a, tag)
+        def round_w2(copy, a, c0, c1, room, r0=0):
             copy(
-                w2_bf[a][:, c0 * PACK : c1 * PACK].rearrange("p (c i t) -> p c t i", t=PACK, i=4),
+                room[:, (c0 - r0) * PACK : (c1 - r0) * PACK].rearrange("p (c i t) -> p c t i", t=PACK, i=4),
                 w2_raw[a][:, :, c0:c1].rearrange("p t (c i) -> p c t i", i=4),
             )
+
+        def quantize_w2(a, u0, u1, room, held=None):
+            codes, scales = quantize(room[:], (u1 - u0) * P, "w2%d%d" % (a, u0), held)
+            for u in range(u0, u1):
+                w2_q[a, u] = codes[:, (u - u0) * P : (u - u0 + 1) * P], scales[:, (u - u0) * P : (u - u0 + 1) * P]
 
         h_q = {}
         w2_q = {}
@@ -215,7 +217,7 @@ def tile_list_register_file_step_kernel(
                 nc.tensor.matmul_mx(
                     bank[:],
                     lhsT=w3[:, b, u * P : (u + 1) * P].bitcast(FP8X4),
-                    lhsT_scale=late_planes[:, b, W + u * P : W + (u + 1) * P],
+                    lhsT_scale=planes[:, b, W + H + u * P : W + H + (u + 1) * P],
                     rhs=codes.bitcast(FP8X4),
                     rhs_scale=scales,
                     start=(b == 0),
@@ -229,11 +231,11 @@ def tile_list_register_file_step_kernel(
         def gate(h, u):
             bank = psum.tile([P, W], F32, name="bank", tag="bank")
             for a in range(PASSES):
-                codes, scales = w2_q[a]
+                codes, scales = w2_q[a, u]
                 nc.tensor.matmul_mx(
                     bank[:],
-                    lhsT=codes[:, u * P : (u + 1) * P].bitcast(FP8X4),
-                    lhsT_scale=scales[:, u * P : (u + 1) * P],
+                    lhsT=codes.bitcast(FP8X4),
+                    lhsT_scale=scales,
                     start=(a == 0),
                     stop=(a == PASSES - 1),
                     **table_operand(a, h, 0, W),
@@ -290,20 +292,19 @@ def tile_list_register_file_step_kernel(
         gather(1, 0, W // 2, W)
         for q in range(PACK):
             feature_bank(0, 0, q)
-        order_w1(1)
-        nc.vector.tensor_copy(late_rows[:, 0:W].bitcast(I32), gather_rows(1, "w1_raw1")[:].bitcast(I32))
-        move_rows(nc.sync, late_planes, late_rows)
+        order_w1(nc.vector, 1, "picked_rows0")
+        move_rows(nc.sync, late_planes, gather_rows(1, "w1_raw0"))
         gather(1, 1)
-        w3 = tile([P, PASSES, N], U32, "w3", "late_rows")
+        w3 = tile([P, PASSES, N], U32, "w3", "w1_raw0")
         nc.sync.dma_start(w3[:].bitcast(I32), w3_words.rearrange("b p c i -> p b (c i)").bitcast(I32))
-        old_both = tile([P, HALVES * TILES * W], F32, "old_both", "w1_raw1")
+        old_both = tile([P, HALVES * TILES * W], F32, "old_both", "tab_rows")
         load_old(0, old_both)
         load_old(1, old_both)
 
-        h_room = tile([P, 14 * W], BF16, "h_room", "table1")
+        h_room = tile([P, 14 * W], BF16, "h_room", "w1_raw1")
 
         def h_bf(h, b):
-            c = (3, 0, 7, 10)[PASSES * h + b] * W
+            c = (0, 4, 7, 10)[PASSES * h + b] * W
             return h_room[:, c : c + PACK * W]
 
         def gains_of(h, b, on_pool, q0=0, q1=PACK):
@@ -311,30 +312,34 @@ def tile_list_register_file_step_kernel(
                 apply_gain(nc.gpsimd if q in on_pool else nc.vector, h_bf(h, b), h, b, q)
 
         def quantize_h(h, b, held=None):
-            h_q[h, b] = quantize(h_bf(h, b), 1, "h%d%d" % (h, b), held)[0]
+            h_q[h, b] = quantize(h_bf(h, b), W, "h%d%d" % (h, b), held)
 
-        gains_of(0, 0, (0,))
-        round_w2(nc.scalar.copy, 0, 0, P, "silu001")
+        gains_of(0, 0, (0, 1))
+        first_bf = tile([P, PACK * N], BF16, "first_bf", "silu000")
+        round_w2(nc.scalar.copy, 0, 0, P, first_bf)
         for q in range(PACK):
             feature_bank(0, 1, q)
             if q > 0:
-                round_w2(nc.scalar.copy, 0, q * P, (q + 1) * P)
+                round_w2(nc.scalar.copy, 0, q * P, (q + 1) * P, first_bf)
         gains_of(0, 1, (0,), 0, 2)
-        round_w2(nc.vector.tensor_copy, 1, 0, N, "silu010")
-        quantize_h(0, 0)
-        for q in range(PACK):
-            feature_bank(1, 0, q)
-        gains_of(0, 1, (3,), 2, 4)
-        gains_of(1, 0, (0,))
-        quantize_h(0, 1, 0)
-        w2_q[0] = quantize(w2_bf[0][:], 1, "w20", 1)[0]
-        w2_q[1] = quantize(w2_bf[1][:], 1, "w21", 2)[0]
-        quantize_h(1, 0)
-        for q in range(PACK):
-            feature_bank(1, 1, q)
-        gains_of(1, 1, (0,))
-        quantize_h(1, 1)
-        behind = tile([P, 2 * TILES * W], F32, "behind", "table1")
+        high_bf = shared.tile([P, PACK * N // 2], BF16, name="high_bf", offset=HOLD + W, align_bytes=64)
+        round_w2(nc.vector.tensor_copy, 1, N // 2, N, high_bf, N // 2)
+        quantize_w2(1, 2, 4, high_bf)
+        quantize_h(0, 0, 0)
+        low_bf = tile([P, PACK * N // 2], BF16, "low_bf", "silu011")
+        round_w2(nc.scalar.copy, 1, 0, P, low_bf)
+        round_w2(nc.scalar.copy, 1, P, 2 * P, low_bf)
+        gains_of(0, 1, (), 2, 4)
+        quantize_w2(0, 0, 4, first_bf)
+        quantize_w2(1, 0, 2, low_bf)
+        quantize_h(0, 1)
+        for b in range(PASSES):
+            for q in range(PACK):
+                feature_bank(1, b, q)
+        for b in range(PASSES):
+            gains_of(1, b, (0,))
+            quantize_h(1, b)
+        behind = tile([P, 2 * TILES * W], F32, "behind", "w1_raw1")
         step_tiles = [behind[:, 0 : TILES * W], tile([P, TILES * W], F32, "steps1")[:]]
 
         def diff_room(h, u):

@@ -253,7 +253,7 @@ def tile_list_register_file_step_kernel(
         def step(h, u):
             m = step_tiles[h][:, u * W : (u + 1) * W]
             if (h, u) == on_gpsimd[0]:
-                m = tile([P, W], F32, "step02", "tanh01")[:]
+                m = tile([P, W], F32, "step03", "tanh02")[:]
             if (h, u) in on_gpsimd:
                 nc.gpsimd.tensor_tensor(m, tanhs[h, u][:], diffs[h, u], ALU.mult)
             else:
@@ -268,7 +268,7 @@ def tile_list_register_file_step_kernel(
             nc.sync.dma_start(out[u * P : (u + 1) * P, h * W + c0 : h * W + c1], r)
 
         units = [(h, u) for h in range(HALVES) for u in range(TILES)]
-        on_gpsimd = units[2:]
+        on_gpsimd = units[3:]
 
         gather(0, 0)
         warm_bank = psum.tile([P, W], F32, name="bank", tag="bank")

@@ -24,7 +24,8 @@ W = 512
 HALVES = S // W
 TILES = N // P
 EARLY_ROW = W + H + N
-HOLD = 2048
+HOLD = 4096
+RAW = HOLD + 16 * W
 
 
 def tile_list_register_file_step_kernel(
@@ -46,7 +47,7 @@ def tile_list_register_file_step_kernel(
 
         def load_w1(b, a0, a1):
             if a0 == 0:
-                w1_raw[b] = tile([P, PASSES, 2 * W], U8, "w1_raw%d" % b)
+                w1_raw[b] = shared.tile([P, PASSES, 2 * W], U8, name="w1_raw%d" % b, offset=RAW + (1 - b) * 36864, align_bytes=64)
             src = w1_words[:, :, 2 * W * b : 2 * W * (b + 1)].bitcast(I32).rearrange("a p c -> p a c")
             nc.sync.dma_start(w1_raw[b][:, a0:a1, :].bitcast(I32), src[:, a0:a1, :])
 
@@ -96,7 +97,10 @@ def tile_list_register_file_step_kernel(
         w1 = {}
 
         def order_w1(engine, b, tag=None):
-            w1[b] = tile([P, PASSES * 2 * W], U8, "w1_%d" % b, tag)
+            if b == 0:
+                w1[b] = tile([P, PASSES * 2 * W], U8, "w1_%d" % b, tag)
+            else:
+                w1[b] = shared.tile([P, PASSES * 2 * W], U8, name="w1_1", offset=64, align_bytes=64)
             engine.tensor_copy(
                 w1[b][:].bitcast(U16).rearrange("p (a t m) -> p a t m", a=PASSES, t=PACK),
                 w1_raw[b][:].rearrange("p a c -> p (a c)").bitcast(U16).rearrange("p (a m t) -> p a t m", a=PASSES, t=PACK),
@@ -139,7 +143,9 @@ def tile_list_register_file_step_kernel(
         picked = {}
 
         def gather(a, h, c0=0, c1=W, tag=None):
-            if c0 == 0:
+            if (a, h) == (1, 1):
+                picked[a, h] = shared.tile([P, W], U32, name="picked11", offset=RAW - 3 * W, align_bytes=64)
+            elif c0 == 0:
                 picked[a, h] = tile([P, W], U32, "picked%d%d" % (a, h), tag)
             listed = offsets_of(h)[:, c0 // 16 : c1 // 16]
             nc.vector.tensor_copy(picked[a, h][:, c0:c1], table[a][:].indirect(listed))
@@ -292,16 +298,18 @@ def tile_list_register_file_step_kernel(
         gather(1, 0, W // 2, W)
         for q in range(PACK):
             feature_bank(0, 0, q)
-        order_w1(nc.vector, 1, "picked_rows0")
-        move_rows(nc.sync, late_planes, gather_rows(1, "w1_raw0"))
+        order_w1(nc.vector, 1)
+        late_rows = shared.tile([P, W], U8, name="late_rows", offset=RAW + W, align_bytes=64)
+        nc.vector.tensor_copy(late_rows[:], tab_rows[:].indirect(offsets_of(1)))
+        move_rows(nc.sync, late_planes, late_rows)
         gather(1, 1)
-        w3 = tile([P, PASSES, N], U32, "w3", "w1_raw0")
+        w3 = tile([P, PASSES, N], U32, "w3", "table1")
         nc.sync.dma_start(w3[:].bitcast(I32), w3_words.rearrange("b p c i -> p b (c i)").bitcast(I32))
         old_both = tile([P, HALVES * TILES * W], F32, "old_both", "tab_rows")
         load_old(0, old_both)
         load_old(1, old_both)
 
-        h_room = tile([P, 14 * W], BF16, "h_room", "w1_raw1")
+        h_room = shared.tile([P, 14 * W], BF16, name="h_room", offset=RAW + 2 * W, align_bytes=64)
 
         def h_bf(h, b):
             c = (0, 4, 7, 10)[PASSES * h + b] * W
@@ -339,7 +347,7 @@ def tile_list_register_file_step_kernel(
         for b in range(PASSES):
             gains_of(1, b, (0,))
             quantize_h(1, b)
-        behind = tile([P, 2 * TILES * W], F32, "behind", "w1_raw1")
+        behind = shared.tile([P, 2 * TILES * W], F32, name="behind", offset=RAW + 2 * W, align_bytes=64)
         step_tiles = [behind[:, 0 : TILES * W], tile([P, TILES * W], F32, "steps1")[:]]
 
         def diff_room(h, u):

@@ -23,9 +23,11 @@ PASSES = 2
 W = 512
 HALVES = S // W
 TILES = N // P
-EARLY_ROW = W + H + N
+EARLY_ROW = W + H
 HOLD = 4096
-RAW = HOLD + 16 * W
+BOTH = HOLD + 8 * W
+RAW = BOTH + 45 * W
+OLD = RAW + 40 * W
 
 
 def tile_list_register_file_step_kernel(
@@ -47,14 +49,14 @@ def tile_list_register_file_step_kernel(
 
         def load_w1(b, a0, a1):
             if a0 == 0:
-                w1_raw[b] = shared.tile([P, PASSES, 2 * W], U8, name="w1_raw%d" % b, offset=RAW + (1 - b) * 36864, align_bytes=64)
+                w1_raw[b] = shared.tile([P, PASSES, 2 * W], U8, name="w1_raw%d" % b, offset=RAW + (1 - b) * 36 * W, align_bytes=64)
             src = w1_words[:, :, 2 * W * b : 2 * W * (b + 1)].bitcast(I32).rearrange("a p c -> p a c")
             nc.sync.dma_start(w1_raw[b][:, a0:a1, :].bitcast(I32), src[:, a0:a1, :])
 
         load_w1(0, 0, 1)
         load_w1(0, 1, 2)
 
-        tab_rows = tile([P, T], U8, "tab_rows")
+        tab_rows = shared.tile([P, T], U8, name="tab_rows", offset=OLD + 31 * W, align_bytes=64)
         w1_rows = tile([P, H], U8, "w1_rows")
         late_planes = tile([P, PASSES, W], U8, "late_planes")
         rows = shared.tile([P, EARLY_ROW], U8, name="rows", offset=0, align_bytes=64)
@@ -75,20 +77,20 @@ def tile_list_register_file_step_kernel(
 
         load_rows(nc.sync, tab_rows[0:P:4, :], tab_scales)
         load_rows(nc.sync, w1_rows[0:P:4, :], w1_scales)
-        load_rows(nc.scalar, rows[0:P:4, W + H :], w3_scales)
 
         nc.scalar.activation(warm[:, 1:2], warm[:, 0:1], ACT.Silu)
 
         table = []
         for a in range(PASSES):
-            words = tile([P, T], U32, "table%d" % a)
+            if a == 0:
+                words = shared.tile([P, T], U32, name="table0", offset=BOTH + 31 * W, align_bytes=64)
+            else:
+                words = tile([P, T], U32, "table1")
             nc.sync.dma_start(words[:].bitcast(I32), tab_words[a].rearrange("p t i -> p (t i)").bitcast(I32))
             table.append(words)
             if a == 0:
                 nc.sync.dma_start(gain_rows[0:PASSES, :], gain.rearrange("(b k) -> b k", b=PASSES))
 
-
-        load_w1(1, 0, 2)
         gain_bank = psum.tile([P, PACK * P], F32, name="gain_bank", tag="bank")
         for t in range(PACK):
             nc.tensor.transpose(gain_bank[:, t:W:PACK], gain_rows[:, t:W:PACK], identity[:])
@@ -124,7 +126,8 @@ def tile_list_register_file_step_kernel(
             rows[:, W : W + H].rearrange("p (b t m) -> p b t m", b=2, t=PACK),
             w1_rows[:].rearrange("p (b m t) -> p b t m", b=2, t=PACK),
         )
-        move_rows(nc.scalar, planes, rows)
+        move_rows(nc.scalar, planes[:, :, 0 : 2 * W], rows[:, 0 : 2 * W])
+        move_rows(nc.scalar, planes[:, :, 2 * W :], rows[:, 2 * W :])
         order_w1(nc.gpsimd, 0, "w1_rows")
 
         w2_raw = {}
@@ -223,7 +226,7 @@ def tile_list_register_file_step_kernel(
                 nc.tensor.matmul_mx(
                     bank[:],
                     lhsT=w3[:, b, u * P : (u + 1) * P].bitcast(FP8X4),
-                    lhsT_scale=planes[:, b, W + H + u * P : W + H + (u + 1) * P],
+                    lhsT_scale=w3_planes[:, b, u * P : (u + 1) * P],
                     rhs=codes.bitcast(FP8X4),
                     rhs_scale=scales,
                     start=(b == 0),
@@ -288,10 +291,11 @@ def tile_list_register_file_step_kernel(
                 start=(i == 0),
                 stop=(i == 2),
             )
-        gain_copy = shared.tile([P, PASSES, PACK], F32, name="gain_copy", offset=0, align_bytes=64)
+        gain_copy = tile([P, PASSES, PACK], F32, "gain_copy")
         nc.scalar.copy(gain_copy[:], gains[:, 0:PASSES, :])
         gather(0, 1)
-        w2_both = tile([P, PASSES * PACK * N], F32, "w2_both", "table0")
+        load_w1(1, 0, 2)
+        w2_both = shared.tile([P, PASSES * PACK * N], F32, name="w2_both", offset=BOTH, align_bytes=64)
         load_w2(0, w2_both[:, 0 : PACK * N])
         load_w2(1, w2_both[:, PACK * N : 2 * PACK * N])
         gather(1, 0, 0, W // 2)
@@ -305,7 +309,12 @@ def tile_list_register_file_step_kernel(
         gather(1, 1)
         w3 = tile([P, PASSES, N], U32, "w3", "table1")
         nc.sync.dma_start(w3[:].bitcast(I32), w3_words.rearrange("b p c i -> p b (c i)").bitcast(I32))
-        old_both = tile([P, HALVES * TILES * W], F32, "old_both", "tab_rows")
+        w3_planes = shared.tile([P, PASSES, N], U8, name="w3_planes", offset=OLD + 32 * W, align_bytes=64)
+        nc.vector.memset(w3_planes[:].rearrange("p a c -> p (a c)").bitcast(I32), 0)
+        w3_rows = w3_scales.bitcast(I32).rearrange("a q c -> q a c")
+        for d in (0, 2, 1, 3):
+            nc.sync.dma_start(w3_planes[32 * d : 32 * d + 4, :, :].bitcast(I32), w3_rows[4 * d : 4 * d + 4])
+        old_both = shared.tile([P, HALVES * TILES * W], F32, name="old_both", offset=OLD, align_bytes=64)
         load_old(0, old_both)
         load_old(1, old_both)
 

@@ -21,13 +21,9 @@ P = 128
 PACK = 4
 PASSES = 2
 W = 512
-HALVES = S // W
-TILES = N // P
-EARLY_ROW = W + H
-HOLD = 4096
-BOTH = HOLD + 8 * W
-RAW = BOTH + 45 * W
-OLD = RAW + 40 * W
+KIB = 1024
+BANKS = 8
+QUADS = (0, 2, 1, 3)
 
 
 def tile_list_register_file_step_kernel(
@@ -36,341 +32,366 @@ def tile_list_register_file_step_kernel(
     nc = tc.nc
     with ExitStack() as ctx:
         keep = ctx.enter_context(tc.tile_pool(name="keep", bufs=1))
-        shared = ctx.enter_context(tc.tile_pool(name="shared", bufs=1))
-        psum = ctx.enter_context(tc.psum_pool(name="psum", bufs=8))
+        placed = ctx.enter_context(tc.tile_pool(name="placed", bufs=1))
+        psum = ctx.enter_context(tc.psum_pool(name="psum", bufs=1))
 
-        def tile(shape, dtype, name, tag=None):
-            return keep.tile(shape, dtype, name=name, tag=tag or name, align_bytes=64)
+        def tile(shape, dtype, name):
+            return keep.tile(shape, dtype, name=name, align_bytes=64)
+
+        def place(shape, dtype, name, offset):
+            return placed.tile(shape, dtype, name=name, offset=offset, align_bytes=64)
+
+        banks = [psum.tile([P, W], F32, name="bank%d" % i) for i in range(BANKS)]
+        arena = tile([P, 82 * KIB // 4], F32, "arena")
+        rooms = {}
+
+        def f32_at(kib, columns=W):
+            room, c = (rooms["h"], (kib + 2) * KIB // 4) if kib < 12 else (arena, (kib - 12) * KIB // 4)
+            return room[:, c : c + columns]
+
+        def bf16_at(kib, columns):
+            return f32_at(kib, columns // 2).bitcast(BF16)
 
         offsets = keep.tile([P, S // 16], U16, name="offsets")
         nc.sync.dma_start(offsets[:], offs)
 
-        w1_raw = {}
+        w1_raw = [tile([P, PASSES, 2 * W], U8, "w1_raw0"), place([P, PASSES, 2 * W], U8, "w1_raw1", 39 * KIB)]
 
-        def load_w1(b, a0, a1):
-            if a0 == 0:
-                w1_raw[b] = shared.tile([P, PASSES, 2 * W], U8, name="w1_raw%d" % b, offset=RAW + (1 - b) * 36 * W, align_bytes=64)
+        def load_w1(b):
             src = w1_words[:, :, 2 * W * b : 2 * W * (b + 1)].bitcast(I32).rearrange("a p c -> p a c")
-            nc.sync.dma_start(w1_raw[b][:, a0:a1, :].bitcast(I32), src[:, a0:a1, :])
+            nc.sync.dma_start(w1_raw[b][:].bitcast(I32), src)
 
-        load_w1(0, 0, 1)
-        load_w1(0, 1, 2)
-
-        tab_rows = shared.tile([P, T], U8, name="tab_rows", offset=OLD + 31 * W, align_bytes=64)
+        tab_rows = tile([P, T], U8, "tab_rows")
         w1_rows = tile([P, H], U8, "w1_rows")
+        rows = tile([P, 3 * W], U8, "rows")
+        planes = tile([P, PASSES, 3 * W], U8, "planes")
         late_planes = tile([P, PASSES, W], U8, "late_planes")
-        rows = shared.tile([P, EARLY_ROW], U8, name="rows", offset=0, align_bytes=64)
-        planes = tile([P, PASSES, EARLY_ROW], U8, "planes")
         warm = tile([P, 2], F32, "warm")
-        nc.gpsimd.memset(tab_rows[:].bitcast(I32), 0)
+        gain_rows = place([P, W], F32, "gain_rows", 4 * KIB - 512)
+        identity = tile([P, P], F32, "identity")
+        nc.vector.memset(tab_rows[:].bitcast(I32), 0)
         nc.vector.memset(w1_rows[:].bitcast(I32), 0)
+        nc.vector.memset(warm[:, 0:1], 0.0)
+        nc.vector.memset(gain_rows[:], 0.0)
         nc.vector.memset(planes[:].rearrange("p a c -> p (a c)").bitcast(I32), 0)
         nc.vector.memset(late_planes[:].rearrange("p a c -> p (a c)").bitcast(I32), 0)
-        nc.vector.memset(warm[:, 0:1], 0.0)
-        gain_rows = tile([P, W], F32, "gain_rows")
-        identity = tile([P, P], F32, "identity")
-        nc.gpsimd.memset(gain_rows[:], 0.0)
         make_identity(nc, identity[:])
 
-        def load_rows(queue, dst, scales):
-            queue.dma_start(dst.bitcast(I32), scales.bitcast(I32).rearrange("a q c -> q a c"))
+        def load_rows(dst, scales):
+            nc.sync.dma_start(dst.bitcast(I32), scales.bitcast(I32).rearrange("a q c -> q a c"))
 
-        load_rows(nc.sync, tab_rows[0:P:4, :], tab_scales)
-        load_rows(nc.sync, w1_rows[0:P:4, :], w1_scales)
-
+        load_rows(tab_rows[0:P:4, :], tab_scales)
+        load_rows(w1_rows[0:P:4, :], w1_scales)
+        load_w1(0)
         nc.scalar.activation(warm[:, 1:2], warm[:, 0:1], ACT.Silu)
 
-        table = []
-        for a in range(PASSES):
-            if a == 0:
-                words = shared.tile([P, T], U32, name="table0", offset=BOTH + 31 * W, align_bytes=64)
-            else:
-                words = tile([P, T], U32, "table1")
-            nc.sync.dma_start(words[:].bitcast(I32), tab_words[a].rearrange("p t i -> p (t i)").bitcast(I32))
-            table.append(words)
-            if a == 0:
-                nc.sync.dma_start(gain_rows[0:PASSES, :], gain.rearrange("(b k) -> b k", b=PASSES))
+        table = [place([P, T], U32, "table%d" % a, (46 + 8 * a) * KIB) for a in range(PASSES)]
 
-        gain_bank = psum.tile([P, PACK * P], F32, name="gain_bank", tag="bank")
+        def load_table(a):
+            nc.sync.dma_start(table[a][:].bitcast(I32), tab_words[a].rearrange("p t i -> p (t i)").bitcast(I32))
+
+        load_table(0)
+        nc.sync.dma_start(gain_rows[0:2, :], gain.rearrange("(b k) -> b k", b=2))
+        load_table(1)
+        load_w1(1)
+
         for t in range(PACK):
-            nc.tensor.transpose(gain_bank[:, t:W:PACK], gain_rows[:, t:W:PACK], identity[:])
-        gains = gain_bank[:].rearrange("p (b t) -> p b t", t=PACK)
+            nc.tensor.transpose(banks[0][:, t:W:PACK], gain_rows[:, t:W:PACK], identity[:])
+        gains = banks[0][:].rearrange("p (b t) -> p b t", t=PACK)
 
-        w1 = {}
+        w1 = [tile([P, PASSES * 2 * W], U8, "w1_%d" % b) for b in range(2)]
 
-        def order_w1(engine, b, tag=None):
-            if b == 0:
-                w1[b] = tile([P, PASSES * 2 * W], U8, "w1_%d" % b, tag)
-            else:
-                w1[b] = shared.tile([P, PASSES * 2 * W], U8, name="w1_1", offset=64, align_bytes=64)
-            engine.tensor_copy(
+        def order_w1(b):
+            nc.scalar.copy(
                 w1[b][:].bitcast(U16).rearrange("p (a t m) -> p a t m", a=PASSES, t=PACK),
                 w1_raw[b][:].rearrange("p a c -> p (a c)").bitcast(U16).rearrange("p (a m t) -> p a t m", a=PASSES, t=PACK),
             )
 
-        def offsets_of(h):
-            return offsets[:, h * (W // 16) : (h + 1) * (W // 16)]
+        def offsets_of(h, c0=0, c1=W):
+            return offsets[:, (h * W + c0) // 16 : (h * W + c1) // 16]
 
-        def gather_rows(h, tag=None):
-            picked_rows = tile([P, W], U8, "picked_rows%d" % h, tag)
-            nc.vector.tensor_copy(picked_rows[:], tab_rows[:].indirect(offsets_of(h)))
-            return picked_rows
+        picked_rows = [tile([P, W], U8, "picked_rows0"), place([P, W], U8, "picked_rows1", 4 * KIB)]
+
+        def gather_rows(h):
+            nc.vector.tensor_copy(picked_rows[h][:], tab_rows[:].indirect(offsets_of(h)))
 
         def move_rows(queue, dst, src):
-            for d in (0, 2, 1, 3):
+            for d in QUADS:
                 queue.dma_start(dst[32 * d : 32 * d + 4, :, :].bitcast(I32), src[32 * d : 32 * d + 32 : 4, :].bitcast(I32))
 
-        first_rows = gather_rows(0)
-        nc.vector.tensor_copy(rows[:, 0:W].bitcast(I32), first_rows[:].bitcast(I32))
+        order_w1(0)
+        gather_rows(0)
         nc.vector.tensor_copy(
-            rows[:, W : W + H].rearrange("p (b t m) -> p b t m", b=2, t=PACK),
+            rows[:, W:].rearrange("p (b t m) -> p b t m", b=2, t=PACK),
             w1_rows[:].rearrange("p (b m t) -> p b t m", b=2, t=PACK),
         )
-        move_rows(nc.scalar, planes[:, :, 0 : 2 * W], rows[:, 0 : 2 * W])
-        move_rows(nc.scalar, planes[:, :, 2 * W :], rows[:, 2 * W :])
-        order_w1(nc.gpsimd, 0, "w1_rows")
+        nc.vector.tensor_copy(rows[:, 0:W].bitcast(I32), picked_rows[0][:].bitcast(I32))
+        move_rows(nc.scalar, planes, rows)
+        order_w1(1)
+        gather_rows(1)
 
-        w2_raw = {}
+        def load_w2(raw, a, half):
+            src = w2[a * W : (a + 1) * W, half * (N // 2) : (half + 1) * (N // 2)]
+            nc.sync.dma_start(raw[:, a], src.rearrange("(p t) n -> p t n", t=PACK))
 
-        def load_w2(a, room):
-            w2_raw[a] = room.rearrange("p (t n) -> p t n", t=PACK)
-            nc.sync.dma_start(w2_raw[a], w2[a * W : (a + 1) * W, :].rearrange("(p t) n -> p t n", t=PACK))
+        move_rows(nc.sync, late_planes, picked_rows[1])
+        floats = place([P, 8 * KIB], F32, "floats", 4 * KIB + 512)
+        first_raw = floats[:, 6 * KIB :].rearrange("p (a t n) -> p a t n", a=PASSES, t=PACK)
+        for a in range(PASSES):
+            load_w2(first_raw, a, 0)
 
-        olds = {}
+        w3 = place([P, PASSES, N], U32, "w3", 0)
+        nc.sync.dma_start(w3[:].bitcast(I32), w3_words.rearrange("b p c i -> p b (c i)").bitcast(I32))
+        second_raw = floats[:, 0 : 2 * KIB].rearrange("p (a t n) -> p a t n", a=PASSES, t=PACK)
+        olds = floats[:, 2 * KIB : 6 * KIB].rearrange("p (h u j) -> p h u j", h=2, u=4)
 
-        def load_old(h, both):
-            olds[h] = both[:, h * PACK * N : (h + 1) * PACK * N].rearrange("p (u j) -> p u j", u=TILES)
-            nc.sync.dma_start(olds[h], old[:, h * W : (h + 1) * W].rearrange("(u p) j -> p u j", p=P))
+        def load_old(h, u0):
+            src = old[u0 * P : (u0 + 2) * P, h * W : (h + 1) * W].rearrange("(u p) j -> p u j", p=P)
+            nc.sync.dma_start(olds[:, h, u0 : u0 + 2, :], src)
 
+        load_old(0, 0)
+        w3_planes = rows[:, 0 : 2 * W].rearrange("p (a c) -> p a c", a=PASSES)
+        w3_rows = w3_scales.bitcast(I32).rearrange("a q c -> q a c")
+        for d in QUADS:
+            nc.sync.dma_start(w3_planes[32 * d : 32 * d + 4].bitcast(I32), w3_rows[4 * d : 4 * d + 4])
+        for a in range(PASSES):
+            load_w2(second_raw, a, 1)
+        load_old(0, 2)
+        load_old(1, 0)
+        load_old(1, 2)
 
-        picked = {}
+        picked = {(a, h): tile([P, W], U32, "picked%d%d" % (a, h)) for a, h in ((0, 0), (1, 0), (1, 1))}
+        picked[0, 1] = place([P, W], U32, "picked01", 39 * KIB)
 
-        def gather(a, h, c0=0, c1=W, tag=None):
-            if (a, h) == (1, 1):
-                picked[a, h] = shared.tile([P, W], U32, name="picked11", offset=RAW - 3 * W, align_bytes=64)
-            elif c0 == 0:
-                picked[a, h] = tile([P, W], U32, "picked%d%d" % (a, h), tag)
-            listed = offsets_of(h)[:, c0 // 16 : c1 // 16]
-            nc.vector.tensor_copy(picked[a, h][:, c0:c1], table[a][:].indirect(listed))
+        def gather(a, h, c0=0, c1=W):
+            nc.vector.tensor_copy(picked[a, h][:, c0:c1], table[a][:].indirect(offsets_of(h, c0, c1)))
 
         def table_operand(a, h, c0, c1):
             return {"rhs": picked[a, h][:, c0:c1].bitcast(FP8X4), "rhs_scale": (planes, late_planes)[h][:, a, c0:c1]}
 
-        silus = {}
+        gather(0, 0)
+        gain_copy = tile([P, 2, PACK], F32, "gain_copy")
+        nc.scalar.copy(gain_copy[:], gains[:, 0:2, :])
+        for i in range(6):
+            nc.tensor.matmul_mx(
+                banks[0][:, W // 2 :],
+                lhsT=w1_raw[0][:, 0, 0 : 2 * P].bitcast(FP4X4),
+                lhsT_scale=picked_rows[0][:, 0:P],
+                rhs=picked[0, 0][:, 0 : W // 2].bitcast(FP8X4),
+                rhs_scale=picked_rows[0][:, 0 : W // 2],
+                start=(i == 0),
+                stop=(i == 5),
+            )
+        gather(1, 0, 0, W // 2)
+        gather(1, 0, W // 2, W)
+        gather(0, 1)
+        gather(1, 1)
 
-        def feature_bank(h, b, q):
-            if (h, b, q) == (0, 1, 0):
-                silus[h, b, q] = shared.tile([P, W], F32, name="silu010", offset=HOLD, align_bytes=64)
-            elif (h, b, q) == (1, 0, 1):
-                silus[h, b, q] = w2_both[:, PACK * N : PACK * N + W]
-            else:
-                silus[h, b, q] = tile([P, W], F32, "silu%d%d%d" % (h, b, q))
-            bank = psum.tile([P, PACK * P], F32, name="bank", tag="bank")
-            for t in range(PACK):
+        made = []
+
+        def feature_bank(h, b, j0, width, t0, silu):
+            bank = banks[1 + len(made) % (BANKS - 1)]
+            made.append(bank)
+            slices = W // width
+            for e in range(slices):
                 for a in range(PASSES):
-                    c = W + b * W + t * P
+                    t = t0 + e
+                    c = (1 + b) * W + t * P
                     nc.tensor.matmul_mx(
-                        bank[:, t * P : (t + 1) * P],
+                        bank[:, e * width : (e + 1) * width],
                         lhsT=w1[b][:, 2 * (a * W + t * P) : 2 * (a * W + (t + 1) * P)].bitcast(FP4X4),
                         lhsT_scale=planes[:, a, c : c + P],
                         start=(a == 0),
                         stop=(a == PASSES - 1),
-                        **table_operand(a, h, q * P, (q + 1) * P),
+                        **table_operand(a, h, j0, j0 + width),
                     )
             nc.scalar.activation(
-                silus[h, b, q][:].rearrange("p (n t) -> p n t", t=PACK),
-                bank[:].rearrange("p (t n) -> p n t", t=PACK),
-                ACT.Silu,
+                silu.rearrange("p (n e) -> p n e", e=slices), bank[:].rearrange("p (e n) -> p n e", e=slices), ACT.Silu
             )
 
-        def apply_gain(engine, x, h, b, q):
+        def narrow(h, b, j0, kib):
+            feature_bank(h, b, j0, P, 0, f32_at(kib))
+
+        def wide(h, b, j0, silu):
+            for pair in range(2):
+                feature_bank(h, b, j0, 2 * P, 2 * pair, silu[:, pair * W : (pair + 1) * W])
+
+        def gain_narrow(engine, b, src, dst, units):
             factor = gain_copy[:, b, :] if engine is nc.gpsimd else gains[:, b, :]
             engine.tensor_tensor(
-                x[:, q * W : (q + 1) * W].rearrange("p (n t) -> p n t", t=PACK),
-                silus[h, b, q][:].rearrange("p (n t) -> p n t", t=PACK),
-                factor.unsqueeze(1).broadcast_to([P, P, PACK]),
+                bf16_at(dst, units * W).rearrange("p (n t) -> p n t", t=PACK),
+                f32_at(src, units * W).rearrange("p (n t) -> p n t", t=PACK),
+                factor.unsqueeze(1).broadcast_to([P, units * P, PACK]),
                 ALU.mult,
             )
 
-        def quantize(x, width, name, held=None):
-            codes = tile([P, width], U32, name + "_codes")
-            if held is None:
-                scales = tile([P, width], U8, name + "_scales")
-            else:
-                scales = shared.tile([P, width], U8, name=name + "_scales", offset=HOLD + held * W, align_bytes=64)
-            nc.vector.quantize_mx(out=codes[:].bitcast(FP8X4), scales=scales[:], in_=x)
-            return codes[:], scales[:]
-
-
-        def round_w2(copy, a, c0, c1, room, r0=0):
-            copy(
-                room[:, (c0 - r0) * PACK : (c1 - r0) * PACK].rearrange("p (c i t) -> p c t i", t=PACK, i=4),
-                w2_raw[a][:, :, c0:c1].rearrange("p t (c i) -> p c t i", i=4),
+        def gain_wide(b, src, dst):
+            nc.vector.tensor_tensor(
+                bf16_at(dst, 2 * W).rearrange("p (n u e) -> p n u e", u=2, e=2),
+                src.rearrange("p (u n e) -> p n u e", u=2, e=2),
+                gains[:, b, :].rearrange("p (u e) -> p u e", e=2).unsqueeze(1).broadcast_to([P, 2 * P, 2, 2]),
+                ALU.mult,
             )
 
-        def quantize_w2(a, u0, u1, room, held=None):
-            codes, scales = quantize(room[:], (u1 - u0) * P, "w2%d%d" % (a, u0), held)
-            for u in range(u0, u1):
-                w2_q[a, u] = codes[:, (u - u0) * P : (u - u0 + 1) * P], scales[:, (u - u0) * P : (u - u0 + 1) * P]
+        def quantize(x, width, name, scales=None):
+            codes = tile([P, width], U32, name + "_codes")
+            if scales is None:
+                scales = tile([P, width], U8, name + "_scales")
+            nc.vector.quantize_mx(out=codes[:].bitcast(FP8X4), scales=scales[:], in_=x)
+            return codes, scales
 
-        h_q = {}
+        def round_w2(copy, raw, room):
+            copy(room.rearrange("p (c i t) -> p c t i", t=PACK, i=4), raw.rearrange("p t (c i) -> p c t i", i=4))
+
         w2_q = {}
-        diffs = {}
-        ys = {}
-        tanhs = {}
 
-        def output_diff(h, u):
-            bank = psum.tile([P, W], F32, name="bank", tag="bank")
-            for b in range(PASSES):
-                codes, scales = h_q[h, b]
-                nc.tensor.matmul_mx(
-                    bank[:],
-                    lhsT=w3[:, b, u * P : (u + 1) * P].bitcast(FP8X4),
-                    lhsT_scale=w3_planes[:, b, u * P : (u + 1) * P],
-                    rhs=codes.bitcast(FP8X4),
-                    rhs_scale=scales,
-                    start=(b == 0),
-                    stop=(b == PASSES - 1),
-                )
-            d = diff_room(h, u)
-            nc.vector.tensor_tensor(d, bank[:], olds[h][:, u, :], ALU.subtract)
-            diffs[h, u] = d
-            ys[h, u] = bank
+        H1, H0, SILU = 0, 4, 12
+        rooms["h"] = place([P, 14 * KIB // 4], F32, "h_room", 47 * KIB)
+        first_room = bf16_at(H1 - 2, 4 * W)
+        round_w2(nc.vector.tensor_copy, first_raw[:, 0], first_room[:, 0 : 2 * W])
+        narrow(0, 0, 0, SILU)
+        narrow(0, 0, P, SILU + 2)
+        wide(0, 0, 2 * P, f32_at(SILU + 4, 2 * W))
+        gain_wide(0, f32_at(SILU + 4, 2 * W), H0 + 2)
+        gain_narrow(nc.gpsimd, 0, SILU, H0, 2)
+        wide(0, 1, 0, f32_at(SILU + 8, 2 * W))
+        narrow(0, 1, 2 * P, SILU + 12)
+        narrow(0, 1, 3 * P, SILU + 14)
+        gain_wide(1, f32_at(SILU + 8, 2 * W), H0 + 4)
+        gain_narrow(nc.vector, 1, SILU + 12, H0 + 6, 1)
+        gain_narrow(nc.gpsimd, 1, SILU + 14, H0 + 7, 1)
+        held_silu = place([P, 2 * W], F32, "held_silu", 41 * KIB)
+        wide(1, 0, 2 * P, held_silu[:])
+        gain_wide(0, held_silu[:], H1 + 2)
+        round_w2(nc.scalar.copy, first_raw[:, 1], first_room[:, 2 * W :])
+        codes, scales = quantize(first_room, 4 * P, "first", place([P, 4 * P], U8, "first_scales", 41 * KIB))
+        for a in range(PASSES):
+            for u in range(2):
+                c = (2 * a + u) * P
+                w2_q[a, u] = codes[:, c : c + P], scales[:, c : c + P]
+        h_q = {0: quantize(bf16_at(H0, 8 * W), 2 * W, "h0", place([P, 2 * W], U8, "h0_scales", 42 * KIB))}
+        wide(1, 0, 0, f32_at(SILU + 18, 2 * W))
+        narrow(1, 1, 0, SILU + 22)
+        narrow(1, 1, P, SILU + 24)
+        wide(1, 1, 2 * P, f32_at(SILU + 26, 2 * W))
+        gain_wide(0, f32_at(SILU + 18, 2 * W), H1)
+        gain_narrow(nc.gpsimd, 1, SILU + 22, H1 + 4, 2)
+        gain_wide(1, f32_at(SILU + 26, 2 * W), H1 + 6)
+
+        STAY, SECOND = 42, 58
+        units = [(0, 0), (0, 1), (1, 0), (1, 1), (0, 2), (0, 3), (1, 2), (1, 3)]
+        gate_bank = dict(zip(units, (3, 4, 7, 1, 7, 1, 7, 1)))
+        y_bank = dict(zip(units, (5, 6, 0, 3, 2, 4, 5, 6)))
+        stay = {unit: f32_at(STAY + 2 * i) for i, unit in enumerate(units)}
+        held_diff = place([P, W], F32, "held_diff", 37 * KIB)
+        diff = {unit: f32_at(SECOND + 4 + 2 * i) for i, unit in enumerate(units[2:] + units[:1])}
+        diff[0, 0] = f32_at(SILU + 26)
+        diff[0, 1] = held_diff[:]
+        step = {unit: f32_at(SECOND + 18 + 2 * i) for i, unit in enumerate(units)}
+        step[0, 0] = f32_at(H1)
+        step[1, 0] = stay[0, 1]
+        step[1, 1] = f32_at(SECOND + 3)
+        result = {unit: f32_at(SILU + 2 * i) for i, unit in enumerate(units)}
+        result[0, 0] = olds[:, 1, 1, :]
+        result[0, 1] = stay[1, 0]
+        result[1, 1] = olds[:, 0, 3, :]
+        result[0, 2] = olds[:, 1, 2, :]
+        result[0, 3] = olds[:, 1, 3, :]
 
         def gate(h, u):
-            bank = psum.tile([P, W], F32, name="bank", tag="bank")
             for a in range(PASSES):
                 codes, scales = w2_q[a, u]
                 nc.tensor.matmul_mx(
-                    bank[:],
+                    banks[gate_bank[h, u]][:],
                     lhsT=codes.bitcast(FP8X4),
                     lhsT_scale=scales,
                     start=(a == 0),
                     stop=(a == PASSES - 1),
                     **table_operand(a, h, 0, W),
                 )
-            th = tile([P, W], F32, "tanh%d%d" % (h, u))
-            nc.scalar.activation(th[:], bank[:], ACT.Tanh, scale=-0.5)
-            if (h, u) in on_gpsimd:
-                stay = tile([P, W], F32, "stay%d%d" % (h, u))
-                nc.scalar.activation(stay[:], th[:], ACT.Copy, scale=0.5, bias=0.5)
-                th = stay
-            tanhs[h, u] = th
 
-        steps = {}
+        def output(h, u):
+            codes, scales = h_q[h]
+            for b in range(PASSES):
+                nc.tensor.matmul_mx(
+                    banks[y_bank[h, u]][:],
+                    lhsT=w3[:, b, u * P : (u + 1) * P].bitcast(FP8X4),
+                    lhsT_scale=w3_planes[:, b, u * P : (u + 1) * P],
+                    rhs=codes[:, b * W : (b + 1) * W].bitcast(FP8X4),
+                    rhs_scale=scales[:, b * W : (b + 1) * W],
+                    start=(b == 0),
+                    stop=(b == PASSES - 1),
+                )
 
-        def step(h, u):
-            m = step_tiles[h][:, u * W : (u + 1) * W]
-            if (h, u) == on_gpsimd[0]:
-                m = tile([P, W], F32, "step03", "tanh02")[:]
-            if (h, u) in on_gpsimd:
-                nc.gpsimd.tensor_tensor(m, tanhs[h, u][:], diffs[h, u], ALU.mult)
-            else:
-                nc.vector.scalar_tensor_tensor(m, tanhs[h, u][:], 1.0, diffs[h, u], ALU.add, ALU.mult)
-            steps[h, u] = m
+        def sigmoid(h, u):
+            nc.scalar.activation(stay[h, u], banks[gate_bank[h, u]][:], ACT.Sigmoid, scale=-1.0)
 
-        def finish(h, u, c0, c1):
-            room = units[(units.index((h, u)) + 3) % len(units)]
-            r = olds[room[0]][:, room[1], c0:c1]
-            factor = -1.0 if (h, u) in on_gpsimd else -0.5
-            nc.vector.scalar_tensor_tensor(r, steps[h, u][:, c0:c1], factor, ys[h, u][:, c0:c1], ALU.mult, ALU.add)
+        def difference(h, u):
+            nc.vector.tensor_tensor(diff[h, u], banks[y_bank[h, u]][:], olds[:, h, u, :], ALU.subtract)
+
+        def product(engine, h, u):
+            engine.tensor_tensor(step[h, u], stay[h, u], diff[h, u], ALU.mult)
+
+        def finish(h, u, c0=0, c1=W):
+            r = result[h, u][:, c0:c1]
+            nc.vector.tensor_tensor(r, banks[y_bank[h, u]][:, c0:c1], step[h, u][:, c0:c1], ALU.subtract)
             nc.sync.dma_start(out[u * P : (u + 1) * P, h * W + c0 : h * W + c1], r)
 
-        units = [(h, u) for h in range(HALVES) for u in range(TILES)]
-        on_gpsimd = units[3:]
-
-        gather(0, 0)
-        warm_bank = psum.tile([P, W], F32, name="bank", tag="bank")
-        for i in range(3):
-            nc.tensor.matmul_mx(
-                warm_bank[:],
-                lhsT=w1_raw[0][:, 0, 0 : 2 * P].bitcast(FP4X4),
-                lhsT_scale=first_rows[:, 0:P],
-                rhs=picked[0, 0][:].bitcast(FP8X4),
-                rhs_scale=first_rows[:],
-                start=(i == 0),
-                stop=(i == 2),
-            )
-        gain_copy = tile([P, PASSES, PACK], F32, "gain_copy")
-        nc.scalar.copy(gain_copy[:], gains[:, 0:PASSES, :])
-        gather(0, 1)
-        load_w1(1, 0, 2)
-        w2_both = shared.tile([P, PASSES * PACK * N], F32, name="w2_both", offset=BOTH, align_bytes=64)
-        load_w2(0, w2_both[:, 0 : PACK * N])
-        load_w2(1, w2_both[:, PACK * N : 2 * PACK * N])
-        gather(1, 0, 0, W // 2)
-        gather(1, 0, W // 2, W)
-        for q in range(PACK):
-            feature_bank(0, 0, q)
-        order_w1(nc.vector, 1)
-        late_rows = shared.tile([P, W], U8, name="late_rows", offset=RAW + W, align_bytes=64)
-        nc.vector.tensor_copy(late_rows[:], tab_rows[:].indirect(offsets_of(1)))
-        move_rows(nc.sync, late_planes, late_rows)
-        gather(1, 1)
-        w3 = tile([P, PASSES, N], U32, "w3", "table1")
-        nc.sync.dma_start(w3[:].bitcast(I32), w3_words.rearrange("b p c i -> p b (c i)").bitcast(I32))
-        w3_planes = shared.tile([P, PASSES, N], U8, name="w3_planes", offset=OLD + 32 * W, align_bytes=64)
-        nc.vector.memset(w3_planes[:].rearrange("p a c -> p (a c)").bitcast(I32), 0)
-        w3_rows = w3_scales.bitcast(I32).rearrange("a q c -> q a c")
-        for d in (0, 2, 1, 3):
-            nc.sync.dma_start(w3_planes[32 * d : 32 * d + 4, :, :].bitcast(I32), w3_rows[4 * d : 4 * d + 4])
-        old_both = shared.tile([P, HALVES * TILES * W], F32, name="old_both", offset=OLD, align_bytes=64)
-        load_old(0, old_both)
-        load_old(1, old_both)
-
-        h_room = shared.tile([P, 14 * W], BF16, name="h_room", offset=RAW + 2 * W, align_bytes=64)
-
-        def h_bf(h, b):
-            c = (0, 4, 7, 10)[PASSES * h + b] * W
-            return h_room[:, c : c + PACK * W]
-
-        def gains_of(h, b, on_pool, q0=0, q1=PACK):
-            for q in range(q0, q1):
-                apply_gain(nc.gpsimd if q in on_pool else nc.vector, h_bf(h, b), h, b, q)
-
-        def quantize_h(h, b, held=None):
-            h_q[h, b] = quantize(h_bf(h, b), W, "h%d%d" % (h, b), held)
-
-        gains_of(0, 0, (0, 1))
-        first_bf = tile([P, PACK * N], BF16, "first_bf", "silu000")
-        round_w2(nc.scalar.copy, 0, 0, P, first_bf)
-        for q in range(PACK):
-            feature_bank(0, 1, q)
-            if q > 0:
-                round_w2(nc.scalar.copy, 0, q * P, (q + 1) * P, first_bf)
-        gains_of(0, 1, (0,), 0, 2)
-        high_bf = shared.tile([P, PACK * N // 2], BF16, name="high_bf", offset=HOLD + W, align_bytes=64)
-        round_w2(nc.vector.tensor_copy, 1, N // 2, N, high_bf, N // 2)
-        quantize_w2(1, 2, 4, high_bf)
-        quantize_h(0, 0, 0)
-        low_bf = tile([P, PACK * N // 2], BF16, "low_bf", "silu011")
-        round_w2(nc.scalar.copy, 1, 0, P, low_bf)
-        round_w2(nc.scalar.copy, 1, P, 2 * P, low_bf)
-        gains_of(0, 1, (), 2, 4)
-        quantize_w2(0, 0, 4, first_bf)
-        quantize_w2(1, 0, 2, low_bf)
-        quantize_h(0, 1)
-        for b in range(PASSES):
-            for q in range(PACK):
-                feature_bank(1, b, q)
-        for b in range(PASSES):
-            gains_of(1, b, (0,))
-            quantize_h(1, b)
-        behind = shared.tile([P, 2 * TILES * W], F32, name="behind", offset=RAW + 2 * W, align_bytes=64)
-        step_tiles = [behind[:, 0 : TILES * W], tile([P, TILES * W], F32, "steps1")[:]]
-
-        def diff_room(h, u):
-            if h == 0 and u > 2:
-                return behind[:, (TILES + u) * W : (TILES + u + 1) * W]
-            return tile([P, W], F32, "diff%d%d" % (h, u))[:]
-
-        for i, unit in enumerate(units):
-            gate(*unit)
-            output_diff(*unit)
-            step(*unit)
-            if i >= 3:
-                finish(*units[i - 3], 0, W)
-        finish(*units[-3], 0, W)
-        finish(*units[-2], 0, W)
-        finish(*units[-1], 0, W // 2)
-        finish(*units[-1], W // 2, W)
+        gate(0, 0)
+        gate(0, 1)
+        output(0, 0)
+        output(0, 1)
+        gate(1, 0)
+        gate(1, 1)
+        output(0, 2)
+        sigmoid(0, 0)
+        difference(0, 0)
+        h_q[1] = quantize(bf16_at(H1, 8 * W), 2 * W, "h1")
+        output(1, 0)
+        output(1, 1)
+        sigmoid(0, 1)
+        product(nc.gpsimd, 0, 0)
+        difference(0, 1)
+        difference(0, 2)
+        second_room = bf16_at(SECOND, 4 * W)
+        round_w2(nc.scalar.copy, second_raw[:, 0], second_room[:, 0 : 2 * W])
+        sigmoid(1, 0)
+        round_w2(nc.scalar.copy, second_raw[:, 1], second_room[:, 2 * W :])
+        sigmoid(1, 1)
+        output(0, 3)
+        difference(1, 0)
+        product(nc.gpsimd, 0, 1)
+        difference(1, 1)
+        finish(0, 0)
+        codes, scales = quantize(second_room, 4 * P, "second", place([P, 4 * P], U8, "second_scales", 37 * KIB))
+        for a in range(PASSES):
+            for u in range(2, 4):
+                c = (2 * a + u - 2) * P
+                w2_q[a, u] = codes[:, c : c + P], scales[:, c : c + P]
+        product(nc.vector, 1, 0)
+        product(nc.gpsimd, 1, 1)
+        gate(0, 2)
+        sigmoid(0, 2)
+        gate(0, 3)
+        sigmoid(0, 3)
+        output(1, 2)
+        finish(0, 1)
+        gate(1, 2)
+        sigmoid(1, 2)
+        output(1, 3)
+        gate(1, 3)
+        sigmoid(1, 3)
+        finish(1, 0)
+        product(nc.gpsimd, 0, 2)
+        difference(0, 3)
+        finish(1, 1)
+        product(nc.gpsimd, 0, 3)
+        difference(1, 2)
+        finish(0, 2)
+        product(nc.gpsimd, 1, 2)
+        difference(1, 3)
+        finish(0, 3)
+        product(nc.gpsimd, 1, 3)
+        finish(1, 2)
+        finish(1, 3, 0, W // 2)
+        finish(1, 3, W // 2, W)

@@ -101,8 +101,8 @@ def tile_list_register_file_step_kernel(
 
         w1 = [tile([P, PASSES * 2 * W], U8, "w1_%d" % b) for b in range(2)]
 
-        def order_w1(b):
-            nc.scalar.copy(
+        def order_w1(copy, b):
+            copy(
                 w1[b][:].bitcast(U16).rearrange("p (a t m) -> p a t m", a=PASSES, t=PACK),
                 w1_raw[b][:].rearrange("p a c -> p (a c)").bitcast(U16).rearrange("p (a m t) -> p a t m", a=PASSES, t=PACK),
             )
@@ -119,7 +119,7 @@ def tile_list_register_file_step_kernel(
             for d in QUADS:
                 queue.dma_start(dst[32 * d : 32 * d + 4, :, :].bitcast(I32), src[32 * d : 32 * d + 32 : 4, :].bitcast(I32))
 
-        order_w1(0)
+        order_w1(nc.scalar.copy, 0)
         gather_rows(0)
         nc.vector.tensor_copy(
             rows[:, W:].rearrange("p (b t m) -> p b t m", b=2, t=PACK),
@@ -127,7 +127,7 @@ def tile_list_register_file_step_kernel(
         )
         nc.vector.tensor_copy(rows[:, 0:W].bitcast(I32), picked_rows[0][:].bitcast(I32))
         move_rows(nc.scalar, planes, rows)
-        order_w1(1)
+        order_w1(nc.scalar.copy, 1)
         gather_rows(1)
 
         def load_w2(raw, a, half):
@@ -172,6 +172,11 @@ def tile_list_register_file_step_kernel(
         gather(0, 0)
         gain_copy = tile([P, 2, PACK], F32, "gain_copy")
         nc.scalar.copy(gain_copy[:], gains[:, 0:2, :])
+        gain_whole = tile([P, 2, W], F32, "gain_whole")
+        nc.scalar.copy(
+            gain_whole[:].rearrange("p b (n t) -> p b n t", t=PACK),
+            gain_copy[:].unsqueeze(2).broadcast_to([P, 2, P, PACK]),
+        )
         for i in range(6):
             nc.tensor.matmul_mx(
                 banks[0][:, W // 2 :],
@@ -216,12 +221,19 @@ def tile_list_register_file_step_kernel(
             for pair in range(2):
                 feature_bank(h, b, j0, 2 * P, 2 * pair, silu[:, pair * W : (pair + 1) * W])
 
-        def gain_narrow(engine, b, src, dst, units):
-            factor = gain_copy[:, b, :] if engine is nc.gpsimd else gains[:, b, :]
-            engine.tensor_tensor(
-                bf16_at(dst, units * W).rearrange("p (n t) -> p n t", t=PACK),
-                f32_at(src, units * W).rearrange("p (n t) -> p n t", t=PACK),
-                factor.unsqueeze(1).broadcast_to([P, units * P, PACK]),
+        def gain_narrow(b, src, dst):
+            nc.vector.tensor_tensor(
+                bf16_at(dst, W).rearrange("p (n t) -> p n t", t=PACK),
+                f32_at(src).rearrange("p (n t) -> p n t", t=PACK),
+                gains[:, b, :].unsqueeze(1).broadcast_to([P, P, PACK]),
+                ALU.mult,
+            )
+
+        def gain_gpsimd(b, src, dst, units):
+            nc.gpsimd.tensor_tensor(
+                bf16_at(dst, units * W).rearrange("p (u c) -> p u c", c=W),
+                f32_at(src, units * W).rearrange("p (u c) -> p u c", c=W),
+                gain_whole[:, b, :].unsqueeze(1).broadcast_to([P, units, W]),
                 ALU.mult,
             )
 
@@ -253,13 +265,13 @@ def tile_list_register_file_step_kernel(
         narrow(0, 0, P, SILU + 2)
         wide(0, 0, 2 * P, f32_at(SILU + 4, 2 * W))
         gain_wide(0, f32_at(SILU + 4, 2 * W), H0 + 2)
-        gain_narrow(nc.gpsimd, 0, SILU, H0, 2)
+        gain_gpsimd(0, SILU, H0, 2)
         wide(0, 1, 0, f32_at(SILU + 8, 2 * W))
-        narrow(0, 1, 2 * P, SILU + 12)
+        narrow(0, 1, 2 * P, H1)
         narrow(0, 1, 3 * P, SILU + 14)
         gain_wide(1, f32_at(SILU + 8, 2 * W), H0 + 4)
-        gain_narrow(nc.vector, 1, SILU + 12, H0 + 6, 1)
-        gain_narrow(nc.gpsimd, 1, SILU + 14, H0 + 7, 1)
+        gain_narrow(1, H1, H0 + 6)
+        gain_gpsimd(1, SILU + 14, H0 + 7, 1)
         held_silu = place([P, 2 * W], F32, "held_silu", 41 * KIB)
         wide(1, 0, 2 * P, held_silu[:])
         gain_wide(0, held_silu[:], H1 + 2)
@@ -275,13 +287,13 @@ def tile_list_register_file_step_kernel(
         narrow(1, 1, P, SILU + 24)
         wide(1, 1, 2 * P, f32_at(SILU + 26, 2 * W))
         gain_wide(0, f32_at(SILU + 18, 2 * W), H1)
-        gain_narrow(nc.gpsimd, 1, SILU + 22, H1 + 4, 2)
+        gain_gpsimd(1, SILU + 22, H1 + 4, 2)
         gain_wide(1, f32_at(SILU + 26, 2 * W), H1 + 6)
 
         STAY, SECOND = 42, 58
         units = [(0, 0), (0, 1), (1, 0), (1, 1), (0, 2), (0, 3), (1, 2), (1, 3)]
-        gate_bank = dict(zip(units, (3, 4, 7, 1, 7, 1, 7, 1)))
-        y_bank = dict(zip(units, (5, 6, 0, 3, 2, 4, 5, 6)))
+        gate_bank = dict(zip(units, (3, 4, 3, 4, 3, 4, 3, 4)))
+        y_bank = dict(zip(units, (5, 6, 2, 0, 7, 1, 5, 6)))
         stay = {unit: f32_at(STAY + 2 * i) for i, unit in enumerate(units)}
         held_diff = place([P, W], F32, "held_diff", 37 * KIB)
         diff = {unit: f32_at(SECOND + 4 + 2 * i) for i, unit in enumerate(units[2:] + units[:1])}
@@ -327,29 +339,30 @@ def tile_list_register_file_step_kernel(
             nc.scalar.activation(stay[h, u], banks[gate_bank[h, u]][:], ACT.Sigmoid, scale=-1.0)
 
         def difference(h, u):
-            nc.vector.tensor_tensor(diff[h, u], banks[y_bank[h, u]][:], olds[:, h, u, :], ALU.subtract)
+            nc.vector.tensor_tensor(diff[h, u], olds[:, h, u, :], banks[y_bank[h, u]][:], ALU.subtract)
 
         def product(engine, h, u):
             engine.tensor_tensor(step[h, u], stay[h, u], diff[h, u], ALU.mult)
 
         def finish(h, u, c0=0, c1=W):
             r = result[h, u][:, c0:c1]
-            nc.vector.tensor_tensor(r, banks[y_bank[h, u]][:, c0:c1], step[h, u][:, c0:c1], ALU.subtract)
+            nc.vector.tensor_tensor(r, step[h, u][:, c0:c1], banks[y_bank[h, u]][:, c0:c1], ALU.add)
             nc.sync.dma_start(out[u * P : (u + 1) * P, h * W + c0 : h * W + c1], r)
 
         gate(0, 0)
         gate(0, 1)
         output(0, 0)
         output(0, 1)
-        gate(1, 0)
-        gate(1, 1)
         output(0, 2)
+        output(0, 3)
         sigmoid(0, 0)
+        gate(1, 0)
+        sigmoid(0, 1)
+        gate(1, 1)
         difference(0, 0)
         h_q[1] = quantize(bf16_at(H1, 8 * W), 2 * W, "h1")
         output(1, 0)
         output(1, 1)
-        sigmoid(0, 1)
         product(nc.gpsimd, 0, 0)
         difference(0, 1)
         difference(0, 2)
@@ -358,7 +371,6 @@ def tile_list_register_file_step_kernel(
         sigmoid(1, 0)
         round_w2(nc.scalar.copy, second_raw[:, 1], second_room[:, 2 * W :])
         sigmoid(1, 1)
-        output(0, 3)
         difference(1, 0)
         product(nc.gpsimd, 0, 1)
         difference(1, 1)

@@ -46,7 +46,7 @@ def tile_list_register_file_step_kernel(
         rooms = {}
 
         def f32_at(kib, columns=W):
-            room, c = (rooms["h"], (kib + 2) * KIB // 4) if kib < 12 else (arena, (kib - 12) * KIB // 4)
+            room, c = (rooms["h"], kib * KIB // 4) if kib < 12 else (arena, (kib - 12) * KIB // 4)
             return room[:, c : c + columns]
 
         def bf16_at(kib, columns):
@@ -55,7 +55,7 @@ def tile_list_register_file_step_kernel(
         offsets = keep.tile([P, S // 16], U16, name="offsets")
         nc.sync.dma_start(offsets[:], offs)
 
-        w1_raw = [tile([P, PASSES, 2 * W], U8, "w1_raw0"), place([P, PASSES, 2 * W], U8, "w1_raw1", 39 * KIB)]
+        w1_raw = [tile([P, PASSES, 2 * W], U8, "w1_raw0"), place([P, PASSES, 2 * W], U8, "w1_raw1", 70 * KIB)]
 
         def load_w1(b):
             src = w1_words[:, :, 2 * W * b : 2 * W * (b + 1)].bitcast(I32).rearrange("a p c -> p a c")
@@ -85,7 +85,7 @@ def tile_list_register_file_step_kernel(
         load_w1(0)
         nc.scalar.activation(warm[:, 1:2], warm[:, 0:1], ACT.Silu)
 
-        table = [place([P, T], U32, "table%d" % a, (46 + 8 * a) * KIB) for a in range(PASSES)]
+        table = [place([P, T], U32, "table%d" % a, (54 + 8 * a) * KIB) for a in range(PASSES)]
 
         def load_table(a):
             nc.sync.dma_start(table[a][:].bitcast(I32), tab_words[a].rearrange("p t i -> p (t i)").bitcast(I32))
@@ -132,13 +132,15 @@ def tile_list_register_file_step_kernel(
 
         def load_w2(raw, a, half):
             src = w2[a * W : (a + 1) * W, half * (N // 2) : (half + 1) * (N // 2)]
-            nc.sync.dma_start(raw[:, a], src.rearrange("(p t) n -> p t n", t=PACK))
+            nc.sync.dma_start(raw, src.rearrange("(p t) n -> p t n", t=PACK))
 
         move_rows(nc.sync, late_planes, picked_rows[1])
-        floats = place([P, 8 * KIB], F32, "floats", 4 * KIB + 512)
-        first_raw = floats[:, 6 * KIB :].rearrange("p (a t n) -> p a t n", a=PASSES, t=PACK)
+        floats = place([P, 10 * KIB], F32, "floats", 4 * KIB + 512)
+        rooms["h"] = floats[:, 7 * KIB :]
+        H1, H0, SILU = 0, 4, 12
+        first_raw = [x.rearrange("p (t n) -> p t n", t=PACK) for x in (f32_at(H0, 2 * W), floats[:, 6 * KIB : 7 * KIB])]
         for a in range(PASSES):
-            load_w2(first_raw, a, 0)
+            load_w2(first_raw[a], a, 0)
 
         w3 = place([P, PASSES, N], U32, "w3", 0)
         nc.sync.dma_start(w3[:].bitcast(I32), w3_words.rearrange("b p c i -> p b (c i)").bitcast(I32))
@@ -155,13 +157,13 @@ def tile_list_register_file_step_kernel(
         for d in QUADS:
             nc.sync.dma_start(w3_planes[32 * d : 32 * d + 4].bitcast(I32), w3_rows[4 * d : 4 * d + 4])
         for a in range(PASSES):
-            load_w2(second_raw, a, 1)
+            load_w2(second_raw[:, a], a, 1)
         load_old(0, 2)
         load_old(1, 0)
         load_old(1, 2)
 
         picked = {(a, h): tile([P, W], U32, "picked%d%d" % (a, h)) for a, h in ((0, 0), (1, 0), (1, 1))}
-        picked[0, 1] = place([P, W], U32, "picked01", 39 * KIB)
+        picked[0, 1] = place([P, W], U32, "picked01", 70 * KIB)
 
         def gather(a, h, c0=0, c1=W):
             nc.vector.tensor_copy(picked[a, h][:, c0:c1], table[a][:].indirect(offsets_of(h, c0, c1)))
@@ -257,10 +259,8 @@ def tile_list_register_file_step_kernel(
 
         w2_q = {}
 
-        H1, H0, SILU = 0, 4, 12
-        rooms["h"] = place([P, 14 * KIB // 4], F32, "h_room", 47 * KIB)
-        first_room = bf16_at(H1 - 2, 4 * W)
-        round_w2(nc.vector.tensor_copy, first_raw[:, 0], first_room[:, 0 : 2 * W])
+        first_room = (place([P, 2 * W], BF16, "first_room", 61 * KIB)[:], bf16_at(H1, 2 * W))
+        round_w2(nc.vector.tensor_copy, first_raw[0], first_room[0])
         narrow(0, 0, 0, SILU)
         narrow(0, 0, P, SILU + 2)
         wide(0, 0, 2 * P, f32_at(SILU + 4, 2 * W))
@@ -272,16 +272,16 @@ def tile_list_register_file_step_kernel(
         gain_wide(1, f32_at(SILU + 8, 2 * W), H0 + 4)
         gain_narrow(1, H1, H0 + 6)
         gain_gpsimd(1, SILU + 14, H0 + 7, 1)
-        held_silu = place([P, 2 * W], F32, "held_silu", 41 * KIB)
+        held_silu = place([P, 2 * W], F32, "held_silu", 49 * KIB)
         wide(1, 0, 2 * P, held_silu[:])
         gain_wide(0, held_silu[:], H1 + 2)
-        round_w2(nc.scalar.copy, first_raw[:, 1], first_room[:, 2 * W :])
-        codes, scales = quantize(first_room, 4 * P, "first", place([P, 4 * P], U8, "first_scales", 41 * KIB))
+        round_w2(nc.scalar.copy, first_raw[1], first_room[1])
         for a in range(PASSES):
+            held = place([P, 2 * P], U8, "first%d_scales" % a, 49 * KIB + 2 * P * a)
+            codes, scales = quantize(first_room[a], 2 * P, "first%d" % a, held)
             for u in range(2):
-                c = (2 * a + u) * P
-                w2_q[a, u] = codes[:, c : c + P], scales[:, c : c + P]
-        h_q = {0: quantize(bf16_at(H0, 8 * W), 2 * W, "h0", place([P, 2 * W], U8, "h0_scales", 42 * KIB))}
+                w2_q[a, u] = codes[:, u * P : (u + 1) * P], scales[:, u * P : (u + 1) * P]
+        h_q = {0: quantize(bf16_at(H0, 8 * W), 2 * W, "h0", place([P, 2 * W], U8, "h0_scales", 50 * KIB))}
         wide(1, 0, 0, f32_at(SILU + 18, 2 * W))
         narrow(1, 1, 0, SILU + 22)
         narrow(1, 1, P, SILU + 24)
@@ -295,7 +295,7 @@ def tile_list_register_file_step_kernel(
         gate_bank = dict(zip(units, (3, 4, 3, 4, 3, 4, 3, 4)))
         y_bank = dict(zip(units, (5, 6, 2, 0, 7, 1, 5, 6)))
         stay = {unit: f32_at(STAY + 2 * i) for i, unit in enumerate(units)}
-        held_diff = place([P, W], F32, "held_diff", 37 * KIB)
+        held_diff = place([P, W], F32, "held_diff", 47 * KIB)
         diff = {unit: f32_at(SECOND + 4 + 2 * i) for i, unit in enumerate(units[2:] + units[:1])}
         diff[0, 0] = f32_at(SILU + 26)
         diff[0, 1] = held_diff[:]
@@ -375,7 +375,7 @@ def tile_list_register_file_step_kernel(
         product(nc.gpsimd, 0, 1)
         difference(1, 1)
         finish(0, 0)
-        codes, scales = quantize(second_room, 4 * P, "second", place([P, 4 * P], U8, "second_scales", 37 * KIB))
+        codes, scales = quantize(second_room, 4 * P, "second", place([P, 4 * P], U8, "second_scales", 47 * KIB))
         for a in range(PASSES):
             for u in range(2, 4):
                 c = (2 * a + u - 2) * P

@@ -42,7 +42,7 @@ def tile_list_register_file_step_kernel(
             return placed.tile(shape, dtype, name=name, offset=offset, align_bytes=64)
 
         banks = [psum.tile([P, W], F32, name="bank%d" % i) for i in range(BANKS)]
-        arena = tile([P, 82 * KIB // 4], F32, "arena")
+        arena = tile([P, 84 * KIB // 4], F32, "arena")
         rooms = {}
 
         def f32_at(kib, columns=W):
@@ -290,21 +290,22 @@ def tile_list_register_file_step_kernel(
         gain_gpsimd(1, SILU + 22, H1 + 4, 2)
         gain_wide(1, f32_at(SILU + 26, 2 * W), H1 + 6)
 
-        STAY, SECOND = 42, 58
+        STAY, SECOND = 42, 60
         units = [(0, 0), (0, 1), (1, 0), (1, 1), (0, 2), (0, 3), (1, 2), (1, 3)]
         gate_bank = dict(zip(units, (3, 4, 3, 4, 3, 4, 3, 4)))
         y_bank = dict(zip(units, (5, 6, 2, 0, 7, 1, 5, 6)))
-        stay = {unit: f32_at(STAY + 2 * i) for i, unit in enumerate(units)}
+        stay = {unit: f32_at(STAY + 2 * (i + (i > 1))) for i, unit in enumerate(units)}
         held_diff = place([P, W], F32, "held_diff", 47 * KIB)
-        diff = {unit: f32_at(SECOND + 4 + 2 * i) for i, unit in enumerate(units[2:] + units[:1])}
+        diff = {unit: f32_at(SECOND + 4 + 2 * i) for i, unit in enumerate(units[3:] + units[2:3])}
         diff[0, 0] = f32_at(SILU + 26)
         diff[0, 1] = held_diff[:]
         step = {unit: f32_at(SECOND + 18 + 2 * i) for i, unit in enumerate(units)}
         step[0, 0] = f32_at(H1)
-        step[1, 0] = stay[0, 1]
-        step[1, 1] = f32_at(SECOND + 3)
+        step[1, 0] = f32_at(STAY + 1)
+        step[1, 1] = f32_at(STAY + 3)
+        step[0, 2] = f32_at(SECOND + 3)
         result = {unit: f32_at(SILU + 2 * i) for i, unit in enumerate(units)}
-        result[0, 0] = olds[:, 1, 1, :]
+        result[0, 0] = diff[1, 0]
         result[0, 1] = stay[1, 0]
         result[1, 1] = olds[:, 0, 3, :]
         result[0, 2] = olds[:, 1, 2, :]
@@ -374,14 +375,14 @@ def tile_list_register_file_step_kernel(
         difference(1, 0)
         product(nc.gpsimd, 0, 1)
         difference(1, 1)
-        finish(0, 0)
         codes, scales = quantize(second_room, 4 * P, "second", place([P, 4 * P], U8, "second_scales", 47 * KIB))
         for a in range(PASSES):
             for u in range(2, 4):
                 c = (2 * a + u - 2) * P
                 w2_q[a, u] = codes[:, c : c + P], scales[:, c : c + P]
         product(nc.vector, 1, 0)
-        product(nc.gpsimd, 1, 1)
+        product(nc.vector, 1, 1)
+        finish(0, 0)
         gate(0, 2)
         sigmoid(0, 2)
         gate(0, 3)
@@ -405,5 +406,5 @@ def tile_list_register_file_step_kernel(
         finish(0, 3)
         product(nc.gpsimd, 1, 3)
         finish(1, 2)
-        finish(1, 3, 0, W // 2)
-        finish(1, 3, W // 2, W)
+        finish(1, 3, 0, 3 * W // 4)
+        finish(1, 3, 3 * W // 4, W)

@@ -46,7 +46,7 @@ def tile_list_register_file_step_kernel(
         rooms = {}
 
         def f32_at(kib, columns=W):
-            room, c = (rooms["h"], kib * KIB // 4) if kib < 12 else (arena, (kib - 12) * KIB // 4)
+            room, c = (rooms["h"], kib * KIB // 4) if kib < 16 else (arena, (kib - 16) * KIB // 4)
             return room[:, c : c + columns]
 
         def bf16_at(kib, columns):
@@ -135,9 +135,9 @@ def tile_list_register_file_step_kernel(
             nc.sync.dma_start(raw, src.rearrange("(p t) n -> p t n", t=PACK))
 
         move_rows(nc.sync, late_planes, picked_rows[1])
-        floats = place([P, 10 * KIB], F32, "floats", 4 * KIB + 512)
+        floats = place([P, 11 * KIB], F32, "floats", 4 * KIB + 512)
         rooms["h"] = floats[:, 7 * KIB :]
-        H1, H0, SILU = 0, 4, 12
+        H1, H0, SILU = 6, 0, 16
         first_raw = [x.rearrange("p (t n) -> p t n", t=PACK) for x in (f32_at(H0, 2 * W), floats[:, 6 * KIB : 7 * KIB])]
         for a in range(PASSES):
             load_w2(first_raw[a], a, 0)
@@ -171,7 +171,8 @@ def tile_list_register_file_step_kernel(
         def table_operand(a, h, c0, c1):
             return {"rhs": picked[a, h][:, c0:c1].bitcast(FP8X4), "rhs_scale": (planes, late_planes)[h][:, a, c0:c1]}
 
-        gather(0, 0)
+        gather(0, 0, 0, W // 2)
+        gather(0, 0, W // 2, W)
         gain_copy = tile([P, 2, PACK], F32, "gain_copy")
         nc.scalar.copy(gain_copy[:], gains[:, 0:2, :])
         gain_whole = tile([P, 2, W], F32, "gain_whole")
@@ -197,7 +198,7 @@ def tile_list_register_file_step_kernel(
         made = []
 
         def feature_bank(h, b, j0, width, t0, silu):
-            bank = banks[1 + len(made) % (BANKS - 1)]
+            bank = banks[1 + len(made) % 5]
             made.append(bank)
             slices = W // width
             for e in range(slices):
@@ -226,7 +227,7 @@ def tile_list_register_file_step_kernel(
         def gain_narrow(b, src, dst):
             nc.vector.tensor_tensor(
                 bf16_at(dst, W).rearrange("p (n t) -> p n t", t=PACK),
-                f32_at(src).rearrange("p (n t) -> p n t", t=PACK),
+                src.rearrange("p (n t) -> p n t", t=PACK),
                 gains[:, b, :].unsqueeze(1).broadcast_to([P, P, PACK]),
                 ALU.mult,
             )
@@ -259,7 +260,7 @@ def tile_list_register_file_step_kernel(
 
         w2_q = {}
 
-        first_room = (place([P, 2 * W], BF16, "first_room", 61 * KIB)[:], bf16_at(H1, 2 * W))
+        first_room = [place([P, 2 * W], BF16, "first_room0", 61 * KIB)[:]]
         round_w2(nc.vector.tensor_copy, first_raw[0], first_room[0])
         narrow(0, 0, 0, SILU)
         narrow(0, 0, P, SILU + 2)
@@ -267,21 +268,26 @@ def tile_list_register_file_step_kernel(
         gain_wide(0, f32_at(SILU + 4, 2 * W), H0 + 2)
         gain_gpsimd(0, SILU, H0, 2)
         wide(0, 1, 0, f32_at(SILU + 8, 2 * W))
-        narrow(0, 1, 2 * P, H1)
         narrow(0, 1, 3 * P, SILU + 14)
         gain_wide(1, f32_at(SILU + 8, 2 * W), H0 + 4)
-        gain_narrow(1, H1, H0 + 6)
         gain_gpsimd(1, SILU + 14, H0 + 7, 1)
-        held_silu = place([P, 2 * W], F32, "held_silu", 49 * KIB)
-        wide(1, 0, 2 * P, held_silu[:])
-        gain_wide(0, held_silu[:], H1 + 2)
+        wide(1, 0, 2 * P, f32_at(H1 + 4, 2 * W))
+        gain_wide(0, f32_at(H1 + 4, 2 * W), H1 + 2)
+        held_silu = place([P, W], F32, "held_silu", 51 * KIB)
+        feature_bank(0, 1, 2 * P, P, 0, held_silu[:])
+        gain_narrow(1, held_silu[:], H0 + 6)
+        first_room.append(bf16_at(H1 + 4, 2 * W))
         round_w2(nc.scalar.copy, first_raw[1], first_room[1])
-        for a in range(PASSES):
-            held = place([P, 2 * P], U8, "first%d_scales" % a, 49 * KIB + 2 * P * a)
+
+        def quantize_first(a):
+            held = place([P, 2 * P], U8, "first%d_scales" % a, 51 * KIB + 2 * P * a)
             codes, scales = quantize(first_room[a], 2 * P, "first%d" % a, held)
             for u in range(2):
                 w2_q[a, u] = codes[:, u * P : (u + 1) * P], scales[:, u * P : (u + 1) * P]
-        h_q = {0: quantize(bf16_at(H0, 8 * W), 2 * W, "h0", place([P, 2 * W], U8, "h0_scales", 50 * KIB))}
+
+        quantize_first(0)
+        h_q = {0: quantize(bf16_at(H0, 8 * W), 2 * W, "h0", place([P, 2 * W], U8, "h0_scales", 52 * KIB))}
+        quantize_first(1)
         wide(1, 0, 0, f32_at(SILU + 18, 2 * W))
         narrow(1, 1, 0, SILU + 22)
         narrow(1, 1, P, SILU + 24)
@@ -290,12 +296,12 @@ def tile_list_register_file_step_kernel(
         gain_gpsimd(1, SILU + 22, H1 + 4, 2)
         gain_wide(1, f32_at(SILU + 26, 2 * W), H1 + 6)
 
-        STAY, SECOND = 42, 60
+        STAY, SECOND = 46, 64
         units = [(0, 0), (0, 1), (1, 0), (1, 1), (0, 2), (0, 3), (1, 2), (1, 3)]
-        gate_bank = dict(zip(units, (3, 4, 3, 4, 3, 4, 3, 4)))
-        y_bank = dict(zip(units, (5, 6, 2, 0, 7, 1, 5, 6)))
+        gate_bank = dict(zip(units, (6, 7, 6, 7, 6, 7, 6, 7)))
+        y_bank = dict(zip(units, (2, 3, 1, 0, 4, 5, 2, 3)))
         stay = {unit: f32_at(STAY + 2 * (i + (i > 1))) for i, unit in enumerate(units)}
-        held_diff = place([P, W], F32, "held_diff", 47 * KIB)
+        held_diff = place([P, W], F32, "held_diff", 49 * KIB)
         diff = {unit: f32_at(SECOND + 4 + 2 * i) for i, unit in enumerate(units[3:] + units[2:3])}
         diff[0, 0] = f32_at(SILU + 26)
         diff[0, 1] = held_diff[:]
@@ -342,8 +348,8 @@ def tile_list_register_file_step_kernel(
         def difference(h, u):
             nc.vector.tensor_tensor(diff[h, u], olds[:, h, u, :], banks[y_bank[h, u]][:], ALU.subtract)
 
-        def product(engine, h, u):
-            engine.tensor_tensor(step[h, u], stay[h, u], diff[h, u], ALU.mult)
+        def product(engine, h, u, c0=0, c1=W):
+            engine.tensor_tensor(step[h, u][:, c0:c1], stay[h, u][:, c0:c1], diff[h, u][:, c0:c1], ALU.mult)
 
         def finish(h, u, c0=0, c1=W):
             r = result[h, u][:, c0:c1]
@@ -375,7 +381,7 @@ def tile_list_register_file_step_kernel(
         difference(1, 0)
         product(nc.gpsimd, 0, 1)
         difference(1, 1)
-        codes, scales = quantize(second_room, 4 * P, "second", place([P, 4 * P], U8, "second_scales", 47 * KIB))
+        codes, scales = quantize(second_room, 4 * P, "second", place([P, 4 * P], U8, "second_scales", 49 * KIB))
         for a in range(PASSES):
             for u in range(2, 4):
                 c = (2 * a + u - 2) * P
@@ -404,7 +410,8 @@ def tile_list_register_file_step_kernel(
         product(nc.gpsimd, 1, 2)
         difference(1, 3)
         finish(0, 3)
-        product(nc.gpsimd, 1, 3)
+        product(nc.gpsimd, 1, 3, 0, 3 * W // 4)
+        product(nc.gpsimd, 1, 3, 3 * W // 4, W)
         finish(1, 2)
         finish(1, 3, 0, 3 * W // 4)
         finish(1, 3, 3 * W // 4, W)

@@ -63,9 +63,8 @@ def tile_list_register_file_step_kernel(
 
         tab_rows = tile([P, T], U8, "tab_rows")
         w1_rows = tile([P, H], U8, "w1_rows")
-        rows = tile([P, 3 * W], U8, "rows")
-        planes = tile([P, PASSES, 3 * W], U8, "planes")
-        late_planes = tile([P, PASSES, W], U8, "late_planes")
+        rows = tile([P, 4 * W], U8, "rows")
+        planes = [tile([P, PASSES, 2 * W], U8, "planes%d" % i) for i in range(2)]
         warm = tile([P, 2], F32, "warm")
         gain_rows = place([P, W], F32, "gain_rows", 4 * KIB - 512)
         identity = tile([P, P], F32, "identity")
@@ -73,8 +72,8 @@ def tile_list_register_file_step_kernel(
         nc.vector.memset(w1_rows[:].bitcast(I32), 0)
         nc.vector.memset(warm[:, 0:1], 0.0)
         nc.vector.memset(gain_rows[:], 0.0)
-        nc.vector.memset(planes[:].rearrange("p a c -> p (a c)").bitcast(I32), 0)
-        nc.vector.memset(late_planes[:].rearrange("p a c -> p (a c)").bitcast(I32), 0)
+        for plane in planes:
+            nc.vector.memset(plane[:].rearrange("p a c -> p (a c)").bitcast(I32), 0)
         make_identity(nc, identity[:])
 
         def load_rows(dst, scales):
@@ -122,11 +121,11 @@ def tile_list_register_file_step_kernel(
         order_w1(nc.scalar.copy, 0)
         gather_rows(0)
         nc.vector.tensor_copy(
-            rows[:, W:].rearrange("p (b t m) -> p b t m", b=2, t=PACK),
+            rows[:, W : 3 * W].rearrange("p (b t m) -> p b t m", b=2, t=PACK),
             w1_rows[:].rearrange("p (b m t) -> p b t m", b=2, t=PACK),
         )
         nc.vector.tensor_copy(rows[:, 0:W].bitcast(I32), picked_rows[0][:].bitcast(I32))
-        move_rows(nc.scalar, planes, rows)
+        move_rows(nc.sync, planes[0], rows[:, 0 : 2 * W])
         order_w1(nc.scalar.copy, 1)
         gather_rows(1)
 
@@ -134,7 +133,8 @@ def tile_list_register_file_step_kernel(
             src = w2[a * W : (a + 1) * W, half * (N // 2) : (half + 1) * (N // 2)]
             nc.sync.dma_start(raw, src.rearrange("(p t) n -> p t n", t=PACK))
 
-        move_rows(nc.sync, late_planes, picked_rows[1])
+        nc.vector.tensor_copy(rows[:, 3 * W :].bitcast(I32), picked_rows[1][:].bitcast(I32))
+        move_rows(nc.sync, planes[1], rows[:, 2 * W :])
         floats = place([P, 11 * KIB], F32, "floats", 4 * KIB + 512)
         rooms["h"] = floats[:, 7 * KIB :]
         H1, H0, SILU = 6, 0, 16
@@ -169,7 +169,7 @@ def tile_list_register_file_step_kernel(
             nc.vector.tensor_copy(picked[a, h][:, c0:c1], table[a][:].indirect(offsets_of(h, c0, c1)))
 
         def table_operand(a, h, c0, c1):
-            return {"rhs": picked[a, h][:, c0:c1].bitcast(FP8X4), "rhs_scale": (planes, late_planes)[h][:, a, c0:c1]}
+            return {"rhs": picked[a, h][:, c0:c1].bitcast(FP8X4), "rhs_scale": planes[h][:, a, h * W + c0 : h * W + c1]}
 
         gather(0, 0, 0, W // 2)
         gather(0, 0, W // 2, W)
@@ -204,11 +204,11 @@ def tile_list_register_file_step_kernel(
             for e in range(slices):
                 for a in range(PASSES):
                     t = t0 + e
-                    c = (1 + b) * W + t * P
+                    c = (1 - b) * W + t * P
                     nc.tensor.matmul_mx(
                         bank[:, e * width : (e + 1) * width],
                         lhsT=w1[b][:, 2 * (a * W + t * P) : 2 * (a * W + (t + 1) * P)].bitcast(FP4X4),
-                        lhsT_scale=planes[:, a, c : c + P],
+                        lhsT_scale=planes[b][:, a, c : c + P],
                         start=(a == 0),
                         stop=(a == PASSES - 1),
                         **table_operand(a, h, j0, j0 + width),
@@ -260,7 +260,7 @@ def tile_list_register_file_step_kernel(
 
         w2_q = {}
 
-        first_room = [place([P, 2 * W], BF16, "first_room0", 61 * KIB)[:]]
+        first_room = [bf16_at(SILU + 16, 2 * W)]
         round_w2(nc.vector.tensor_copy, first_raw[0], first_room[0])
         narrow(0, 0, 0, SILU)
         narrow(0, 0, P, SILU + 2)
@@ -298,7 +298,7 @@ def tile_list_register_file_step_kernel(
 
         STAY, SECOND = 46, 64
         units = [(0, 0), (0, 1), (1, 0), (1, 1), (0, 2), (0, 3), (1, 2), (1, 3)]
-        gate_bank = dict(zip(units, (6, 7, 6, 7, 6, 7, 6, 7)))
+        gate_bank = dict(zip(units, (6, 7, 6, 6, 7, 6, 7, 6)))
         y_bank = dict(zip(units, (2, 3, 1, 0, 4, 5, 2, 3)))
         stay = {unit: f32_at(STAY + 2 * (i + (i > 1))) for i, unit in enumerate(units)}
         held_diff = place([P, W], F32, "held_diff", 49 * KIB)
@@ -365,7 +365,6 @@ def tile_list_register_file_step_kernel(
         sigmoid(0, 0)
         gate(1, 0)
         sigmoid(0, 1)
-        gate(1, 1)
         difference(0, 0)
         h_q[1] = quantize(bf16_at(H1, 8 * W), 2 * W, "h1")
         output(1, 0)
@@ -376,6 +375,7 @@ def tile_list_register_file_step_kernel(
         second_room = bf16_at(SECOND, 4 * W)
         round_w2(nc.scalar.copy, second_raw[:, 0], second_room[:, 0 : 2 * W])
         sigmoid(1, 0)
+        gate(1, 1)
         round_w2(nc.scalar.copy, second_raw[:, 1], second_room[:, 2 * W :])
         sigmoid(1, 1)
         difference(1, 0)

@@ -72,9 +72,10 @@ def tile_list_register_file_step_kernel(
         nc.vector.memset(w1_rows[:].bitcast(I32), 0)
         nc.vector.memset(warm[:, 0:1], 0.0)
         nc.vector.memset(gain_rows[:], 0.0)
+        nc.vector.memset(identity[:], 0.0)
         for plane in planes:
             nc.vector.memset(plane[:].rearrange("p a c -> p (a c)").bitcast(I32), 0)
-        make_identity(nc, identity[:])
+        make_identity(nc, identity[:], nomemset=True)
 
         def load_rows(dst, scales):
             nc.sync.dma_start(dst.bitcast(I32), scales.bitcast(I32).rearrange("a q c -> q a c"))
@@ -175,10 +176,10 @@ def tile_list_register_file_step_kernel(
         gather(0, 0, W // 2, W)
         gain_copy = tile([P, 2, PACK], F32, "gain_copy")
         nc.scalar.copy(gain_copy[:], gains[:, 0:2, :])
-        gain_whole = tile([P, 2, W], F32, "gain_whole")
+        gain_whole = tile([P, 2, P], F32, "gain_whole")
         nc.scalar.copy(
             gain_whole[:].rearrange("p b (n t) -> p b n t", t=PACK),
-            gain_copy[:].unsqueeze(2).broadcast_to([P, 2, P, PACK]),
+            gain_copy[:].unsqueeze(2).broadcast_to([P, 2, P // PACK, PACK]),
         )
         for i in range(6):
             nc.tensor.matmul_mx(
@@ -234,9 +235,9 @@ def tile_list_register_file_step_kernel(
 
         def gain_gpsimd(b, src, dst, units):
             nc.gpsimd.tensor_tensor(
-                bf16_at(dst, units * W).rearrange("p (u c) -> p u c", c=W),
-                f32_at(src, units * W).rearrange("p (u c) -> p u c", c=W),
-                gain_whole[:, b, :].unsqueeze(1).broadcast_to([P, units, W]),
+                bf16_at(dst, units * W).rearrange("p (u c) -> p u c", c=P),
+                f32_at(src, units * W).rearrange("p (u c) -> p u c", c=P),
+                gain_whole[:, b, :].unsqueeze(1).broadcast_to([P, units * PACK, P]),
                 ALU.mult,
             )
 

from contextlib import ExitStack

import concourse.mybir as mybir
from concourse.masks import make_identity

K, T, S, H, N = 1024, 2048, 1024, 1024, 512
FLOPS = 2 * S * (K * H + K * N + H * N)

F32 = mybir.dt.float32
BF16 = mybir.dt.bfloat16
I32 = mybir.dt.int32
U32 = mybir.dt.uint32
U16 = mybir.dt.uint16
U8 = mybir.dt.uint8
FP8X4 = mybir.dt.float8_e4m3fn_x4
FP4X4 = mybir.dt.float4_e2m1fn_x4
ACT = mybir.ActivationFunctionType
ALU = mybir.AluOpType

P = 128
PACK = 4
PASSES = 2
W = 512
KIB = 1024
BANKS = 8
QUADS = (0, 2, 1, 3)


def tile_list_register_file_step_kernel(
    tc, tab_words, tab_scales, offs, w1_words, w1_scales, w2, gain, w3_words, w3_scales, old, out
):
    nc = tc.nc
    with ExitStack() as ctx:
        keep = ctx.enter_context(tc.tile_pool(name="keep", bufs=1))
        placed = ctx.enter_context(tc.tile_pool(name="placed", bufs=1))
        psum = ctx.enter_context(tc.psum_pool(name="psum", bufs=1))

        def tile(shape, dtype, name):
            return keep.tile(shape, dtype, name=name, align_bytes=64)

        def place(shape, dtype, name, offset):
            return placed.tile(shape, dtype, name=name, offset=offset, align_bytes=64)

        banks = [psum.tile([P, W], F32, name="bank%d" % i) for i in range(BANKS)]
        arena = tile([P, 84 * KIB // 4], F32, "arena")
        rooms = {}

        def f32_at(kib, columns=W):
            room, c = (rooms["h"], kib * KIB // 4) if kib < 16 else (arena, (kib - 16) * KIB // 4)
            return room[:, c : c + columns]

        def bf16_at(kib, columns):
            return f32_at(kib, columns // 2).bitcast(BF16)

        offsets = keep.tile([P, S // 16], U16, name="offsets")
        nc.sync.dma_start(offsets[:], offs)

        w1_raw = [tile([P, PASSES, 2 * W], U8, "w1_raw0"), place([P, PASSES, 2 * W], U8, "w1_raw1", 70 * KIB)]

        def load_w1(b):
            src = w1_words[:, :, 2 * W * b : 2 * W * (b + 1)].bitcast(I32).rearrange("a p c -> p a c")
            nc.sync.dma_start(w1_raw[b][:].bitcast(I32), src)

        tab_rows = tile([P, T], U8, "tab_rows")
        w1_rows = tile([P, H], U8, "w1_rows")
        rows = tile([P, 4 * W], U8, "rows")
        planes = [tile([P, PASSES, 2 * W], U8, "planes%d" % i) for i in range(2)]
        warm = tile([P, 2], F32, "warm")
        gain_rows = place([P, W], F32, "gain_rows", 4 * KIB - 512)
        identity = tile([P, P], F32, "identity")
        nc.vector.memset(tab_rows[:].bitcast(I32), 0)
        nc.vector.memset(w1_rows[:].bitcast(I32), 0)
        nc.vector.memset(warm[:, 0:1], 0.0)
        nc.vector.memset(gain_rows[:], 0.0)
        nc.vector.memset(identity[:], 0.0)
        for plane in planes:
            nc.vector.memset(plane[:].rearrange("p a c -> p (a c)").bitcast(I32), 0)
        make_identity(nc, identity[:], nomemset=True)

        def load_rows(dst, scales):
            nc.sync.dma_start(dst.bitcast(I32), scales.bitcast(I32).rearrange("a q c -> q a c"))

        load_rows(tab_rows[0:P:4, :], tab_scales)
        load_rows(w1_rows[0:P:4, :], w1_scales)
        load_w1(0)
        nc.scalar.activation(warm[:, 1:2], warm[:, 0:1], ACT.Silu)

        table = [place([P, T], U32, "table%d" % a, (54 + 8 * a) * KIB) for a in range(PASSES)]

        def load_table(a):
            nc.sync.dma_start(table[a][:].bitcast(I32), tab_words[a].rearrange("p t i -> p (t i)").bitcast(I32))

        load_table(0)
        nc.sync.dma_start(gain_rows[0:2, :], gain.rearrange("(b k) -> b k", b=2))
        load_table(1)
        load_w1(1)

        for t in range(PACK):
            nc.tensor.transpose(banks[0][:, t:W:PACK], gain_rows[:, t:W:PACK], identity[:])
        gains = banks[0][:].rearrange("p (b t) -> p b t", t=PACK)

        w1 = [tile([P, PASSES * 2 * W], U8, "w1_%d" % b) for b in range(2)]

        def order_w1(copy, b):
            copy(
                w1[b][:].bitcast(U16).rearrange("p (a t m) -> p a t m", a=PASSES, t=PACK),
                w1_raw[b][:].rearrange("p a c -> p (a c)").bitcast(U16).rearrange("p (a m t) -> p a t m", a=PASSES, t=PACK),
            )

        def offsets_of(h, c0=0, c1=W):
            return offsets[:, (h * W + c0) // 16 : (h * W + c1) // 16]

        picked_rows = [tile([P, W], U8, "picked_rows0"), place([P, W], U8, "picked_rows1", 4 * KIB)]

        def gather_rows(h):
            nc.vector.tensor_copy(picked_rows[h][:], tab_rows[:].indirect(offsets_of(h)))

        def move_rows(queue, dst, src):
            for d in QUADS:
                queue.dma_start(dst[32 * d : 32 * d + 4, :, :].bitcast(I32), src[32 * d : 32 * d + 32 : 4, :].bitcast(I32))

        order_w1(nc.scalar.copy, 0)
        gather_rows(0)
        nc.vector.tensor_copy(
            rows[:, W : 3 * W].rearrange("p (b t m) -> p b t m", b=2, t=PACK),
            w1_rows[:].rearrange("p (b m t) -> p b t m", b=2, t=PACK),
        )
        nc.vector.tensor_copy(rows[:, 0:W].bitcast(I32), picked_rows[0][:].bitcast(I32))
        move_rows(nc.sync, planes[0], rows[:, 0 : 2 * W])
        order_w1(nc.scalar.copy, 1)
        gather_rows(1)

        def load_w2(raw, a, half):
            src = w2[a * W : (a + 1) * W, half * (N // 2) : (half + 1) * (N // 2)]
            nc.sync.dma_start(raw, src.rearrange("(p t) n -> p t n", t=PACK))

        nc.vector.tensor_copy(rows[:, 3 * W :].bitcast(I32), picked_rows[1][:].bitcast(I32))
        move_rows(nc.sync, planes[1], rows[:, 2 * W :])
        floats = place([P, 11 * KIB], F32, "floats", 4 * KIB + 512)
        rooms["h"] = floats[:, 7 * KIB :]
        H1, H0, SILU = 6, 0, 16
        first_raw = [x.rearrange("p (t n) -> p t n", t=PACK) for x in (f32_at(H0, 2 * W), floats[:, 6 * KIB : 7 * KIB])]
        for a in range(PASSES):
            load_w2(first_raw[a], a, 0)

        w3 = place([P, PASSES, N], U32, "w3", 0)
        nc.sync.dma_start(w3[:].bitcast(I32), w3_words.rearrange("b p c i -> p b (c i)").bitcast(I32))
        second_raw = floats[:, 0 : 2 * KIB].rearrange("p (a t n) -> p a t n", a=PASSES, t=PACK)
        olds = floats[:, 2 * KIB : 6 * KIB].rearrange("p (h u j) -> p h u j", h=2, u=4)

        def load_old(h, u0):
            src = old[u0 * P : (u0 + 2) * P, h * W : (h + 1) * W].rearrange("(u p) j -> p u j", p=P)
            nc.sync.dma_start(olds[:, h, u0 : u0 + 2, :], src)

        load_old(0, 0)
        w3_planes = rows[:, 0 : 2 * W].rearrange("p (a c) -> p a c", a=PASSES)
        w3_rows = w3_scales.bitcast(I32).rearrange("a q c -> q a c")
        for d in QUADS:
            nc.sync.dma_start(w3_planes[32 * d : 32 * d + 4].bitcast(I32), w3_rows[4 * d : 4 * d + 4])
        for a in range(PASSES):
            load_w2(second_raw[:, a], a, 1)
        load_old(0, 2)
        load_old(1, 0)
        load_old(1, 2)

        picked = {(a, h): tile([P, W], U32, "picked%d%d" % (a, h)) for a, h in ((0, 0), (1, 0), (1, 1))}
        picked[0, 1] = place([P, W], U32, "picked01", 70 * KIB)

        def gather(a, h, c0=0, c1=W):
            nc.vector.tensor_copy(picked[a, h][:, c0:c1], table[a][:].indirect(offsets_of(h, c0, c1)))

        def table_operand(a, h, c0, c1):
            return {"rhs": picked[a, h][:, c0:c1].bitcast(FP8X4), "rhs_scale": planes[h][:, a, h * W + c0 : h * W + c1]}

        gather(0, 0, 0, W // 2)
        gather(0, 0, W // 2, W)
        gain_copy = tile([P, 2, PACK], F32, "gain_copy")
        nc.scalar.copy(gain_copy[:], gains[:, 0:2, :])
        gain_whole = tile([P, 2, P], F32, "gain_whole")
        nc.scalar.copy(
            gain_whole[:].rearrange("p b (n t) -> p b n t", t=PACK),
            gain_copy[:].unsqueeze(2).broadcast_to([P, 2, P // PACK, PACK]),
        )
        for i in range(6):
            nc.tensor.matmul_mx(
                banks[0][:, W // 2 :],
                lhsT=w1_raw[0][:, 0, 0 : 2 * P].bitcast(FP4X4),
                lhsT_scale=picked_rows[0][:, 0:P],
                rhs=picked[0, 0][:, 0 : W // 2].bitcast(FP8X4),
                rhs_scale=picked_rows[0][:, 0 : W // 2],
                start=(i == 0),
                stop=(i == 5),
            )
        gather(1, 0, 0, W // 2)
        gather(1, 0, W // 2, W)
        gather(0, 1)
        gather(1, 1)

        made = []

        def feature_bank(h, b, j0, width, t0, silu):
            bank = banks[1 + len(made) % 5]
            made.append(bank)
            slices = W // width
            for e in range(slices):
                for a in range(PASSES):
                    t = t0 + e
                    c = (1 - b) * W + t * P
                    nc.tensor.matmul_mx(
                        bank[:, e * width : (e + 1) * width],
                        lhsT=w1[b][:, 2 * (a * W + t * P) : 2 * (a * W + (t + 1) * P)].bitcast(FP4X4),
                        lhsT_scale=planes[b][:, a, c : c + P],
                        start=(a == 0),
                        stop=(a == PASSES - 1),
                        **table_operand(a, h, j0, j0 + width),
                    )
            nc.scalar.activation(
                silu.rearrange("p (n e) -> p n e", e=slices), bank[:].rearrange("p (e n) -> p n e", e=slices), ACT.Silu
            )

        def narrow(h, b, j0, kib):
            feature_bank(h, b, j0, P, 0, f32_at(kib))

        def wide(h, b, j0, silu):
            for pair in range(2):
                feature_bank(h, b, j0, 2 * P, 2 * pair, silu[:, pair * W : (pair + 1) * W])

        def gain_narrow(b, src, dst):
            nc.vector.tensor_tensor(
                bf16_at(dst, W).rearrange("p (n t) -> p n t", t=PACK),
                src.rearrange("p (n t) -> p n t", t=PACK),
                gains[:, b, :].unsqueeze(1).broadcast_to([P, P, PACK]),
                ALU.mult,
            )

        def gain_gpsimd(b, src, dst, units):
            nc.gpsimd.tensor_tensor(
                bf16_at(dst, units * W).rearrange("p (u c) -> p u c", c=P),
                f32_at(src, units * W).rearrange("p (u c) -> p u c", c=P),
                gain_whole[:, b, :].unsqueeze(1).broadcast_to([P, units * PACK, P]),
                ALU.mult,
            )

        def gain_wide(b, src, dst):
            nc.vector.tensor_tensor(
                bf16_at(dst, 2 * W).rearrange("p (n u e) -> p n u e", u=2, e=2),
                src.rearrange("p (u n e) -> p n u e", u=2, e=2),
                gains[:, b, :].rearrange("p (u e) -> p u e", e=2).unsqueeze(1).broadcast_to([P, 2 * P, 2, 2]),
                ALU.mult,
            )

        def quantize(x, width, name, scales=None):
            codes = tile([P, width], U32, name + "_codes")
            if scales is None:
                scales = tile([P, width], U8, name + "_scales")
            nc.vector.quantize_mx(out=codes[:].bitcast(FP8X4), scales=scales[:], in_=x)
            return codes, scales

        def round_w2(copy, raw, room):
            copy(room.rearrange("p (c i t) -> p c t i", t=PACK, i=4), raw.rearrange("p t (c i) -> p c t i", i=4))

        w2_q = {}

        first_room = [bf16_at(SILU + 16, 2 * W)]
        round_w2(nc.vector.tensor_copy, first_raw[0], first_room[0])
        narrow(0, 0, 0, SILU)
        narrow(0, 0, P, SILU + 2)
        wide(0, 0, 2 * P, f32_at(SILU + 4, 2 * W))
        gain_wide(0, f32_at(SILU + 4, 2 * W), H0 + 2)
        gain_gpsimd(0, SILU, H0, 2)
        wide(0, 1, 0, f32_at(SILU + 8, 2 * W))
        narrow(0, 1, 3 * P, SILU + 14)
        gain_wide(1, f32_at(SILU + 8, 2 * W), H0 + 4)
        gain_gpsimd(1, SILU + 14, H0 + 7, 1)
        wide(1, 0, 2 * P, f32_at(H1 + 4, 2 * W))
        gain_wide(0, f32_at(H1 + 4, 2 * W), H1 + 2)
        held_silu = place([P, W], F32, "held_silu", 51 * KIB)
        feature_bank(0, 1, 2 * P, P, 0, held_silu[:])
        gain_narrow(1, held_silu[:], H0 + 6)
        first_room.append(bf16_at(H1 + 4, 2 * W))
        round_w2(nc.scalar.copy, first_raw[1], first_room[1])

        def quantize_first(a):
            held = place([P, 2 * P], U8, "first%d_scales" % a, 51 * KIB + 2 * P * a)
            codes, scales = quantize(first_room[a], 2 * P, "first%d" % a, held)
            for u in range(2):
                w2_q[a, u] = codes[:, u * P : (u + 1) * P], scales[:, u * P : (u + 1) * P]

        quantize_first(0)
        h_q = {0: quantize(bf16_at(H0, 8 * W), 2 * W, "h0", place([P, 2 * W], U8, "h0_scales", 52 * KIB))}
        quantize_first(1)
        wide(1, 0, 0, f32_at(SILU + 18, 2 * W))
        narrow(1, 1, 0, SILU + 22)
        narrow(1, 1, P, SILU + 24)
        wide(1, 1, 2 * P, f32_at(SILU + 26, 2 * W))
        gain_wide(0, f32_at(SILU + 18, 2 * W), H1)
        gain_gpsimd(1, SILU + 22, H1 + 4, 2)
        gain_wide(1, f32_at(SILU + 26, 2 * W), H1 + 6)

        STAY, SECOND = 46, 64
        units = [(0, 0), (0, 1), (1, 0), (1, 1), (0, 2), (0, 3), (1, 2), (1, 3)]
        gate_bank = dict(zip(units, (6, 7, 6, 6, 7, 6, 7, 6)))
        y_bank = dict(zip(units, (2, 3, 1, 0, 4, 5, 2, 3)))
        stay = {unit: f32_at(STAY + 2 * (i + (i > 1))) for i, unit in enumerate(units)}
        held_diff = place([P, W], F32, "held_diff", 49 * KIB)
        diff = {unit: f32_at(SECOND + 4 + 2 * i) for i, unit in enumerate(units[3:] + units[2:3])}
        diff[0, 0] = f32_at(SILU + 26)
        diff[0, 1] = held_diff[:]
        step = {unit: f32_at(SECOND + 18 + 2 * i) for i, unit in enumerate(units)}
        step[0, 0] = f32_at(H1)
        step[1, 0] = f32_at(STAY + 1)
        step[1, 1] = f32_at(STAY + 3)
        step[0, 2] = f32_at(SECOND + 3)
        result = {unit: f32_at(SILU + 2 * i) for i, unit in enumerate(units)}
        result[0, 0] = diff[1, 0]
        result[0, 1] = stay[1, 0]
        result[1, 1] = olds[:, 0, 3, :]
        result[0, 2] = olds[:, 1, 2, :]
        result[0, 3] = olds[:, 1, 3, :]

        def gate(h, u):
            for a in range(PASSES):
                codes, scales = w2_q[a, u]
                nc.tensor.matmul_mx(
                    banks[gate_bank[h, u]][:],
                    lhsT=codes.bitcast(FP8X4),
                    lhsT_scale=scales,
                    start=(a == 0),
                    stop=(a == PASSES - 1),
                    **table_operand(a, h, 0, W),
                )

        def output(h, u):
            codes, scales = h_q[h]
            for b in range(PASSES):
                nc.tensor.matmul_mx(
                    banks[y_bank[h, u]][:],
                    lhsT=w3[:, b, u * P : (u + 1) * P].bitcast(FP8X4),
                    lhsT_scale=w3_planes[:, b, u * P : (u + 1) * P],
                    rhs=codes[:, b * W : (b + 1) * W].bitcast(FP8X4),
                    rhs_scale=scales[:, b * W : (b + 1) * W],
                    start=(b == 0),
                    stop=(b == PASSES - 1),
                )

        def sigmoid(h, u):
            nc.scalar.activation(stay[h, u], banks[gate_bank[h, u]][:], ACT.Sigmoid, scale=-1.0)

        def difference(h, u):
            nc.vector.tensor_tensor(diff[h, u], olds[:, h, u, :], banks[y_bank[h, u]][:], ALU.subtract)

        def product(engine, h, u, c0=0, c1=W):
            engine.tensor_tensor(step[h, u][:, c0:c1], stay[h, u][:, c0:c1], diff[h, u][:, c0:c1], ALU.mult)

        def finish(h, u, c0=0, c1=W):
            r = result[h, u][:, c0:c1]
            nc.vector.tensor_tensor(r, step[h, u][:, c0:c1], banks[y_bank[h, u]][:, c0:c1], ALU.add)
            nc.sync.dma_start(out[u * P : (u + 1) * P, h * W + c0 : h * W + c1], r)

        gate(0, 0)
        gate(0, 1)
        output(0, 0)
        output(0, 1)
        output(0, 2)
        output(0, 3)
        sigmoid(0, 0)
        gate(1, 0)
        sigmoid(0, 1)
        difference(0, 0)
        h_q[1] = quantize(bf16_at(H1, 8 * W), 2 * W, "h1")
        output(1, 0)
        output(1, 1)
        product(nc.gpsimd, 0, 0)
        difference(0, 1)
        difference(0, 2)
        second_room = bf16_at(SECOND, 4 * W)
        round_w2(nc.scalar.copy, second_raw[:, 0], second_room[:, 0 : 2 * W])
        sigmoid(1, 0)
        gate(1, 1)
        round_w2(nc.scalar.copy, second_raw[:, 1], second_room[:, 2 * W :])
        sigmoid(1, 1)
        difference(1, 0)
        product(nc.gpsimd, 0, 1)
        difference(1, 1)
        codes, scales = quantize(second_room, 4 * P, "second", place([P, 4 * P], U8, "second_scales", 49 * KIB))
        for a in range(PASSES):
            for u in range(2, 4):
                c = (2 * a + u - 2) * P
                w2_q[a, u] = codes[:, c : c + P], scales[:, c : c + P]
        product(nc.vector, 1, 0)
        product(nc.vector, 1, 1)
        finish(0, 0)
        gate(0, 2)
        sigmoid(0, 2)
        gate(0, 3)
        sigmoid(0, 3)
        output(1, 2)
        finish(0, 1)
        gate(1, 2)
        sigmoid(1, 2)
        output(1, 3)
        gate(1, 3)
        sigmoid(1, 3)
        finish(1, 0)
        product(nc.gpsimd, 0, 2)
        difference(0, 3)
        finish(1, 1)
        product(nc.gpsimd, 0, 3)
        difference(1, 2)
        finish(0, 2)
        product(nc.gpsimd, 1, 2)
        difference(1, 3)
        finish(0, 3)
        product(nc.gpsimd, 1, 3, 0, 3 * W // 4)
        product(nc.gpsimd, 1, 3, 3 * W // 4, W)
        finish(1, 2)
        finish(1, 3, 0, 3 * W // 4)
        finish(1, 3, 3 * W // 4, W)
